import numpy as np
import ml_dtypes


def mxq(x, axis, fmt="e4m3"):
    dtype, down = {"e4m3": (ml_dtypes.float8_e4m3fn, 7), "e5m2": (ml_dtypes.float8_e5m2, 14)}[fmt]
    v = np.moveaxis(np.asarray(x, np.float32).astype(ml_dtypes.bfloat16).astype(np.float64), axis, -1)
    blocks = v.reshape(v.shape[:-1] + (-1, 32))
    amax = np.abs(blocks).max(-1, keepdims=True)
    byte = np.maximum(np.where(amax > 0, np.frexp(amax)[1] - 1 + 127, 0) - down, 1)
    scale = np.exp2(byte - 127.0)
    codes = (blocks / scale).astype(np.float32).astype(dtype).astype(np.float64)
    return np.moveaxis((codes * scale).reshape(v.shape), -1, axis)


WIDE = False


def mx_kscale(k):
    if not WIDE:
        return np.ones(k)
    levels = np.array([10, -10, 5, -5, 0])
    if k % 512:
        return np.exp2(np.random.permutation(np.resize(levels, k // 32))).repeat(32)
    a = np.empty((k // 512, 16))
    for p in range(k // 512):
        a[p, :8] = np.random.permutation(np.resize(levels, 8))
        for g in range(8):
            far = levels[np.abs(levels - a[p, g]) >= 10]
            a[p, g + 8] = far[np.random.randint(len(far))]
    return np.exp2(a.ravel()).repeat(32)


def f64(x):
    return np.asarray(x).astype(np.float64)


def striped(idx):
    return np.tile(idx.reshape(-1, 16).T, (8, 1)).astype(np.uint16)


def unstriped(offs):
    return offs[:16].T.reshape(-1).astype(np.int64)


def relu(v):
    return np.maximum(v, 0.0)


K, T, S, V, H, N = 1024, 2048, 1024, 512, 512, 256


def setup_inputs():
    n = np.random.standard_normal
    s = mx_kscale(K)[:, None]
    u = mx_kscale(H)
    return {
        "xT": (n((K, T)) * s).astype(np.float32),
        "w1": (n((K, H)) / np.sqrt(K) / s * u).astype(np.float32),
        "w2": (n((H, N)) / np.sqrt(2 * H) / u[:, None]).astype(np.float32),
        "w3": (n((H, N)) / np.sqrt(2 * H) / u[:, None]).astype(np.float32),
        "offs": striped(np.random.permutation(T)[:S]),
        "cen": striped(np.random.permutation(S)[:V]),
        "pos1": striped(np.random.permutation(S)[:V]),
        "pos2": striped(np.random.permutation(S)[:V]),
        "pos3": striped(np.random.permutation(S)[:V]),
        "pos4": striped(np.random.permutation(S)[:V]),
    }


def reference(xT, w1, w2, w3, offs, cen, pos1, pos2, pos3, pos4):
    xq = mxq(f64(xT)[:, unstriped(offs)], 0, "e4m3")
    h = relu(mxq(f64(w1), 0, "e4m3").T @ xq)
    hc = h[:, unstriped(cen)]
    z = (h[:, unstriped(pos1)] + h[:, unstriped(pos2)] + h[:, unstriped(pos3)] + h[:, unstriped(pos4)]) / 4
    return mxq(f64(w2), 0, "e4m3").T @ mxq(hc, 0, "e4m3") + mxq(f64(w3), 0, "e4m3").T @ mxq(z, 0, "e4m3")

@@ -1,0 +1,221 @@
+from contextlib import ExitStack
+
+import concourse.mybir as mybir
+from concourse.masks import make_identity
+
+K, T, S, V, H, N = 1024, 2048, 1024, 512, 512, 256
+FLOPS = 2 * K * H * S + 2 * 2 * H * N * V
+
+F32 = mybir.dt.float32
+BF16 = mybir.dt.bfloat16
+U32 = mybir.dt.uint32
+U16 = mybir.dt.uint16
+U8 = mybir.dt.uint8
+FP8X4 = mybir.dt.float8_e4m3fn_x4
+COPY = mybir.ActivationFunctionType.Copy
+RELU = mybir.ActivationFunctionType.Relu
+
+P = 128
+PACK = 4
+K_PASS = P * PACK
+HALF = 512
+
+CHUNKS = [
+    [(0, 1024, 1024), (1024, 1024, 704)],
+    [(0, 1024, 0), (1024, 1024, 512)],
+    [(0, 1024, 0), (1024, 1024, 0)],
+    [(0, 1024, 0), (1024, 512, 0), (1536, 512, 256)],
+]
+
+
+def tile_picked_sagecat_mean_e_kernel(tc, xT, w1, w2, w3, offs, cen, pos1, pos2, pos3, pos4, out):
+    nc = tc.nc
+    with ExitStack() as ctx:
+        keep = ctx.enter_context(tc.tile_pool(name="keep", bufs=1))
+        ring = ctx.enter_context(tc.tile_pool(name="ring", bufs=8))
+        psum = ctx.enter_context(tc.psum_pool(name="psum", bufs=4))
+
+        def sb(name, shape, dtype):
+            return keep.tile(shape, dtype, name=name, align_bytes=64)
+
+        def load_list(name, src):
+            tile = sb(name, list(src.shape), U16)
+            nc.sync.dma_start(tile[:], src)
+            return tile
+
+        def quantize(name, src, tag=None):
+            width = src.shape[1] // PACK
+            codes = keep.tile([P, width], U32, name=name + "_codes", tag=(tag or name + "_codes"), align_bytes=64)
+            scales = sb(name + "_scales", [P, width], U8)
+            nc.vector.quantize_mx(out=codes[:].bitcast(FP8X4), scales=scales[:], in_=src)
+            return codes, scales
+
+        def mx(acc, lhs, lcols, rhs, rcols, start, stop):
+            nc.tensor.matmul_mx(out=acc, lhsT=lhs[0][:, lcols].bitcast(FP8X4), lhsT_scale=lhs[1][:, lcols],
+                                rhs=rhs[0][:, rcols].bitcast(FP8X4), rhs_scale=rhs[1][:, rcols], start=start, stop=stop)
+
+        ident = sb("ident", [P, P], F32)
+        make_identity(nc, ident[:])
+
+        x_raw = {}
+        lists = {}
+        for pair in range(4):
+            g, u = divmod(pair, 2)
+            rows = xT[g * K_PASS:(g + 1) * K_PASS, :].rearrange("(p j) t -> p j t", j=PACK)
+            for c0, width, vcols in CHUNKS[pair]:
+                raw = sb("x%d_%d" % (pair, c0), [P, 2, width], F32)
+                nc.sync.dma_start(raw[:], rows[:, 2 * u:2 * u + 2, c0:c0 + width])
+                x_raw[pair, c0] = raw
+            if pair == 0:
+                lists["offs"] = load_list("offs", offs)
+        w1_raw = []
+        for g in range(2):
+            raw = sb("w1_raw%d" % g, [P, PACK, H], F32)
+            nc.sync.dma_start(raw[:], w1[g * K_PASS:(g + 1) * K_PASS, :].rearrange("(p j) c -> p j c", j=PACK))
+            w1_raw.append(raw)
+        for name, src in (("pos1", pos1), ("pos2", pos2), ("pos3", pos3), ("pos4", pos4), ("cen", cen)):
+            lists[name] = load_list(name, src)
+        w23_raw = []
+        for name, src in (("w3_raw", w3), ("w2_raw", w2)):
+            raw = sb(name, [P, PACK, N], F32)
+            nc.sync.dma_start(raw[:], src.rearrange("(p j) c -> p j c", j=PACK))
+            w23_raw.append(raw)
+
+        def cast_pair(pair):
+            win = ring.tile([P, T * 2], BF16, name="pairs", tag="pairs", bufs=2, align_bytes=64)
+            view = win[:].rearrange("p (t e) -> p t e", e=2)
+            for c0, width, vcols in CHUNKS[pair]:
+                src = x_raw[pair, c0][:].rearrange("p e t -> p t e")
+                scols = width - vcols
+                if scols:
+                    nc.scalar.activation(view[:, c0:c0 + scols, :], src[:, 0:scols, :], COPY)
+                if vcols:
+                    nc.vector.tensor_copy(view[:, c0 + scols:c0 + width, :], src[:, scols:width, :])
+            return win
+
+        def gather_pair(win, dst, u, first, count):
+            words = dst[:].bitcast(U32).rearrange("p (n u) -> p n u", u=2)
+            nc.vector.tensor_copy(words[:, :, u], win[:].bitcast(U32).indirect(lists["offs"][:, first // 16:(first + count) // 16]))
+
+        x0_in = sb("x0_in", [P, S * PACK], BF16)
+        for u in range(2):
+            gather_pair(cast_pair(u), x0_in, u, 0, S)
+        x0 = quantize("x0", x0_in[:])
+        x1_in = [sb("x1_in%d" % a, [P, HALF * PACK], BF16) for a in range(2)]
+        win = cast_pair(2)
+        for a in range(2):
+            gather_pair(win, x1_in[a], 0, a * HALF, HALF)
+        win = cast_pair(3)
+
+        def weave_w1(g, t0, nt, tag, eng):
+            tile = keep.tile([P, nt * P * PACK], BF16, name="w1_in%d_%d" % (g, t0), tag=tag, align_bytes=64)
+            src = w1_raw[g][:].rearrange("p j (m t) -> p m t j", t=PACK)
+            if nt == 1:
+                nc.scalar.activation(tile[:].rearrange("p (m j) -> p m j", j=PACK), src[:, :, t0, :], COPY)
+            elif eng is nc.vector:
+                nc.vector.tensor_copy(tile[:].rearrange("p (t m j) -> p m t j", t=nt, j=PACK), src[:, :, t0:t0 + nt, :])
+            else:
+                nc.scalar.activation(tile[:].rearrange("p (t m j) -> p m t j", t=nt, j=PACK), src[:, :, t0:t0 + nt, :], COPY)
+            return tile
+
+        w1_q = {}
+
+        def quantize_w1(g, t0, nt, tile, tag):
+            q = quantize("w1_%d_%d" % (g, t0), tile[:], tag)
+            for t in range(nt):
+                w1_q[g, t0 + t] = (q, slice(t * P, (t + 1) * P))
+
+        in_a = weave_w1(0, 0, 4, "wa", nc.scalar)
+        in_b = weave_w1(1, 0, 1, "wb", nc.scalar)
+        in_c = weave_w1(1, 1, 1, "wc", nc.scalar)
+        for a in range(2):
+            gather_pair(win, x1_in[a], 1, a * HALF, HALF)
+        x1 = [quantize("x1_%d" % a, x1_in[a][:]) for a in range(2)]
+        quantize_w1(0, 0, 4, in_a, "qa")
+        quantize_w1(1, 0, 1, in_b, "qb")
+        in_d = weave_w1(1, 2, 2, "wb", nc.vector)
+        quantize_w1(1, 1, 1, in_c, "qc")
+        quantize_w1(1, 2, 2, in_d, "qe")
+
+        h = []
+        for t in range(PACK):
+            plane = sb("h%d" % t, [P, S], F32)
+            accs = [psum.tile([P, HALF], F32, name="acc", tag=("acc" if t < 2 else "z")) for a in range(2)]
+            for a in range(2):
+                mx(accs[a][:], w1_q[0, t][0], w1_q[0, t][1], x0, slice(a * HALF, (a + 1) * HALF), True, False)
+            for a in range(2):
+                mx(accs[a][:], w1_q[1, t][0], w1_q[1, t][1], x1[a], slice(0, HALF), False, True)
+                nc.scalar.activation(plane[:, a * HALF:(a + 1) * HALF], accs[a][:], RELU)
+            h.append(plane)
+
+        w23_in = keep.tile([P, 2 * N * PACK], BF16, name="w23_in", tag="qe", align_bytes=64)
+        for i in range(2):
+            nc.scalar.activation(w23_in[:, i * N * PACK:(i + 1) * N * PACK].rearrange("p (c j) -> p c j", j=PACK),
+                                 w23_raw[i][:].rearrange("p j c -> p c j"), COPY)
+
+        z_sum = [psum.tile([P, PACK, P], F32, name="zsum%d" % vt, tag="z") for vt in range(4)]
+        z_back = None
+        shared = {(3, 0): "c_got0", (3, 1): "c_got1", (3, 2): "c_got2"}
+        for t in range(PACK):
+            for d in range(4):
+                if (t, d) in shared:
+                    got = keep.tile([P, V], F32, name="got", tag=shared[t, d], align_bytes=64)
+                else:
+                    got = ring.tile([P, V], F32, name="got", tag="got", bufs=13)
+                nc.vector.tensor_copy(got[:], h[t][:].indirect(lists["pos%d" % (d + 1)][:]))
+                for vt in range(4):
+                    nc.tensor.matmul(z_sum[vt][:, t, :], got[:, vt * P:(vt + 1) * P], ident[:], start=(d == 0), stop=(d == 3), is_transpose=True)
+            if t % 2 == 1:
+                u = t // 2
+                if z_back is None:
+                    z_back = [psum.tile([P, 2, 256], F32, name="zback%d" % b, tag="acc") for b in range(2)]
+                for vt in range(4):
+                    zt = keep.tile([P, 2 * P], BF16, name="zt", tag="zt%d_%d" % (u, vt), align_bytes=64)
+                    nc.scalar.activation(zt[:].rearrange("v (p e) -> v p e", e=2),
+                                         z_sum[vt][:, 2 * u:2 * u + 2, :].rearrange("v e p -> v p e"), COPY, scale=0.25)
+                    nc.tensor.transpose(z_back[vt // 2][:, u, (vt % 2) * P:(vt % 2 + 1) * P], zt[:].bitcast(F32), ident[:])
+        z_in = [sb("z_in%d" % b, [P, 256 * PACK], BF16) for b in range(2)]
+        for b in range(2):
+            nc.scalar.copy(z_in[b][:].bitcast(F32).rearrange("p (v u) -> p v u", u=2), z_back[b][:].rearrange("p u v -> p v u"))
+
+        pieces = [(0, 256), (256, 128), (384, 128)]
+        in_tags = ["zt1_3", "zt1_2", "c_in2"]
+
+        def gather_cen(b):
+            v0, nv = pieces[b]
+            got = keep.tile([P, PACK, nv], BF16, name="c_got%d" % b, tag="c_got%d" % b, align_bytes=64)
+            for t in range(PACK):
+                nc.vector.tensor_copy(got[:, t, :], h[t][:].indirect(lists["cen"][:, v0 // 16:(v0 + nv) // 16]))
+            tile = keep.tile([P, nv * PACK], BF16, name="c_in%d" % b, tag=in_tags[b], align_bytes=64)
+            if b < 2:
+                nc.scalar.copy(tile[:].rearrange("p (v t) -> p v t", t=PACK), got[:].rearrange("p t v -> p v t"))
+            else:
+                nc.vector.tensor_copy(tile[:].rearrange("p (v t) -> p v t", t=PACK), got[:].rearrange("p t v -> p v t"))
+            return tile
+
+        def start_out(b, zq):
+            v0, nv = pieces[b]
+            accs = [psum.tile([P, nv], F32, name="res", tag=("z" if b < 2 else "acc")) for m in range(2)]
+            for m in range(2):
+                mx(accs[m][:], w23, slice(m * P, (m + 1) * P), zq, slice(v0 % 256, v0 % 256 + nv), True, False)
+            return accs
+
+        def finish_out(b, accs, cq):
+            v0, nv = pieces[b]
+            res = sb("res%d" % b, [P, 2, nv], F32)
+            for m in range(2):
+                mx(accs[m][:], w23, slice(N + m * P, N + (m + 1) * P), cq, slice(0, nv), False, True)
+                if m == 0 or b != 1:
+                    nc.scalar.copy(res[:, m, :], accs[m][:])
+                else:
+                    nc.vector.tensor_copy(res[:, m, :], accs[m][:])
+            nc.sync.dma_start(out[:, v0:v0 + nv].rearrange("(m p) v -> p m v", p=P), res[:])
+
+        w23 = quantize("w23", w23_in[:])
+        c_in = [gather_cen(b) for b in range(3)]
+        zq = quantize("z0", z_in[0][:])
+        finish_out(0, start_out(0, zq), quantize("c0", c_in[0][:]))
+        zq = quantize("z1", z_in[1][:])
+        accs = [start_out(b, zq) for b in (1, 2)]
+        finish_out(2, accs[1], quantize("c2", c_in[2][:]))
+        finish_out(1, accs[0], quantize("c1", c_in[1][:]))

@@ -21,10 +21,8 @@ K_PASS = P * PACK
 HALF = 512
 
 CHUNKS = [
-    [(0, 1024, 1024), (1024, 1024, 704)],
-    [(0, 1024, 0), (1024, 1024, 512)],
-    [(0, 1024, 0), (1024, 1024, 0)],
-    [(0, 1024, 0), (1024, 512, 0), (1536, 512, 256)],
+    [(0, 512, 256), (512, 512, 256), (1024, 512, 256), (1536, 512, 352)],
+    [(0, 512, 0), (512, 512, 192), (1024, 512, 192), (1536, 256, 128), (1792, 128, 0), (1920, 128, 128)],
 ]
 
 
@@ -50,23 +48,22 @@ def tile_picked_sagecat_mean_e_kernel(tc, xT, w1, w2, w3, offs, cen, pos1, pos2,
             nc.vector.quantize_mx(out=codes[:].bitcast(FP8X4), scales=scales[:], in_=src)
             return codes, scales
 
-        def mx(acc, lhs, lcols, rhs, rcols, start, stop):
+        def mx(acc, lhs, lcols, rhs, rhs_scale, start, stop):
             nc.tensor.matmul_mx(out=acc, lhsT=lhs[0][:, lcols].bitcast(FP8X4), lhsT_scale=lhs[1][:, lcols],
-                                rhs=rhs[0][:, rcols].bitcast(FP8X4), rhs_scale=rhs[1][:, rcols], start=start, stop=stop)
+                                rhs=rhs.bitcast(FP8X4), rhs_scale=rhs_scale, start=start, stop=stop)
 
         ident = sb("ident", [P, P], F32)
         make_identity(nc, ident[:])
 
         x_raw = {}
         lists = {}
-        for pair in range(4):
-            g, u = divmod(pair, 2)
+        for g in range(2):
             rows = xT[g * K_PASS:(g + 1) * K_PASS, :].rearrange("(p j) t -> p j t", j=PACK)
-            for c0, width, vcols in CHUNKS[pair]:
-                raw = sb("x%d_%d" % (pair, c0), [P, 2, width], F32)
-                nc.sync.dma_start(raw[:], rows[:, 2 * u:2 * u + 2, c0:c0 + width])
-                x_raw[pair, c0] = raw
-            if pair == 0:
+            for c0, width, vcols in CHUNKS[g]:
+                raw = sb("x%d_%d" % (g, c0), [P, PACK, width], F32)
+                nc.sync.dma_start(raw[:], rows[:, :, c0:c0 + width])
+                x_raw[g, c0] = raw
+            if g == 0:
                 lists["offs"] = load_list("offs", offs)
         w1_raw = []
         for g in range(2):
@@ -81,41 +78,47 @@ def tile_picked_sagecat_mean_e_kernel(tc, xT, w1, w2, w3, offs, cen, pos1, pos2,
             nc.sync.dma_start(raw[:], src.rearrange("(p j) c -> p j c", j=PACK))
             w23_raw.append(raw)
 
-        def cast_pair(pair):
-            win = ring.tile([P, T * 2], BF16, name="pairs", tag="pairs", bufs=2, align_bytes=64)
-            view = win[:].rearrange("p (t e) -> p t e", e=2)
-            for c0, width, vcols in CHUNKS[pair]:
-                src = x_raw[pair, c0][:].rearrange("p e t -> p t e")
+        def weave(eng, dst, src):
+            dst = dst.rearrange("p (c i t) -> p c t i", i=4, t=PACK)
+            src = src.rearrange("p t (c i) -> p c t i", i=4)
+            if eng is nc.vector:
+                nc.vector.tensor_copy(dst, src)
+            else:
+                nc.scalar.activation(dst, src, COPY)
+
+        x_scales = sb("x_scales", [P, T], U8)
+        nc.gpsimd.memset(x_scales[:].bitcast(U32), 0)
+
+        def quantize_x(g):
+            words = keep.tile([P, T], U32, name="x_words", tag="x_words%d" % g, align_bytes=64)
+            for c0, width, vcols in CHUNKS[g]:
+                tile = ring.tile([P, width * PACK], BF16, name="x_in", tag="x_in", bufs=4, align_bytes=64)
                 scols = width - vcols
                 if scols:
-                    nc.scalar.activation(view[:, c0:c0 + scols, :], src[:, 0:scols, :], COPY)
+                    weave(nc.scalar, tile[:, 0:scols * PACK], x_raw[g, c0][:, :, 0:scols])
                 if vcols:
-                    nc.vector.tensor_copy(view[:, c0 + scols:c0 + width, :], src[:, scols:width, :])
-            return win
+                    weave(nc.vector, tile[:, scols * PACK:width * PACK], x_raw[g, c0][:, :, scols:width])
+                nc.vector.quantize_mx(out=words[:, c0:c0 + width].bitcast(FP8X4), scales=x_scales[4 * g:P, c0:c0 + width], in_=tile[:])
+            return words
 
-        def gather_pair(win, dst, u, first, count):
-            words = dst[:].bitcast(U32).rearrange("p (n u) -> p n u", u=2)
-            nc.vector.tensor_copy(words[:, :, u], win[:].bitcast(U32).indirect(lists["offs"][:, first // 16:(first + count) // 16]))
+        def pick(name, src, dtype, tag, first, count):
+            tile = keep.tile([P, count], dtype, name=name, tag=tag, align_bytes=64)
+            nc.vector.tensor_copy(tile[:], src[:].indirect(lists["offs"][:, first // 16:(first + count) // 16]))
+            return tile
 
-        x0_in = sb("x0_in", [P, S * PACK], BF16)
-        for u in range(2):
-            gather_pair(cast_pair(u), x0_in, u, 0, S)
-        x0 = quantize("x0", x0_in[:])
-        x1_in = [sb("x1_in%d" % a, [P, HALF * PACK], BF16) for a in range(2)]
-        win = cast_pair(2)
-        for a in range(2):
-            gather_pair(win, x1_in[a], 0, a * HALF, HALF)
-        win = cast_pair(3)
+        all0 = quantize_x(0)
+        xw0 = pick("xw0", all0, U32, "xw0", 0, S)
+        all1 = quantize_x(1)
 
         def weave_w1(g, t0, nt, tag, eng):
             tile = keep.tile([P, nt * P * PACK], BF16, name="w1_in%d_%d" % (g, t0), tag=tag, align_bytes=64)
-            src = w1_raw[g][:].rearrange("p j (m t) -> p m t j", t=PACK)
+            src = w1_raw[g][:].rearrange("p j (m t) -> p m j t", t=PACK)
             if nt == 1:
-                nc.scalar.activation(tile[:].rearrange("p (m j) -> p m j", j=PACK), src[:, :, t0, :], COPY)
+                nc.scalar.activation(tile[:].rearrange("p (m j) -> p m j", j=PACK), src[:, :, :, t0], COPY)
             elif eng is nc.vector:
-                nc.vector.tensor_copy(tile[:].rearrange("p (t m j) -> p m t j", t=nt, j=PACK), src[:, :, t0:t0 + nt, :])
+                nc.vector.tensor_copy(tile[:].rearrange("p (t m j) -> p m j t", t=nt, j=PACK), src[:, :, :, t0:t0 + nt])
             else:
-                nc.scalar.activation(tile[:].rearrange("p (t m j) -> p m t j", t=nt, j=PACK), src[:, :, t0:t0 + nt, :], COPY)
+                nc.scalar.activation(tile[:].rearrange("p (t m j) -> p m j t", t=nt, j=PACK), src[:, :, :, t0:t0 + nt], COPY)
             return tile
 
         w1_q = {}
@@ -125,43 +128,68 @@ def tile_picked_sagecat_mean_e_kernel(tc, xT, w1, w2, w3, offs, cen, pos1, pos2,
             for t in range(nt):
                 w1_q[g, t0 + t] = (q, slice(t * P, (t + 1) * P))
 
-        in_a = weave_w1(0, 0, 4, "wa", nc.scalar)
+        in_a = weave_w1(0, 0, 2, "wa", nc.scalar)
+        in_e = weave_w1(0, 2, 2, "we", nc.scalar)
         in_b = weave_w1(1, 0, 1, "wb", nc.scalar)
         in_c = weave_w1(1, 1, 1, "wc", nc.scalar)
-        for a in range(2):
-            gather_pair(win, x1_in[a], 1, a * HALF, HALF)
-        x1 = [quantize("x1_%d" % a, x1_in[a][:]) for a in range(2)]
-        quantize_w1(0, 0, 4, in_a, "qa")
+        xs = pick("xs", x_scales, U8, "xs", 0, S)
+        quantize_w1(0, 0, 2, in_a, "qa")
+        spans = [(0, 512), (512, 256), (768, 256)]
+        early = pick("xw1a", all1, U32, "wa", 0, 768)
+        xw1 = [early[:, 0:512], early[:, 512:768]]
         quantize_w1(1, 0, 1, in_b, "qb")
-        in_d = weave_w1(1, 2, 2, "wb", nc.vector)
+        xw1.append(pick("xw1c", all1, U32, "wb", *spans[2])[:])
         quantize_w1(1, 1, 1, in_c, "qc")
-        quantize_w1(1, 2, 2, in_d, "qe")
+        quantize_w1(0, 2, 2, in_e, "wc")
+
+        def first_pass(acc, t, a):
+            cols = slice(spans[a][0], spans[a][0] + spans[a][1])
+            mx(acc, w1_q[0, t][0], w1_q[0, t][1], xw0[:, cols], xs[:, cols], True, False)
+
+        def second_pass(acc, t, a):
+            cols = slice(spans[a][0], spans[a][0] + spans[a][1])
+            mx(acc, w1_q[1, t][0], w1_q[1, t][1], xw1[a], xs[4:P, cols], False, True)
 
         h = []
+        bank_tags = [None, ("acc", "z"), ("z", "z"), ("acc", "acc")]
         for t in range(PACK):
             plane = sb("h%d" % t, [P, S], F32)
-            accs = [psum.tile([P, HALF], F32, name="acc", tag=("acc" if t < 2 else "z")) for a in range(2)]
-            for a in range(2):
-                mx(accs[a][:], w1_q[0, t][0], w1_q[0, t][1], x0, slice(a * HALF, (a + 1) * HALF), True, False)
-            for a in range(2):
-                mx(accs[a][:], w1_q[1, t][0], w1_q[1, t][1], x1[a], slice(0, HALF), False, True)
-                nc.scalar.activation(plane[:, a * HALF:(a + 1) * HALF], accs[a][:], RELU)
+            if t == 0:
+                accs = [psum.tile([P, n], F32, name="acc", tag="acc") for first, n in spans]
+                for a in range(3):
+                    first_pass(accs[a][:], t, a)
+                for a, (first, n) in enumerate(spans):
+                    second_pass(accs[a][:], t, a)
+                    if a < 2:
+                        nc.scalar.activation(plane[:, first:first + n], accs[a][:], RELU)
+                    else:
+                        nc.vector.tensor_scalar_max(plane[:, first:first + n], accs[a][:], 0.0)
+                quantize_w1(1, 2, 2, weave_w1(1, 2, 2, "qb", nc.scalar), "qe")
+            else:
+                accs = [psum.tile([P, HALF], F32, name="acc", tag=tag) for tag in bank_tags[t]]
+                first_pass(accs[0][:], t, 0)
+                second_pass(accs[0][:], t, 0)
+                nc.scalar.activation(plane[:, 0:HALF], accs[0][:], RELU)
+                for a in (1, 2):
+                    part = accs[1][:, spans[a][0] - HALF:spans[a][0] - HALF + spans[a][1]]
+                    first_pass(part, t, a)
+                    second_pass(part, t, a)
+                nc.scalar.activation(plane[:, HALF:S], accs[1][:], RELU)
             h.append(plane)
 
         w23_in = keep.tile([P, 2 * N * PACK], BF16, name="w23_in", tag="qe", align_bytes=64)
         for i in range(2):
-            nc.scalar.activation(w23_in[:, i * N * PACK:(i + 1) * N * PACK].rearrange("p (c j) -> p c j", j=PACK),
-                                 w23_raw[i][:].rearrange("p j c -> p c j"), COPY)
+            weave(nc.scalar, w23_in[:, i * N * PACK:(i + 1) * N * PACK], w23_raw[i][:])
 
         z_sum = [psum.tile([P, PACK, P], F32, name="zsum%d" % vt, tag="z") for vt in range(4)]
         z_back = None
-        shared = {(3, 0): "c_got0", (3, 1): "c_got1", (3, 2): "c_got2"}
+        shared = {(3, 0): "c_got0", (3, 1): "c_got1"}
         for t in range(PACK):
             for d in range(4):
                 if (t, d) in shared:
                     got = keep.tile([P, V], F32, name="got", tag=shared[t, d], align_bytes=64)
                 else:
-                    got = ring.tile([P, V], F32, name="got", tag="got", bufs=13)
+                    got = ring.tile([P, V], F32, name="got", tag="got", bufs=14)
                 nc.vector.tensor_copy(got[:], h[t][:].indirect(lists["pos%d" % (d + 1)][:]))
                 for vt in range(4):
                     nc.tensor.matmul(z_sum[vt][:, t, :], got[:, vt * P:(vt + 1) * P], ident[:], start=(d == 0), stop=(d == 3), is_transpose=True)
@@ -179,43 +207,44 @@ def tile_picked_sagecat_mean_e_kernel(tc, xT, w1, w2, w3, offs, cen, pos1, pos2,
             nc.scalar.copy(z_in[b][:].bitcast(F32).rearrange("p (v u) -> p v u", u=2), z_back[b][:].rearrange("p u v -> p v u"))
 
         pieces = [(0, 256), (256, 128), (384, 128)]
+        got_tags = ["c_got0", "c_got1", "zt1_3"]
         in_tags = ["zt1_3", "zt1_2", "c_in2"]
 
         def gather_cen(b):
             v0, nv = pieces[b]
-            got = keep.tile([P, PACK, nv], BF16, name="c_got%d" % b, tag="c_got%d" % b, align_bytes=64)
+            got = keep.tile([P, PACK, nv], BF16, name="c_got%d" % b, tag=got_tags[b], align_bytes=64)
             for t in range(PACK):
                 nc.vector.tensor_copy(got[:, t, :], h[t][:].indirect(lists["cen"][:, v0 // 16:(v0 + nv) // 16]))
             tile = keep.tile([P, nv * PACK], BF16, name="c_in%d" % b, tag=in_tags[b], align_bytes=64)
             if b < 2:
-                nc.scalar.copy(tile[:].rearrange("p (v t) -> p v t", t=PACK), got[:].rearrange("p t v -> p v t"))
+                nc.scalar.copy(tile[:].rearrange("p (c i t) -> p c t i", i=4, t=PACK), got[:].rearrange("p t (c i) -> p c t i", i=4))
             else:
-                nc.vector.tensor_copy(tile[:].rearrange("p (v t) -> p v t", t=PACK), got[:].rearrange("p t v -> p v t"))
+                weave(nc.vector, tile[:], got[:])
             return tile
 
         def start_out(b, zq):
             v0, nv = pieces[b]
             accs = [psum.tile([P, nv], F32, name="res", tag=("z" if b < 2 else "acc")) for m in range(2)]
             for m in range(2):
-                mx(accs[m][:], w23, slice(m * P, (m + 1) * P), zq, slice(v0 % 256, v0 % 256 + nv), True, False)
+                mx(accs[m][:], w23, slice(m * P, (m + 1) * P), zq[0][:, v0 % 256:v0 % 256 + nv], zq[1][:, v0 % 256:v0 % 256 + nv], True, False)
             return accs
 
         def finish_out(b, accs, cq):
             v0, nv = pieces[b]
             res = sb("res%d" % b, [P, 2, nv], F32)
             for m in range(2):
-                mx(accs[m][:], w23, slice(N + m * P, N + (m + 1) * P), cq, slice(0, nv), False, True)
-                if m == 0 or b != 1:
+                mx(accs[m][:], w23, slice(N + m * P, N + (m + 1) * P), cq[0][:], cq[1][:], False, True)
+                if m == 0 or b != 2:
                     nc.scalar.copy(res[:, m, :], accs[m][:])
                 else:
                     nc.vector.tensor_copy(res[:, m, :], accs[m][:])
             nc.sync.dma_start(out[:, v0:v0 + nv].rearrange("(m p) v -> p m v", p=P), res[:])
 
         w23 = quantize("w23", w23_in[:])
-        c_in = [gather_cen(b) for b in range(3)]
-        zq = quantize("z0", z_in[0][:])
-        finish_out(0, start_out(0, zq), quantize("c0", c_in[0][:]))
-        zq = quantize("z1", z_in[1][:])
-        accs = [start_out(b, zq) for b in (1, 2)]
-        finish_out(2, accs[1], quantize("c2", c_in[2][:]))
-        finish_out(1, accs[0], quantize("c1", c_in[1][:]))
+        c_in = [gather_cen(b) for b in range(2)]
+        zq = [quantize("z%d" % b, z_in[b][:]) for b in range(2)]
+        accs = [start_out(b, zq[min(b, 1)]) for b in range(3)]
+        finish_out(0, accs[0], quantize("c0", c_in[0][:]))
+        c_in.append(gather_cen(2))
+        for b in (1, 2):
+            finish_out(b, accs[b], quantize("c%d" % b, c_in[b][:]))

@@ -22,7 +22,7 @@ HALF = 512
 
 CHUNKS = [
     [(0, 512, 256), (512, 512, 256), (1024, 512, 256), (1536, 512, 352)],
-    [(0, 512, 0), (512, 512, 192), (1024, 512, 192), (1536, 256, 128), (1792, 128, 0), (1920, 128, 128)],
+    [(0, 512, 128), (512, 512, 256), (1024, 512, 256), (1536, 256, 128), (1792, 128, 0), (1920, 128, 128)],
 ]
 
 
@@ -151,7 +151,7 @@ def tile_picked_sagecat_mean_e_kernel(tc, xT, w1, w2, w3, offs, cen, pos1, pos2,
             mx(acc, w1_q[1, t][0], w1_q[1, t][1], xw1[a], xs[4:P, cols], False, True)
 
         h = []
-        bank_tags = [None, ("acc", "z"), ("z", "z"), ("acc", "acc")]
+        bank_tags = [None, ("acc", "acc"), ("acc", "acc"), ("acc", "acc")]
         for t in range(PACK):
             plane = sb("h%d" % t, [P, S], F32)
             if t == 0:
@@ -183,7 +183,7 @@ def tile_picked_sagecat_mean_e_kernel(tc, xT, w1, w2, w3, offs, cen, pos1, pos2,
 
         z_sum = [psum.tile([P, PACK, P], F32, name="zsum%d" % vt, tag="z") for vt in range(4)]
         z_back = None
-        shared = {(3, 0): "c_got0", (3, 1): "c_got1"}
+        shared = {(2, 2): "c_got0", (2, 3): "c_got1"}
         for t in range(PACK):
             for d in range(4):
                 if (t, d) in shared:

@@ -18,65 +18,38 @@ RELU = mybir.ActivationFunctionType.Relu
 P = 128
 PACK = 4
 K_PASS = P * PACK
-HALF = 512
+BANK = 512
+GROUP = 16
+SCALE_ROWS = 4
+NEIGHBOURS = 4
+V_TILES = V // P
 
-CHUNKS = [
-    [(0, 512, 256), (512, 512, 256), (1024, 512, 256), (1536, 512, 352)],
-    [(0, 512, 128), (512, 512, 256), (1024, 512, 256), (1536, 256, 128), (1792, 128, 0), (1920, 128, 128)],
+X_LOADS = [
+    [[(512, 256), (512, 256)], [(512, 256)], [(512, 352)]],
+    [[(512, 128)], [(512, 256)], [(512, 256)], [(256, 128)], [(128, 0)], [(128, 128)]],
 ]
+SPANS = [(0, 512), (512, 256), (768, 256)]
+PIECES = [(0, 256), (256, 128), (384, 128)]
+Z_HALF = V // 2
 
 
 def tile_picked_sagecat_mean_e_kernel(tc, xT, w1, w2, w3, offs, cen, pos1, pos2, pos3, pos4, out):
     nc = tc.nc
     with ExitStack() as ctx:
         keep = ctx.enter_context(tc.tile_pool(name="keep", bufs=1))
-        ring = ctx.enter_context(tc.tile_pool(name="ring", bufs=8))
+        ring = ctx.enter_context(tc.tile_pool(name="ring", bufs=4))
         psum = ctx.enter_context(tc.psum_pool(name="psum", bufs=4))
 
-        def sb(name, shape, dtype):
-            return keep.tile(shape, dtype, name=name, align_bytes=64)
+        def sb(name, shape, dtype, slot=None):
+            return keep.tile(shape, dtype, name=name, tag=(slot or name), align_bytes=64)
 
         def load_list(name, src):
             tile = sb(name, list(src.shape), U16)
             nc.sync.dma_start(tile[:], src)
             return tile
 
-        def quantize(name, src, tag=None):
-            width = src.shape[1] // PACK
-            codes = keep.tile([P, width], U32, name=name + "_codes", tag=(tag or name + "_codes"), align_bytes=64)
-            scales = sb(name + "_scales", [P, width], U8)
-            nc.vector.quantize_mx(out=codes[:].bitcast(FP8X4), scales=scales[:], in_=src)
-            return codes, scales
-
-        def mx(acc, lhs, lcols, rhs, rhs_scale, start, stop):
-            nc.tensor.matmul_mx(out=acc, lhsT=lhs[0][:, lcols].bitcast(FP8X4), lhsT_scale=lhs[1][:, lcols],
-                                rhs=rhs.bitcast(FP8X4), rhs_scale=rhs_scale, start=start, stop=stop)
-
-        ident = sb("ident", [P, P], F32)
-        make_identity(nc, ident[:])
-
-        x_raw = {}
-        lists = {}
-        for g in range(2):
-            rows = xT[g * K_PASS:(g + 1) * K_PASS, :].rearrange("(p j) t -> p j t", j=PACK)
-            for c0, width, vcols in CHUNKS[g]:
-                raw = sb("x%d_%d" % (g, c0), [P, PACK, width], F32)
-                nc.sync.dma_start(raw[:], rows[:, :, c0:c0 + width])
-                x_raw[g, c0] = raw
-            if g == 0:
-                lists["offs"] = load_list("offs", offs)
-        w1_raw = []
-        for g in range(2):
-            raw = sb("w1_raw%d" % g, [P, PACK, H], F32)
-            nc.sync.dma_start(raw[:], w1[g * K_PASS:(g + 1) * K_PASS, :].rearrange("(p j) c -> p j c", j=PACK))
-            w1_raw.append(raw)
-        for name, src in (("pos1", pos1), ("pos2", pos2), ("pos3", pos3), ("pos4", pos4), ("cen", cen)):
-            lists[name] = load_list(name, src)
-        w23_raw = []
-        for name, src in (("w3_raw", w3), ("w2_raw", w2)):
-            raw = sb(name, [P, PACK, N], F32)
-            nc.sync.dma_start(raw[:], src.rearrange("(p j) c -> p j c", j=PACK))
-            w23_raw.append(raw)
+        def entries(tile, first, count):
+            return tile[:, first // GROUP:(first + count) // GROUP]
 
         def weave(eng, dst, src):
             dst = dst.rearrange("p (c i t) -> p c t i", i=4, t=PACK)
@@ -86,165 +59,207 @@ def tile_picked_sagecat_mean_e_kernel(tc, xT, w1, w2, w3, offs, cen, pos1, pos2,
             else:
                 nc.scalar.activation(dst, src, COPY)
 
-        x_scales = sb("x_scales", [P, T], U8)
-        nc.gpsimd.memset(x_scales[:].bitcast(U32), 0)
+        def quantize(name, src, slot=None):
+            width = src.shape[1] // PACK
+            words = sb(name + "_words", [P, width], U32, slot)
+            scales = sb(name + "_scales", [P, width], U8)
+            nc.vector.quantize_mx(out=words[:].bitcast(FP8X4), scales=scales[:], in_=src)
+            return words, scales
 
-        def quantize_x(g):
-            words = keep.tile([P, T], U32, name="x_words", tag="x_words%d" % g, align_bytes=64)
-            for c0, width, vcols in CHUNKS[g]:
-                tile = ring.tile([P, width * PACK], BF16, name="x_in", tag="x_in", bufs=4, align_bytes=64)
-                scols = width - vcols
-                if scols:
-                    weave(nc.scalar, tile[:, 0:scols * PACK], x_raw[g, c0][:, :, 0:scols])
-                if vcols:
-                    weave(nc.vector, tile[:, scols * PACK:width * PACK], x_raw[g, c0][:, :, scols:width])
-                nc.vector.quantize_mx(out=words[:, c0:c0 + width].bitcast(FP8X4), scales=x_scales[4 * g:P, c0:c0 + width], in_=tile[:])
+        def mx(acc, weights, cols, words, scales, start, stop):
+            nc.tensor.matmul_mx(out=acc, lhsT=weights[0][:, cols].bitcast(FP8X4), lhsT_scale=weights[1][:, cols],
+                                rhs=words.bitcast(FP8X4), rhs_scale=scales, start=start, stop=stop)
+
+        ident = sb("ident", [P, P], F32)
+        make_identity(nc, ident[:])
+
+        x_runs = []
+        for g in range(2):
+            rows = xT[g * K_PASS:(g + 1) * K_PASS, :].rearrange("(p j) t -> p j t", j=PACK)
+            runs = []
+            c0 = 0
+            for load in X_LOADS[g]:
+                total = sum(width for width, on_vector in load)
+                raw = sb("x_raw%d_%d" % (g, c0), [P, PACK, total], F32)
+                nc.sync.dma_start(raw[:], rows[:, :, c0:c0 + total])
+                first = 0
+                for width, on_vector in load:
+                    runs.append((c0 + first, width, on_vector, raw[:, :, first:first + width]))
+                    first = first + width
+                c0 = c0 + total
+            x_runs.append(runs)
+            if g == 0:
+                offs_sb = load_list("offs", offs)
+        w1_raw = []
+        for g in range(2):
+            raw = sb("w1_raw%d" % g, [P, PACK, H], F32)
+            nc.sync.dma_start(raw[:], w1[g * K_PASS:(g + 1) * K_PASS, :].rearrange("(p j) c -> p j c", j=PACK))
+            w1_raw.append(raw)
+        pos_sb = [load_list("pos%d" % (d + 1), src) for d, src in enumerate((pos1, pos2, pos3, pos4))]
+        cen_sb = load_list("cen", cen)
+        w32_raw = []
+        for name, src in (("w3_raw", w3), ("w2_raw", w2)):
+            raw = sb(name, [P, PACK, N], F32)
+            nc.sync.dma_start(raw[:], src.rearrange("(p j) c -> p j c", j=PACK))
+            w32_raw.append(raw)
+
+        all_scales = sb("all_scales", [P, T], U8)
+        nc.gpsimd.memset(all_scales[:].bitcast(U32), 0)
+
+        def quantize_nodes(g):
+            words = sb("all_words%d" % g, [P, T], U32)
+            for c0, width, on_vector, raw in x_runs[g]:
+                woven = ring.tile([P, width * PACK], BF16, name="x_woven", tag="x_woven", align_bytes=64)
+                on_scalar = width - on_vector
+                if on_scalar:
+                    weave(nc.scalar, woven[:, 0:on_scalar * PACK], raw[:, :, 0:on_scalar])
+                if on_vector:
+                    weave(nc.vector, woven[:, on_scalar * PACK:width * PACK], raw[:, :, on_scalar:width])
+                nc.vector.quantize_mx(out=words[:, c0:c0 + width].bitcast(FP8X4),
+                                      scales=all_scales[SCALE_ROWS * g:P, c0:c0 + width], in_=woven[:])
             return words
 
-        def pick(name, src, dtype, tag, first, count):
-            tile = keep.tile([P, count], dtype, name=name, tag=tag, align_bytes=64)
-            nc.vector.tensor_copy(tile[:], src[:].indirect(lists["offs"][:, first // 16:(first + count) // 16]))
+        def pick(name, src, dtype, first, count, slot=None):
+            tile = sb(name, [P, count], dtype, slot)
+            nc.vector.tensor_copy(tile[:], src[:].indirect(entries(offs_sb, first, count)))
             return tile
 
-        all0 = quantize_x(0)
-        xw0 = pick("xw0", all0, U32, "xw0", 0, S)
-        all1 = quantize_x(1)
+        x_words0 = pick("x_words0", quantize_nodes(0), U32, 0, S)
+        all_words1 = quantize_nodes(1)
 
-        def weave_w1(g, t0, nt, tag, eng):
-            tile = keep.tile([P, nt * P * PACK], BF16, name="w1_in%d_%d" % (g, t0), tag=tag, align_bytes=64)
+        def weave_w1(g, t0, planes, slot=None):
+            woven = sb("w1_woven%d_%d" % (g, t0), [P, planes * K_PASS], BF16, slot)
             src = w1_raw[g][:].rearrange("p j (m t) -> p m j t", t=PACK)
-            if nt == 1:
-                nc.scalar.activation(tile[:].rearrange("p (m j) -> p m j", j=PACK), src[:, :, :, t0], COPY)
-            elif eng is nc.vector:
-                nc.vector.tensor_copy(tile[:].rearrange("p (t m j) -> p m j t", t=nt, j=PACK), src[:, :, :, t0:t0 + nt])
+            if planes == 1:
+                nc.scalar.activation(woven[:].rearrange("p (m j) -> p m j", j=PACK), src[:, :, :, t0], COPY)
             else:
-                nc.scalar.activation(tile[:].rearrange("p (t m j) -> p m j t", t=nt, j=PACK), src[:, :, :, t0:t0 + nt], COPY)
-            return tile
+                nc.scalar.activation(woven[:].rearrange("p (t m j) -> p m j t", t=planes, j=PACK), src[:, :, :, t0:t0 + planes], COPY)
+            return woven
 
         w1_q = {}
 
-        def quantize_w1(g, t0, nt, tile, tag):
-            q = quantize("w1_%d_%d" % (g, t0), tile[:], tag)
-            for t in range(nt):
-                w1_q[g, t0 + t] = (q, slice(t * P, (t + 1) * P))
+        def quantize_w1(g, t0, planes, woven, slot=None):
+            weights = quantize("w1_%d_%d" % (g, t0), woven[:], slot)
+            for t in range(planes):
+                w1_q[g, t0 + t] = (weights, slice(t * P, (t + 1) * P))
 
-        in_a = weave_w1(0, 0, 2, "wa", nc.scalar)
-        in_e = weave_w1(0, 2, 2, "we", nc.scalar)
-        in_b = weave_w1(1, 0, 1, "wb", nc.scalar)
-        in_c = weave_w1(1, 1, 1, "wc", nc.scalar)
-        xs = pick("xs", x_scales, U8, "xs", 0, S)
-        quantize_w1(0, 0, 2, in_a, "qa")
-        spans = [(0, 512), (512, 256), (768, 256)]
-        early = pick("xw1a", all1, U32, "wa", 0, 768)
-        xw1 = [early[:, 0:512], early[:, 512:768]]
-        quantize_w1(1, 0, 1, in_b, "qb")
-        xw1.append(pick("xw1c", all1, U32, "wb", *spans[2])[:])
-        quantize_w1(1, 1, 1, in_c, "qc")
-        quantize_w1(0, 2, 2, in_e, "wc")
+        woven_00 = weave_w1(0, 0, 2)
+        woven_02 = weave_w1(0, 2, 2)
+        woven_10 = weave_w1(1, 0, 1)
+        woven_11 = weave_w1(1, 1, 1)
+        x_scales = pick("x_scales", all_scales, U8, 0, S)
+        quantize_w1(0, 0, 2, woven_00)
+        early = pick("x_words1_early", all_words1, U32, 0, SPANS[2][0], "w1_woven0_0")
+        x_words1 = [early[:, first:first + count] for first, count in SPANS[:2]]
+        quantize_w1(1, 0, 1, woven_10)
+        x_words1.append(pick("x_words1_late", all_words1, U32, SPANS[2][0], SPANS[2][1], "w1_woven1_0")[:])
+        quantize_w1(1, 1, 1, woven_11)
+        quantize_w1(0, 2, 2, woven_02, "w1_woven1_1")
 
         def first_pass(acc, t, a):
-            cols = slice(spans[a][0], spans[a][0] + spans[a][1])
-            mx(acc, w1_q[0, t][0], w1_q[0, t][1], xw0[:, cols], xs[:, cols], True, False)
+            cols = slice(SPANS[a][0], SPANS[a][0] + SPANS[a][1])
+            mx(acc, w1_q[0, t][0], w1_q[0, t][1], x_words0[:, cols], x_scales[:, cols], True, False)
 
         def second_pass(acc, t, a):
-            cols = slice(spans[a][0], spans[a][0] + spans[a][1])
-            mx(acc, w1_q[1, t][0], w1_q[1, t][1], xw1[a], xs[4:P, cols], False, True)
+            cols = slice(SPANS[a][0], SPANS[a][0] + SPANS[a][1])
+            mx(acc, w1_q[1, t][0], w1_q[1, t][1], x_words1[a], x_scales[SCALE_ROWS:P, cols], False, True)
 
         h = []
-        bank_tags = [None, ("acc", "acc"), ("acc", "acc"), ("acc", "acc")]
         for t in range(PACK):
             plane = sb("h%d" % t, [P, S], F32)
             if t == 0:
-                accs = [psum.tile([P, n], F32, name="acc", tag="acc") for first, n in spans]
-                for a in range(3):
+                accs = [psum.tile([P, count], F32, name="acc", tag="acc") for first, count in SPANS]
+                for a in range(len(SPANS)):
                     first_pass(accs[a][:], t, a)
-                for a, (first, n) in enumerate(spans):
+                for a, (first, count) in enumerate(SPANS):
                     second_pass(accs[a][:], t, a)
-                    if a < 2:
-                        nc.scalar.activation(plane[:, first:first + n], accs[a][:], RELU)
+                    if a < len(SPANS) - 1:
+                        nc.scalar.activation(plane[:, first:first + count], accs[a][:], RELU)
                     else:
-                        nc.vector.tensor_scalar_max(plane[:, first:first + n], accs[a][:], 0.0)
-                quantize_w1(1, 2, 2, weave_w1(1, 2, 2, "qb", nc.scalar), "qe")
+                        nc.vector.tensor_scalar_max(plane[:, first:first + count], accs[a][:], 0.0)
+                quantize_w1(1, 2, 2, weave_w1(1, 2, 2, "w1_1_0_words"))
             else:
-                accs = [psum.tile([P, HALF], F32, name="acc", tag=tag) for tag in bank_tags[t]]
+                accs = [psum.tile([P, BANK], F32, name="acc", tag="acc") for half in range(2)]
                 first_pass(accs[0][:], t, 0)
                 second_pass(accs[0][:], t, 0)
-                nc.scalar.activation(plane[:, 0:HALF], accs[0][:], RELU)
+                nc.scalar.activation(plane[:, 0:BANK], accs[0][:], RELU)
                 for a in (1, 2):
-                    part = accs[1][:, spans[a][0] - HALF:spans[a][0] - HALF + spans[a][1]]
+                    part = accs[1][:, SPANS[a][0] - BANK:SPANS[a][0] - BANK + SPANS[a][1]]
                     first_pass(part, t, a)
                     second_pass(part, t, a)
-                nc.scalar.activation(plane[:, HALF:S], accs[1][:], RELU)
+                nc.scalar.activation(plane[:, BANK:S], accs[1][:], RELU)
             h.append(plane)
 
-        w23_in = keep.tile([P, 2 * N * PACK], BF16, name="w23_in", tag="qe", align_bytes=64)
+        w32_woven = sb("w32_woven", [P, 2 * N * PACK], BF16, "w1_1_2_words")
         for i in range(2):
-            weave(nc.scalar, w23_in[:, i * N * PACK:(i + 1) * N * PACK], w23_raw[i][:])
+            weave(nc.scalar, w32_woven[:, i * N * PACK:(i + 1) * N * PACK], w32_raw[i][:])
 
-        z_sum = [psum.tile([P, PACK, P], F32, name="zsum%d" % vt, tag="z") for vt in range(4)]
-        z_back = None
-        shared = {(2, 2): "c_got0", (2, 3): "c_got1"}
+        z_sum = [psum.tile([P, PACK, P], F32, name="z_sum", tag="z") for vt in range(V_TILES)]
+        lent = {(2, 2): "cen_got0", (2, 3): "cen_got1"}
         for t in range(PACK):
-            for d in range(4):
-                if (t, d) in shared:
-                    got = keep.tile([P, V], F32, name="got", tag=shared[t, d], align_bytes=64)
+            for d in range(NEIGHBOURS):
+                if (t, d) in lent:
+                    got = sb("got", [P, V], F32, lent[t, d])
                 else:
-                    got = ring.tile([P, V], F32, name="got", tag="got", bufs=14)
-                nc.vector.tensor_copy(got[:], h[t][:].indirect(lists["pos%d" % (d + 1)][:]))
-                for vt in range(4):
-                    nc.tensor.matmul(z_sum[vt][:, t, :], got[:, vt * P:(vt + 1) * P], ident[:], start=(d == 0), stop=(d == 3), is_transpose=True)
+                    got = ring.tile([P, V], F32, name="got", tag="got", bufs=PACK * NEIGHBOURS - len(lent))
+                nc.vector.tensor_copy(got[:], h[t][:].indirect(pos_sb[d][:]))
+                for vt in range(V_TILES):
+                    nc.tensor.matmul(z_sum[vt][:, t, :], got[:, vt * P:(vt + 1) * P], ident[:],
+                                     start=(d == 0), stop=(d == NEIGHBOURS - 1), is_transpose=True)
+            if t == 1:
+                z_back = [psum.tile([P, 2, Z_HALF], F32, name="z_back", tag="acc") for half in range(2)]
             if t % 2 == 1:
                 u = t // 2
-                if z_back is None:
-                    z_back = [psum.tile([P, 2, 256], F32, name="zback%d" % b, tag="acc") for b in range(2)]
-                for vt in range(4):
-                    zt = keep.tile([P, 2 * P], BF16, name="zt", tag="zt%d_%d" % (u, vt), align_bytes=64)
-                    nc.scalar.activation(zt[:].rearrange("v (p e) -> v p e", e=2),
-                                         z_sum[vt][:, 2 * u:2 * u + 2, :].rearrange("v e p -> v p e"), COPY, scale=0.25)
-                    nc.tensor.transpose(z_back[vt // 2][:, u, (vt % 2) * P:(vt % 2 + 1) * P], zt[:].bitcast(F32), ident[:])
-        z_in = [sb("z_in%d" % b, [P, 256 * PACK], BF16) for b in range(2)]
-        for b in range(2):
-            nc.scalar.copy(z_in[b][:].bitcast(F32).rearrange("p (v u) -> p v u", u=2), z_back[b][:].rearrange("p u v -> p v u"))
+                for vt in range(V_TILES):
+                    pairs = sb("z_pairs%d_%d" % (u, vt), [P, 2 * P], BF16)
+                    nc.scalar.activation(pairs[:].rearrange("v (p e) -> v p e", e=2),
+                                         z_sum[vt][:, 2 * u:2 * u + 2, :].rearrange("v e p -> v p e"), COPY, scale=1.0 / NEIGHBOURS)
+                    nc.tensor.transpose(z_back[vt // 2][:, u, (vt % 2) * P:(vt % 2 + 1) * P], pairs[:].bitcast(F32), ident[:])
+        z_woven = [sb("z_woven%d" % half, [P, Z_HALF * PACK], BF16) for half in range(2)]
+        for half in range(2):
+            nc.scalar.copy(z_woven[half][:].bitcast(F32).rearrange("p (v u) -> p v u", u=2), z_back[half][:].rearrange("p u v -> p v u"))
 
-        pieces = [(0, 256), (256, 128), (384, 128)]
-        got_tags = ["c_got0", "c_got1", "zt1_3"]
-        in_tags = ["zt1_3", "zt1_2", "c_in2"]
+        last = len(PIECES) - 1
+        got_slots = ["cen_got0", "cen_got1", "z_pairs1_3"]
+        woven_slots = ["z_pairs1_3", "z_pairs1_2", None]
 
         def gather_cen(b):
-            v0, nv = pieces[b]
-            got = keep.tile([P, PACK, nv], BF16, name="c_got%d" % b, tag=got_tags[b], align_bytes=64)
+            v0, count = PIECES[b]
+            got = sb("cen_got%d" % b, [P, PACK, count], BF16, got_slots[b])
             for t in range(PACK):
-                nc.vector.tensor_copy(got[:, t, :], h[t][:].indirect(lists["cen"][:, v0 // 16:(v0 + nv) // 16]))
-            tile = keep.tile([P, nv * PACK], BF16, name="c_in%d" % b, tag=in_tags[b], align_bytes=64)
-            if b < 2:
-                nc.scalar.copy(tile[:].rearrange("p (c i t) -> p c t i", i=4, t=PACK), got[:].rearrange("p t (c i) -> p c t i", i=4))
+                nc.vector.tensor_copy(got[:, t, :], h[t][:].indirect(entries(cen_sb, v0, count)))
+            woven = sb("cen_woven%d" % b, [P, count * PACK], BF16, woven_slots[b])
+            if b < last:
+                nc.scalar.copy(woven[:].rearrange("p (c i t) -> p c t i", i=4, t=PACK), got[:].rearrange("p t (c i) -> p c t i", i=4))
             else:
-                weave(nc.vector, tile[:], got[:])
-            return tile
+                weave(nc.vector, woven[:], got[:])
+            return woven
 
-        def start_out(b, zq):
-            v0, nv = pieces[b]
-            accs = [psum.tile([P, nv], F32, name="res", tag=("z" if b < 2 else "acc")) for m in range(2)]
-            for m in range(2):
-                mx(accs[m][:], w23, slice(m * P, (m + 1) * P), zq[0][:, v0 % 256:v0 % 256 + nv], zq[1][:, v0 % 256:v0 % 256 + nv], True, False)
+        def open_out(b):
+            v0, count = PIECES[b]
+            words, scales = z_q[v0 // Z_HALF]
+            cols = slice(v0 % Z_HALF, v0 % Z_HALF + count)
+            accs = [psum.tile([P, count], F32, name="out_acc", tag=("z" if b < last else "acc")) for m in range(N // P)]
+            for m in range(N // P):
+                mx(accs[m][:], w32, slice(m * P, (m + 1) * P), words[:, cols], scales[:, cols], True, False)
             return accs
 
-        def finish_out(b, accs, cq):
-            v0, nv = pieces[b]
-            res = sb("res%d" % b, [P, 2, nv], F32)
-            for m in range(2):
-                mx(accs[m][:], w23, slice(N + m * P, N + (m + 1) * P), cq[0][:], cq[1][:], False, True)
-                if m == 0 or b != 2:
+        def close_out(b, accs, cen_q):
+            v0, count = PIECES[b]
+            res = sb("res%d" % b, [P, N // P, count], F32)
+            for m in range(N // P):
+                mx(accs[m][:], w32, slice(N + m * P, N + (m + 1) * P), cen_q[0][:], cen_q[1][:], False, True)
+                if m == 0 or b < last:
                     nc.scalar.copy(res[:, m, :], accs[m][:])
                 else:
                     nc.vector.tensor_copy(res[:, m, :], accs[m][:])
-            nc.sync.dma_start(out[:, v0:v0 + nv].rearrange("(m p) v -> p m v", p=P), res[:])
+            nc.sync.dma_start(out[:, v0:v0 + count].rearrange("(m p) v -> p m v", p=P), res[:])
 
-        w23 = quantize("w23", w23_in[:])
-        c_in = [gather_cen(b) for b in range(2)]
-        zq = [quantize("z%d" % b, z_in[b][:]) for b in range(2)]
-        accs = [start_out(b, zq[min(b, 1)]) for b in range(3)]
-        finish_out(0, accs[0], quantize("c0", c_in[0][:]))
-        c_in.append(gather_cen(2))
-        for b in (1, 2):
-            finish_out(b, accs[b], quantize("c%d" % b, c_in[b][:]))
+        w32 = quantize("w32", w32_woven[:])
+        cen_woven = [gather_cen(b) for b in range(last)]
+        z_q = [quantize("z%d" % half, z_woven[half][:]) for half in range(2)]
+        out_accs = [open_out(b) for b in range(len(PIECES))]
+        close_out(0, out_accs[0], quantize("cen0", cen_woven[0][:]))
+        cen_woven.append(gather_cen(last))
+        for b in range(1, len(PIECES)):
+            close_out(b, out_accs[b], quantize("cen%d" % b, cen_woven[b][:]))

@@ -26,10 +26,12 @@ V_TILES = V // P
 
 X_LOADS = [
     [[(512, 256), (512, 256)], [(512, 256)], [(512, 352)]],
-    [[(512, 128)], [(512, 256)], [(512, 256)], [(256, 128)], [(128, 0)], [(128, 128)]],
+    [[(512, 128)], [(512, 256)], [(512, 256)], [(256, 128)], [(128, 0)], [(64, 64), (64, 0)]],
 ]
-SPANS = [(0, 512), (512, 256), (768, 256)]
+SPANS = [(0, 256), (256, 256), (512, 256), (768, 128), (896, 128)]
 PIECES = [(0, 256), (256, 128), (384, 128)]
+W1_LOADS = [2, 1]
+RUN = 8
 Z_HALF = V // 2
 
 
@@ -37,11 +39,15 @@ def tile_picked_sagecat_mean_e_kernel(tc, xT, w1, w2, w3, offs, cen, pos1, pos2,
     nc = tc.nc
     with ExitStack() as ctx:
         keep = ctx.enter_context(tc.tile_pool(name="keep", bufs=1))
+        placed = ctx.enter_context(tc.tile_pool(name="placed", bufs=1))
         ring = ctx.enter_context(tc.tile_pool(name="ring", bufs=4))
         psum = ctx.enter_context(tc.psum_pool(name="psum", bufs=4))
 
         def sb(name, shape, dtype, slot=None):
             return keep.tile(shape, dtype, name=name, tag=(slot or name), align_bytes=64)
+
+        def at(name, shape, dtype, offset):
+            return placed.tile(shape, dtype, name=name, offset=offset, align_bytes=64)
 
         def load_list(name, src):
             tile = sb(name, list(src.shape), U16)
@@ -59,10 +65,10 @@ def tile_picked_sagecat_mean_e_kernel(tc, xT, w1, w2, w3, offs, cen, pos1, pos2,
             else:
                 nc.scalar.activation(dst, src, COPY)
 
-        def quantize(name, src, slot=None):
+        def quantize(name, src, slot=None, scale_slot=None):
             width = src.shape[1] // PACK
-            words = sb(name + "_words", [P, width], U32, slot)
-            scales = sb(name + "_scales", [P, width], U8)
+            words = sb(name + "_words", [P, width], U32) if slot is None else slot
+            scales = sb(name + "_scales", [P, width], U8, scale_slot)
             nc.vector.quantize_mx(out=words[:].bitcast(FP8X4), scales=scales[:], in_=src)
             return words, scales
 
@@ -92,22 +98,29 @@ def tile_picked_sagecat_mean_e_kernel(tc, xT, w1, w2, w3, offs, cen, pos1, pos2,
                 offs_sb = load_list("offs", offs)
         w1_raw = []
         for g in range(2):
-            raw = sb("w1_raw%d" % g, [P, PACK, H], F32)
-            nc.sync.dma_start(raw[:], w1[g * K_PASS:(g + 1) * K_PASS, :].rearrange("(p j) c -> p j c", j=PACK))
-            w1_raw.append(raw)
+            rows = w1[g * K_PASS:(g + 1) * K_PASS, :].rearrange("(p j) c -> p j c", j=PACK)
+            width = H // W1_LOADS[g]
+            parts = []
+            for a in range(W1_LOADS[g]):
+                raw = sb("w1_raw%d_%d" % (g, a), [P, PACK, width], F32)
+                nc.sync.dma_start(raw[:], rows[:, :, a * width:(a + 1) * width])
+                parts.append(raw)
+            w1_raw.append(parts)
         pos_sb = [load_list("pos%d" % (d + 1), src) for d, src in enumerate((pos1, pos2, pos3, pos4))]
         cen_sb = load_list("cen", cen)
         w32_raw = []
         for name, src in (("w3_raw", w3), ("w2_raw", w2)):
             raw = sb(name, [P, PACK, N], F32)
-            nc.sync.dma_start(raw[:], src.rearrange("(p j) c -> p j c", j=PACK))
+            dealt = src.rearrange("(b t r) c -> t b r c", t=PACK, r=RUN)
+            for t in range(PACK):
+                nc.sync.dma_start(raw[:, t, :], dealt[t])
             w32_raw.append(raw)
 
         all_scales = sb("all_scales", [P, T], U8)
         nc.gpsimd.memset(all_scales[:].bitcast(U32), 0)
 
         def quantize_nodes(g):
-            words = sb("all_words%d" % g, [P, T], U32)
+            words = at("all_words1", [P, T], U32, 8192) if g else sb("all_words0", [P, T], U32)
             for c0, width, on_vector, raw in x_runs[g]:
                 woven = ring.tile([P, width * PACK], BF16, name="x_woven", tag="x_woven", align_bytes=64)
                 on_scalar = width - on_vector
@@ -116,7 +129,7 @@ def tile_picked_sagecat_mean_e_kernel(tc, xT, w1, w2, w3, offs, cen, pos1, pos2,
                 if on_vector:
                     weave(nc.vector, woven[:, on_scalar * PACK:width * PACK], raw[:, :, on_scalar:width])
                 nc.vector.quantize_mx(out=words[:, c0:c0 + width].bitcast(FP8X4),
-                                      scales=all_scales[SCALE_ROWS * g:P, c0:c0 + width], in_=woven[:])
+                                      scales=all_scales[SCALE_ROWS * (1 - g):P, c0:c0 + width], in_=woven[:])
             return words
 
         def pick(name, src, dtype, first, count, slot=None):
@@ -127,14 +140,11 @@ def tile_picked_sagecat_mean_e_kernel(tc, xT, w1, w2, w3, offs, cen, pos1, pos2,
         x_words0 = pick("x_words0", quantize_nodes(0), U32, 0, S)
         all_words1 = quantize_nodes(1)
 
-        def weave_w1(g, t0, planes, slot=None):
-            woven = sb("w1_woven%d_%d" % (g, t0), [P, planes * K_PASS], BF16, slot)
-            src = w1_raw[g][:].rearrange("p j (m t) -> p m j t", t=PACK)
-            if planes == 1:
-                nc.scalar.activation(woven[:].rearrange("p (m j) -> p m j", j=PACK), src[:, :, :, t0], COPY)
-            else:
-                nc.scalar.activation(woven[:].rearrange("p (t m j) -> p m j t", t=planes, j=PACK), src[:, :, :, t0:t0 + planes], COPY)
-            return woven
+        def weave_w1(woven, g, a, t, at, copy=nc.scalar.copy):
+            share = K_PASS // W1_LOADS[g]
+            src = w1_raw[g][a][:].rearrange("p j (b t u i) -> p t b u j i", t=PACK, u=2, i=4)
+            dst = woven[:, at * K_PASS + a * share:at * K_PASS + (a + 1) * share]
+            copy(dst.rearrange("p (b u i j) -> p b u j i", u=2, i=4, j=PACK), src[:, t])
 
         w1_q = {}
 
@@ -143,102 +153,120 @@ def tile_picked_sagecat_mean_e_kernel(tc, xT, w1, w2, w3, offs, cen, pos1, pos2,
             for t in range(planes):
                 w1_q[g, t0 + t] = (weights, slice(t * P, (t + 1) * P))
 
-        woven_00 = weave_w1(0, 0, 2)
-        woven_02 = weave_w1(0, 2, 2)
-        woven_10 = weave_w1(1, 0, 1)
-        woven_11 = weave_w1(1, 1, 1)
+        woven_00 = sb("w1_woven0_0", [P, 2 * K_PASS], BF16)
+        woven_02 = sb("w1_woven0_2", [P, 2 * K_PASS], BF16)
+        woven_10 = sb("w1_woven1_0", [P, K_PASS], BF16)
+        woven_11 = sb("w1_woven1_1", [P, K_PASS], BF16)
+        for woven, t0 in ((woven_00, 0), (woven_02, 2)):
+            for a in range(2):
+                for t in range(2):
+                    weave_w1(woven, 0, a, t0 + t, t)
+        woven_12 = sb("w1_woven1_2", [P, K_PASS], BF16)
+        places = [(woven_10, 0), (woven_11, 0), (woven_12, 0)]
+        for t in range(3):
+            weave_w1(places[t][0], 1, 0, t, places[t][1])
         x_scales = pick("x_scales", all_scales, U8, 0, S)
         quantize_w1(0, 0, 2, woven_00)
-        early = pick("x_words1_early", all_words1, U32, 0, SPANS[2][0], "w1_woven0_0")
-        x_words1 = [early[:, first:first + count] for first, count in SPANS[:2]]
+        early = pick("x_words1_early", all_words1, U32, 0, BANK, "w1_raw0_1")
         quantize_w1(1, 0, 1, woven_10)
-        x_words1.append(pick("x_words1_late", all_words1, U32, SPANS[2][0], SPANS[2][1], "w1_woven1_0")[:])
+        late = sb("x_words1_late", [P, BANK], U32, "w1_woven1_0")
+        for first, count in ((512, 256), (768, 256)):
+            nc.vector.tensor_copy(late[:, first - BANK:first - BANK + count], all_words1[:].indirect(entries(offs_sb, first, count)))
         quantize_w1(1, 1, 1, woven_11)
-        quantize_w1(0, 2, 2, woven_02, "w1_woven1_1")
+        woven_13 = at("w1_woven1_3", [P, K_PASS], BF16, 8192 + 2048)
+        weave_w1(woven_13, 1, 0, 3, 0, nc.vector.tensor_copy)
+        quantize_w1(0, 2, 2, woven_02, at("w1_0_2_words", [P, 2 * P], U32, 8192))
+        quantize_w1(1, 2, 1, woven_12)
+        quantize_w1(1, 3, 1, woven_13)
 
-        def first_pass(acc, t, a):
-            cols = slice(SPANS[a][0], SPANS[a][0] + SPANS[a][1])
-            mx(acc, w1_q[0, t][0], w1_q[0, t][1], x_words0[:, cols], x_scales[:, cols], True, False)
+        def first_pass(acc, t, first, count):
+            mx(acc, w1_q[0, t][0], w1_q[0, t][1], x_words0[:, first:first + count], x_scales[SCALE_ROWS:P, first:first + count], True, False)
 
-        def second_pass(acc, t, a):
-            cols = slice(SPANS[a][0], SPANS[a][0] + SPANS[a][1])
-            mx(acc, w1_q[1, t][0], w1_q[1, t][1], x_words1[a], x_scales[SCALE_ROWS:P, cols], False, True)
+        def second_pass(acc, t, first, count):
+            words = early[:, first:first + count] if first < BANK else late[:, first - BANK:first - BANK + count]
+            mx(acc, w1_q[1, t][0], w1_q[1, t][1], words, x_scales[:, first:first + count], False, True)
 
-        h = []
-        for t in range(PACK):
+        halves = [(0, BANK), (BANK, BANK)]
+        spans = [SPANS, halves, halves, halves]
+        tags = [["z"] + ["acc"] * 4, ["z", "acc"], ["acc"] * 2, ["acc"] * 2]
+        accs = {}
+
+        def open_plane(t):
+            accs[t] = [psum.tile([P, count], F32, name="acc", tag=tags[t][a]) for a, (first, count) in enumerate(spans[t])]
+            for a, (first, count) in enumerate(spans[t]):
+                if (t, a) != (1, 1):
+                    first_pass(accs[t][a][:], t, first, count)
+
+        def close_plane(t):
             plane = sb("h%d" % t, [P, S], F32)
-            if t == 0:
-                accs = [psum.tile([P, count], F32, name="acc", tag="acc") for first, count in SPANS]
-                for a in range(len(SPANS)):
-                    first_pass(accs[a][:], t, a)
-                for a, (first, count) in enumerate(SPANS):
-                    second_pass(accs[a][:], t, a)
-                    if a < len(SPANS) - 1:
-                        nc.scalar.activation(plane[:, first:first + count], accs[a][:], RELU)
-                    else:
-                        nc.vector.tensor_scalar_max(plane[:, first:first + count], accs[a][:], 0.0)
-                quantize_w1(1, 2, 2, weave_w1(1, 2, 2, "w1_1_0_words"))
-            else:
-                accs = [psum.tile([P, BANK], F32, name="acc", tag="acc") for half in range(2)]
-                first_pass(accs[0][:], t, 0)
-                second_pass(accs[0][:], t, 0)
-                nc.scalar.activation(plane[:, 0:BANK], accs[0][:], RELU)
-                for a in (1, 2):
-                    part = accs[1][:, SPANS[a][0] - BANK:SPANS[a][0] - BANK + SPANS[a][1]]
-                    first_pass(part, t, a)
-                    second_pass(part, t, a)
-                nc.scalar.activation(plane[:, BANK:S], accs[1][:], RELU)
-            h.append(plane)
+            for a, (first, count) in enumerate(spans[t]):
+                if (t, a) == (1, 1):
+                    first_pass(accs[t][a][:], t, first, count)
+                second_pass(accs[t][a][:], t, first, count)
+                nc.scalar.activation(plane[:, first:first + count], accs[t][a][:], RELU)
+            return plane
 
-        w32_woven = sb("w32_woven", [P, 2 * N * PACK], BF16, "w1_1_2_words")
+        open_plane(0)
+        open_plane(1)
+        h = [close_plane(0)]
+        h.append(close_plane(1))
+        for t in (2, 3):
+            open_plane(t)
+            h.append(close_plane(t))
+
+        w32_woven = sb("w32_woven", [P, 2 * N * PACK], BF16, "w1_1_3_words")
         for i in range(2):
             weave(nc.scalar, w32_woven[:, i * N * PACK:(i + 1) * N * PACK], w32_raw[i][:])
 
         z_sum = [psum.tile([P, PACK, P], F32, name="z_sum", tag="z") for vt in range(V_TILES)]
-        lent = {(2, 2): "cen_got0", (2, 3): "cen_got1"}
-        for t in range(PACK):
+
+        z_pairs = [sb("z_pairs0", [P, 8 * P], BF16), at("z_pairs1", [P, 8 * P], BF16, 4096)]
+
+        lent = {(2, 2): 0, (2, 3): 2048}
+
+        def gather_z(t, v0, count, into=None):
             for d in range(NEIGHBOURS):
                 if (t, d) in lent:
-                    got = sb("got", [P, V], F32, lent[t, d])
+                    got = at("got", [P, count], F32, lent[t, d])[:]
+                elif into is None:
+                    got = ring.tile([P, count], F32, name="got", tag="got", bufs=14)[:]
                 else:
-                    got = ring.tile([P, V], F32, name="got", tag="got", bufs=PACK * NEIGHBOURS - len(lent))
-                nc.vector.tensor_copy(got[:], h[t][:].indirect(pos_sb[d][:]))
-                for vt in range(V_TILES):
-                    nc.tensor.matmul(z_sum[vt][:, t, :], got[:, vt * P:(vt + 1) * P], ident[:],
+                    got = into[:, d, :]
+                nc.vector.tensor_copy(got, h[t][:].indirect(entries(pos_sb[d], v0, count)))
+                for a in range(count // P):
+                    nc.tensor.matmul(z_sum[v0 // P + a][:, t, :], got[:, a * P:(a + 1) * P], ident[:],
                                      start=(d == 0), stop=(d == NEIGHBOURS - 1), is_transpose=True)
-            if t == 1:
-                z_back = [psum.tile([P, 2, Z_HALF], F32, name="z_back", tag="acc") for half in range(2)]
-            if t % 2 == 1:
-                u = t // 2
-                for vt in range(V_TILES):
-                    pairs = sb("z_pairs%d_%d" % (u, vt), [P, 2 * P], BF16)
-                    nc.scalar.activation(pairs[:].rearrange("v (p e) -> v p e", e=2),
-                                         z_sum[vt][:, 2 * u:2 * u + 2, :].rearrange("v e p -> v p e"), COPY, scale=1.0 / NEIGHBOURS)
-                    nc.tensor.transpose(z_back[vt // 2][:, u, (vt % 2) * P:(vt % 2 + 1) * P], pairs[:].bitcast(F32), ident[:])
-        z_woven = [sb("z_woven%d" % half, [P, Z_HALF * PACK], BF16) for half in range(2)]
-        for half in range(2):
-            nc.scalar.copy(z_woven[half][:].bitcast(F32).rearrange("p (v u) -> p v u", u=2), z_back[half][:].rearrange("p u v -> p v u"))
 
-        last = len(PIECES) - 1
-        got_slots = ["cen_got0", "cen_got1", "z_pairs1_3"]
-        woven_slots = ["z_pairs1_3", "z_pairs1_2", None]
+        def turn_back(u, vt):
+            pairs = z_pairs[vt // 2][:, (2 * u + vt % 2) * 2 * P:(2 * u + vt % 2 + 1) * 2 * P]
+            nc.scalar.activation(pairs.rearrange("v (p e) -> v p e", e=2),
+                                 z_sum[vt][:, 2 * u:2 * u + 2, :].rearrange("v e p -> v p e"), COPY, scale=1.0 / NEIGHBOURS)
+            nc.tensor.transpose(z_back[vt // 2][:, u, (vt % 2) * P:(vt % 2 + 1) * P], pairs.bitcast(F32), ident[:])
 
-        def gather_cen(b):
-            v0, count = PIECES[b]
-            got = sb("cen_got%d" % b, [P, PACK, count], BF16, got_slots[b])
-            for t in range(PACK):
-                nc.vector.tensor_copy(got[:, t, :], h[t][:].indirect(entries(cen_sb, v0, count)))
-            woven = sb("cen_woven%d" % b, [P, count * PACK], BF16, woven_slots[b])
-            if b < last:
-                nc.scalar.copy(woven[:].rearrange("p (c i t) -> p c t i", i=4, t=PACK), got[:].rearrange("p t (c i) -> p c t i", i=4))
-            else:
-                weave(nc.vector, woven[:], got[:])
+        def weave_z(half):
+            woven = sb("z_woven%d" % half, [P, Z_HALF * PACK], BF16)
+            nc.scalar.copy(woven[:].bitcast(F32).rearrange("p (v u) -> p v u", u=2), z_back[half][:].rearrange("p u v -> p v u"))
             return woven
 
-        def open_out(b):
+        last = len(PIECES) - 1
+
+        def gather_cen(name, v0, count, offset):
+            got = at(name, [P, PACK, count], BF16, offset)
+            for t in range(PACK):
+                nc.vector.tensor_copy(got[:, t, :], h[t][:].indirect(entries(cen_sb, v0, count)))
+            return got
+
+        def weave_cen(b, got, woven):
+            if b < last:
+                nc.scalar.copy(woven[:].rearrange("p (c i t) -> p c t i", i=4, t=PACK), got.rearrange("p t (c i) -> p c t i", i=4))
+            else:
+                weave(nc.vector, woven[:], got)
+            return woven
+
+        def open_out(b, z_q):
             v0, count = PIECES[b]
-            words, scales = z_q[v0 // Z_HALF]
-            cols = slice(v0 % Z_HALF, v0 % Z_HALF + count)
+            words, scales = z_q
+            cols = slice(0, count)
             accs = [psum.tile([P, count], F32, name="out_acc", tag=("z" if b < last else "acc")) for m in range(N // P)]
             for m in range(N // P):
                 mx(accs[m][:], w32, slice(m * P, (m + 1) * P), words[:, cols], scales[:, cols], True, False)
@@ -255,11 +283,27 @@ def tile_picked_sagecat_mean_e_kernel(tc, xT, w1, w2, w3, offs, cen, pos1, pos2,
                     nc.vector.tensor_copy(res[:, m, :], accs[m][:])
             nc.sync.dma_start(out[:, v0:v0 + count].rearrange("(m p) v -> p m v", p=P), res[:])
 
+        gather_z(0, 0, V)
+        gather_z(1, 0, V)
+        z_back = [psum.tile([P, 2, Z_HALF], F32, name="z_back", tag="acc") for half in range(2)]
+        for vt in range(V_TILES):
+            turn_back(0, vt)
+        gather_z(2, 0, V)
         w32 = quantize("w32", w32_woven[:])
-        cen_woven = [gather_cen(b) for b in range(last)]
-        z_q = [quantize("z%d" % half, z_woven[half][:]) for half in range(2)]
-        out_accs = [open_out(b) for b in range(len(PIECES))]
-        close_out(0, out_accs[0], quantize("cen0", cen_woven[0][:]))
-        cen_woven.append(gather_cen(last))
-        for b in range(1, len(PIECES)):
-            close_out(b, out_accs[b], quantize("cen%d" % b, cen_woven[b][:]))
+        gather_z(3, 0, V)
+        for vt in range(V_TILES):
+            turn_back(1, vt)
+        got0 = gather_cen("cen_got0", 0, 256, 0)
+        got1 = gather_cen("cen_got1", 256, 128, 2048)
+        z_woven0 = weave_z(0)
+        cen_woven0 = weave_cen(0, got0[:], at("cen_woven0", [P, 256 * PACK], BF16, 6080))
+        z_woven1 = weave_z(1)
+        cen_woven1 = weave_cen(1, got1[:], at("cen_woven1", [P, P * PACK], BF16, 4096))
+        out0 = open_out(0, quantize("z0", z_woven0[:]))
+        close_out(0, out0, quantize("cen0", cen_woven0[:]))
+        got2 = gather_cen("cen_got2", 384, 128, 0)
+        out1 = open_out(1, quantize("z1", z_woven1[:, 0:P * PACK]))
+        close_out(1, out1, quantize("cen1", cen_woven1[:]))
+        cen_woven2 = weave_cen(2, got2[:], at("cen_woven2", [P, P * PACK], BF16, 2560))
+        out2 = open_out(2, quantize("z2", z_woven1[:, P * PACK:2 * P * PACK], at("z2_words", [P, P], U32, 2048)))
+        close_out(2, out2, quantize("cen2", cen_woven2[:]))

@@ -25,13 +25,14 @@ NEIGHBOURS = 4
 V_TILES = V // P
 
 X_LOADS = [
-    [[(512, 256), (512, 256)], [(512, 256)], [(512, 352)]],
-    [[(512, 128)], [(512, 256)], [(512, 256)], [(256, 128)], [(128, 0)], [(64, 64), (64, 0)]],
+    [[(512, 256), (512, 256)], [(512, 256)], [(256, 256), (256, 0)]],
+    [[(512, 0)], [(512, 256)], [(256, 256), (256, 0)], [(128, 128), (128, 0)], [(128, 0)], [(64, 64), (64, 0)]],
 ]
 SPANS = [(0, 256), (256, 256), (512, 256), (768, 128), (896, 128)]
 PIECES = [(0, 256), (256, 128), (384, 128)]
 W1_LOADS = [2, 1]
 RUN = 8
+EARLY = 768
 Z_HALF = V // 2
 
 
@@ -122,7 +123,10 @@ def tile_picked_sagecat_mean_e_kernel(tc, xT, w1, w2, w3, offs, cen, pos1, pos2,
         def quantize_nodes(g):
             words = at("all_words1", [P, T], U32, 8192) if g else sb("all_words0", [P, T], U32)
             for c0, width, on_vector, raw in x_runs[g]:
-                woven = ring.tile([P, width * PACK], BF16, name="x_woven", tag="x_woven", align_bytes=64)
+                if width == BANK:
+                    woven = ring.tile([P, width * PACK], BF16, name="x_woven", tag="x_woven", align_bytes=64)
+                else:
+                    woven = sb("x_woven%d_%d" % (g, c0), [P, width * PACK], BF16)
                 on_scalar = width - on_vector
                 if on_scalar:
                     weave(nc.scalar, woven[:, 0:on_scalar * PACK], raw[:, :, 0:on_scalar])
@@ -167,11 +171,10 @@ def tile_picked_sagecat_mean_e_kernel(tc, xT, w1, w2, w3, offs, cen, pos1, pos2,
             weave_w1(places[t][0], 1, 0, t, places[t][1])
         x_scales = pick("x_scales", all_scales, U8, 0, S)
         quantize_w1(0, 0, 2, woven_00)
-        early = pick("x_words1_early", all_words1, U32, 0, BANK, "w1_raw0_1")
+        early = pick("x_words1_early", all_words1, U32, 0, EARLY, "w1_raw0_1")
         quantize_w1(1, 0, 1, woven_10)
-        late = sb("x_words1_late", [P, BANK], U32, "w1_woven1_0")
-        for first, count in ((512, 256), (768, 256)):
-            nc.vector.tensor_copy(late[:, first - BANK:first - BANK + count], all_words1[:].indirect(entries(offs_sb, first, count)))
+        late = sb("x_words1_late", [P, S - EARLY], U32, "w1_woven1_0")
+        nc.vector.tensor_copy(late[:], all_words1[:].indirect(entries(offs_sb, EARLY, S - EARLY)))
         quantize_w1(1, 1, 1, woven_11)
         woven_13 = at("w1_woven1_3", [P, K_PASS], BF16, 8192 + 2048)
         weave_w1(woven_13, 1, 0, 3, 0, nc.vector.tensor_copy)
@@ -183,36 +186,37 @@ def tile_picked_sagecat_mean_e_kernel(tc, xT, w1, w2, w3, offs, cen, pos1, pos2,
             mx(acc, w1_q[0, t][0], w1_q[0, t][1], x_words0[:, first:first + count], x_scales[SCALE_ROWS:P, first:first + count], True, False)
 
         def second_pass(acc, t, first, count):
-            words = early[:, first:first + count] if first < BANK else late[:, first - BANK:first - BANK + count]
+            words = early[:, first:first + count] if first < EARLY else late[:, first - EARLY:first - EARLY + count]
             mx(acc, w1_q[1, t][0], w1_q[1, t][1], words, x_scales[:, first:first + count], False, True)
 
-        halves = [(0, BANK), (BANK, BANK)]
-        spans = [SPANS, halves, halves, halves]
-        tags = [["z"] + ["acc"] * 4, ["z", "acc"], ["acc"] * 2, ["acc"] * 2]
-        accs = {}
+        planes = [sb("h%d" % t, [P, S], F32) for t in range(PACK)]
 
-        def open_plane(t):
-            accs[t] = [psum.tile([P, count], F32, name="acc", tag=tags[t][a]) for a, (first, count) in enumerate(spans[t])]
-            for a, (first, count) in enumerate(spans[t]):
-                if (t, a) != (1, 1):
-                    first_pass(accs[t][a][:], t, first, count)
+        def open_span(t, first, count, tag):
+            acc = psum.tile([P, count], F32, name="acc", tag=tag)
+            first_pass(acc[:], t, first, count)
+            return acc
 
-        def close_plane(t):
-            plane = sb("h%d" % t, [P, S], F32)
-            for a, (first, count) in enumerate(spans[t]):
-                if (t, a) == (1, 1):
-                    first_pass(accs[t][a][:], t, first, count)
-                second_pass(accs[t][a][:], t, first, count)
-                nc.scalar.activation(plane[:, first:first + count], accs[t][a][:], RELU)
-            return plane
+        def close_span(acc, t, first, count):
+            second_pass(acc[:], t, first, count)
+            nc.scalar.activation(planes[t][:, first:first + count], acc[:], RELU)
 
-        open_plane(0)
-        open_plane(1)
-        h = [close_plane(0)]
-        h.append(close_plane(1))
+        def upper_half(t):
+            acc = psum.tile([P, BANK], F32, name="acc", tag="acc")
+            for first, count in ((BANK, EARLY - BANK), (EARLY, S - EARLY)):
+                first_pass(acc[:, first - BANK:first - BANK + count], t, first, count)
+                second_pass(acc[:, first - BANK:first - BANK + count], t, first, count)
+            nc.scalar.activation(planes[t][:, BANK:S], acc[:], RELU)
+
+        accs = [open_span(0, first, count, "acc" if first else "z") for first, count in SPANS]
+        ahead = open_span(1, 0, BANK, "z")
+        for acc, (first, count) in zip(accs, SPANS):
+            close_span(acc, 0, first, count)
+        close_span(ahead, 1, 0, BANK)
+        upper_half(1)
         for t in (2, 3):
-            open_plane(t)
-            h.append(close_plane(t))
+            close_span(open_span(t, 0, BANK, "acc"), t, 0, BANK)
+            upper_half(t)
+        h = planes
 
         w32_woven = sb("w32_woven", [P, 2 * N * PACK], BF16, "w1_1_3_words")
         for i in range(2):

@@ -30,8 +30,8 @@ X_LOADS = [
 ]
 SPANS = [(0, 256), (256, 256), (512, 256), (768, 128), (896, 128)]
 PIECES = [(0, 256), (256, 128), (384, 128)]
-W1_LOADS = [2, 1]
-RUN = 8
+W1_LOADS = [[(0, 384), (384, 128)], [(0, 512)]]
+RUN = 4
 EARLY = 768
 Z_HALF = V // 2
 
@@ -100,11 +100,10 @@ def tile_picked_sagecat_mean_e_kernel(tc, xT, w1, w2, w3, offs, cen, pos1, pos2,
         w1_raw = []
         for g in range(2):
             rows = w1[g * K_PASS:(g + 1) * K_PASS, :].rearrange("(p j) c -> p j c", j=PACK)
-            width = H // W1_LOADS[g]
             parts = []
-            for a in range(W1_LOADS[g]):
+            for a, (c0, width) in enumerate(W1_LOADS[g]):
                 raw = sb("w1_raw%d_%d" % (g, a), [P, PACK, width], F32)
-                nc.sync.dma_start(raw[:], rows[:, :, a * width:(a + 1) * width])
+                nc.sync.dma_start(raw[:], rows[:, :, c0:c0 + width])
                 parts.append(raw)
             w1_raw.append(parts)
         pos_sb = [load_list("pos%d" % (d + 1), src) for d, src in enumerate((pos1, pos2, pos3, pos4))]
@@ -144,11 +143,12 @@ def tile_picked_sagecat_mean_e_kernel(tc, xT, w1, w2, w3, offs, cen, pos1, pos2,
         x_words0 = pick("x_words0", quantize_nodes(0), U32, 0, S)
         all_words1 = quantize_nodes(1)
 
-        def weave_w1(woven, g, a, t, at, copy=nc.scalar.copy):
-            share = K_PASS // W1_LOADS[g]
-            src = w1_raw[g][a][:].rearrange("p j (b t u i) -> p t b u j i", t=PACK, u=2, i=4)
-            dst = woven[:, at * K_PASS + a * share:at * K_PASS + (a + 1) * share]
-            copy(dst.rearrange("p (b u i j) -> p b u j i", u=2, i=4, j=PACK), src[:, t])
+        def weave_w1(woven, g, a, t0, planes, place=0, copy=nc.scalar.copy):
+            c0, width = W1_LOADS[g][a]
+            src = w1_raw[g][a][:].rearrange("p j (b t i) -> p b t j i", t=PACK, i=RUN)
+            dst = woven[:].rearrange("p (t b i j) -> p b t j i", b=P // RUN, i=RUN, j=PACK)
+            blocks = slice(c0 // (PACK * RUN), (c0 + width) // (PACK * RUN))
+            copy(dst[:, blocks, place:place + planes], src[:, :, t0:t0 + planes])
 
         w1_q = {}
 
@@ -161,14 +161,13 @@ def tile_picked_sagecat_mean_e_kernel(tc, xT, w1, w2, w3, offs, cen, pos1, pos2,
         woven_02 = sb("w1_woven0_2", [P, 2 * K_PASS], BF16)
         woven_10 = sb("w1_woven1_0", [P, K_PASS], BF16)
         woven_11 = sb("w1_woven1_1", [P, K_PASS], BF16)
-        for woven, t0 in ((woven_00, 0), (woven_02, 2)):
-            for a in range(2):
-                for t in range(2):
-                    weave_w1(woven, 0, a, t0 + t, t)
+        weave_w1(woven_00, 0, 0, 0, 2)
+        weave_w1(woven_00, 0, 1, 0, 2)
+        weave_w1(woven_02, 0, 1, 2, 2)
+        weave_w1(woven_02, 0, 0, 2, 2)
         woven_12 = sb("w1_woven1_2", [P, K_PASS], BF16)
-        places = [(woven_10, 0), (woven_11, 0), (woven_12, 0)]
-        for t in range(3):
-            weave_w1(places[t][0], 1, 0, t, places[t][1])
+        for t, woven in enumerate((woven_10, woven_11, woven_12)):
+            weave_w1(woven, 1, 0, t, 1)
         x_scales = pick("x_scales", all_scales, U8, 0, S)
         quantize_w1(0, 0, 2, woven_00)
         early = pick("x_words1_early", all_words1, U32, 0, EARLY, "w1_raw0_1")
@@ -177,7 +176,7 @@ def tile_picked_sagecat_mean_e_kernel(tc, xT, w1, w2, w3, offs, cen, pos1, pos2,
         nc.vector.tensor_copy(late[:], all_words1[:].indirect(entries(offs_sb, EARLY, S - EARLY)))
         quantize_w1(1, 1, 1, woven_11)
         woven_13 = at("w1_woven1_3", [P, K_PASS], BF16, 8192 + 2048)
-        weave_w1(woven_13, 1, 0, 3, 0, nc.vector.tensor_copy)
+        weave_w1(woven_13, 1, 0, 3, 1, 0, nc.vector.tensor_copy)
         quantize_w1(0, 2, 2, woven_02, at("w1_0_2_words", [P, 2 * P], U32, 8192))
         quantize_w1(1, 2, 1, woven_12)
         quantize_w1(1, 3, 1, woven_13)

@@ -26,7 +26,7 @@ V_TILES = V // P
 
 X_LOADS = [
     [[(512, 256), (512, 256)], [(512, 256)], [(256, 256), (256, 0)]],
-    [[(512, 0)], [(512, 256)], [(256, 256), (256, 0)], [(128, 128), (128, 0)], [(128, 0)], [(64, 64), (64, 0)]],
+    [[(512, 128), (256, 128)], [(256, 256), (256, 0), (128, 64)], [(128, 128), (128, 0), (128, 64)], [(128, 128), (128, 0)]],
 ]
 SPANS = [(0, 256), (256, 256), (512, 256), (768, 128), (896, 128)]
 PIECES = [(0, 256), (256, 128), (384, 128)]

@@ -284,7 +284,10 @@ def tile_picked_sagecat_mean_e_kernel(tc, xT, w1, w2, w3, offs, cen, pos1, pos2,
                     nc.scalar.copy(res[:, m, :], accs[m][:])
                 else:
                     nc.vector.tensor_copy(res[:, m, :], accs[m][:])
-            nc.sync.dma_start(out[:, v0:v0 + count].rearrange("(m p) v -> p m v", p=P), res[:])
+                if b == last:
+                    nc.sync.dma_start(out[m * P:(m + 1) * P, v0:v0 + count], res[:, m, :])
+            if b < last:
+                nc.sync.dma_start(out[:, v0:v0 + count].rearrange("(m p) v -> p m v", p=P), res[:])
 
         gather_z(0, 0, V)
         gather_z(1, 0, V)

@@ -20,6 +20,7 @@ PACK = 4
 K_PASS = P * PACK
 BANK = 512
 GROUP = 16
+LINE = 4
 SCALE_ROWS = 4
 NEIGHBOURS = 4
 V_TILES = V // P
@@ -28,12 +29,20 @@ X_LOADS = [
     [[(512, 256), (512, 256)], [(512, 256)], [(256, 256), (256, 0)]],
     [[(512, 128), (256, 128)], [(256, 256), (256, 0), (128, 64)], [(128, 128), (128, 0), (128, 64)], [(128, 128), (128, 0)]],
 ]
+W1_LOADS = [[(0, 384), (384, 128)], [(0, 512)]]
+EARLY = 768
 SPANS = [(0, 256), (256, 256), (512, 256), (768, 128), (896, 128)]
 PIECES = [(0, 256), (256, 128), (384, 128)]
-W1_LOADS = [[(0, 384), (384, 128)], [(0, 512)]]
-RUN = 4
-EARLY = 768
 Z_HALF = V // 2
+WOVEN_BUFS = 4
+GOT_BUFS = 14
+
+AT_GOT = {(2, 2): 0, (2, 3): 2048}
+AT_CEN_GOT = [0, 2048, 0]
+AT_Z_PAIRS = 4096
+AT_CEN_WOVEN = [AT_Z_PAIRS + 1984, AT_Z_PAIRS, 2560]
+AT_Z_LAST_WORDS = 2048
+AT_ALL_WORDS = 8192
 
 
 def tile_picked_sagecat_mean_e_kernel(tc, xT, w1, w2, w3, offs, cen, pos1, pos2, pos3, pos4, out):
@@ -41,11 +50,11 @@ def tile_picked_sagecat_mean_e_kernel(tc, xT, w1, w2, w3, offs, cen, pos1, pos2,
     with ExitStack() as ctx:
         keep = ctx.enter_context(tc.tile_pool(name="keep", bufs=1))
         placed = ctx.enter_context(tc.tile_pool(name="placed", bufs=1))
-        ring = ctx.enter_context(tc.tile_pool(name="ring", bufs=4))
+        ring = ctx.enter_context(tc.tile_pool(name="ring", bufs=WOVEN_BUFS))
         psum = ctx.enter_context(tc.psum_pool(name="psum", bufs=4))
 
-        def sb(name, shape, dtype, slot=None):
-            return keep.tile(shape, dtype, name=name, tag=(slot or name), align_bytes=64)
+        def sb(name, shape, dtype, bytes_of=None):
+            return keep.tile(shape, dtype, name=name, tag=(bytes_of or name), align_bytes=64)
 
         def at(name, shape, dtype, offset):
             return placed.tile(shape, dtype, name=name, offset=offset, align_bytes=64)
@@ -58,18 +67,21 @@ def tile_picked_sagecat_mean_e_kernel(tc, xT, w1, w2, w3, offs, cen, pos1, pos2,
         def entries(tile, first, count):
             return tile[:, first // GROUP:(first + count) // GROUP]
 
+        def line_wise(dst, src):
+            return dst.rearrange("p (c i t) -> p c t i", i=LINE, t=PACK), src.rearrange("p t (c i) -> p c t i", i=LINE)
+
         def weave(eng, dst, src):
-            dst = dst.rearrange("p (c i t) -> p c t i", i=4, t=PACK)
-            src = src.rearrange("p t (c i) -> p c t i", i=4)
+            dst, src = line_wise(dst, src)
             if eng is nc.vector:
                 nc.vector.tensor_copy(dst, src)
             else:
                 nc.scalar.activation(dst, src, COPY)
 
-        def quantize(name, src, slot=None, scale_slot=None):
+        def quantize(name, src, words=None):
             width = src.shape[1] // PACK
-            words = sb(name + "_words", [P, width], U32) if slot is None else slot
-            scales = sb(name + "_scales", [P, width], U8, scale_slot)
+            if words is None:
+                words = sb(name + "_words", [P, width], U32)
+            scales = sb(name + "_scales", [P, width], U8)
             nc.vector.quantize_mx(out=words[:].bitcast(FP8X4), scales=scales[:], in_=src)
             return words, scales
 
@@ -101,8 +113,8 @@ def tile_picked_sagecat_mean_e_kernel(tc, xT, w1, w2, w3, offs, cen, pos1, pos2,
         for g in range(2):
             rows = w1[g * K_PASS:(g + 1) * K_PASS, :].rearrange("(p j) c -> p j c", j=PACK)
             parts = []
-            for a, (c0, width) in enumerate(W1_LOADS[g]):
-                raw = sb("w1_raw%d_%d" % (g, a), [P, PACK, width], F32)
+            for part, (c0, width) in enumerate(W1_LOADS[g]):
+                raw = sb("w1_raw%d_%d" % (g, part), [P, PACK, width], F32)
                 nc.sync.dma_start(raw[:], rows[:, :, c0:c0 + width])
                 parts.append(raw)
             w1_raw.append(parts)
@@ -111,7 +123,7 @@ def tile_picked_sagecat_mean_e_kernel(tc, xT, w1, w2, w3, offs, cen, pos1, pos2,
         w32_raw = []
         for name, src in (("w3_raw", w3), ("w2_raw", w2)):
             raw = sb(name, [P, PACK, N], F32)
-            dealt = src.rearrange("(b t r) c -> t b r c", t=PACK, r=RUN)
+            dealt = src.rearrange("(b t r) c -> t b r c", t=PACK, r=LINE)
             for t in range(PACK):
                 nc.sync.dma_start(raw[:, t, :], dealt[t])
             w32_raw.append(raw)
@@ -119,8 +131,7 @@ def tile_picked_sagecat_mean_e_kernel(tc, xT, w1, w2, w3, offs, cen, pos1, pos2,
         all_scales = sb("all_scales", [P, T], U8)
         nc.gpsimd.memset(all_scales[:].bitcast(U32), 0)
 
-        def quantize_nodes(g):
-            words = at("all_words1", [P, T], U32, 8192) if g else sb("all_words0", [P, T], U32)
+        def quantize_nodes(g, words):
             for c0, width, on_vector, raw in x_runs[g]:
                 if width == BANK:
                     woven = ring.tile([P, width * PACK], BF16, name="x_woven", tag="x_woven", align_bytes=64)
@@ -135,26 +146,26 @@ def tile_picked_sagecat_mean_e_kernel(tc, xT, w1, w2, w3, offs, cen, pos1, pos2,
                                       scales=all_scales[SCALE_ROWS * (1 - g):P, c0:c0 + width], in_=woven[:])
             return words
 
-        def pick(name, src, dtype, first, count, slot=None):
-            tile = sb(name, [P, count], dtype, slot)
+        def pick(name, src, dtype, first, count, bytes_of=None):
+            tile = sb(name, [P, count], dtype, bytes_of)
             nc.vector.tensor_copy(tile[:], src[:].indirect(entries(offs_sb, first, count)))
             return tile
 
-        x_words0 = pick("x_words0", quantize_nodes(0), U32, 0, S)
-        all_words1 = quantize_nodes(1)
+        x_words0 = pick("x_words0", quantize_nodes(0, sb("all_words0", [P, T], U32)), U32, 0, S)
+        all_words1 = quantize_nodes(1, at("all_words1", [P, T], U32, AT_ALL_WORDS))
 
-        def weave_w1(woven, g, a, t0, planes, place=0, copy=nc.scalar.copy):
-            c0, width = W1_LOADS[g][a]
-            src = w1_raw[g][a][:].rearrange("p j (b t i) -> p b t j i", t=PACK, i=RUN)
-            dst = woven[:].rearrange("p (t b i j) -> p b t j i", b=P // RUN, i=RUN, j=PACK)
-            blocks = slice(c0 // (PACK * RUN), (c0 + width) // (PACK * RUN))
-            copy(dst[:, blocks, place:place + planes], src[:, :, t0:t0 + planes])
+        def weave_w1(woven, g, part, t0, count, copy=nc.scalar.copy):
+            c0, width = W1_LOADS[g][part]
+            src = w1_raw[g][part][:].rearrange("p j (b t i) -> p b t j i", t=PACK, i=LINE)
+            dst = woven[:].rearrange("p (t b i j) -> p b t j i", b=P // LINE, i=LINE, j=PACK)
+            blocks = slice(c0 // (PACK * LINE), (c0 + width) // (PACK * LINE))
+            copy(dst[:, blocks, 0:count], src[:, :, t0:t0 + count])
 
         w1_q = {}
 
-        def quantize_w1(g, t0, planes, woven, slot=None):
-            weights = quantize("w1_%d_%d" % (g, t0), woven[:], slot)
-            for t in range(planes):
+        def quantize_w1(g, t0, count, woven, words=None):
+            weights = quantize("w1_%d_%d" % (g, t0), woven[:], words)
+            for t in range(count):
                 w1_q[g, t0 + t] = (weights, slice(t * P, (t + 1) * P))
 
         woven_00 = sb("w1_woven0_0", [P, 2 * K_PASS], BF16)
@@ -172,12 +183,11 @@ def tile_picked_sagecat_mean_e_kernel(tc, xT, w1, w2, w3, offs, cen, pos1, pos2,
         quantize_w1(0, 0, 2, woven_00)
         early = pick("x_words1_early", all_words1, U32, 0, EARLY, "w1_raw0_1")
         quantize_w1(1, 0, 1, woven_10)
-        late = sb("x_words1_late", [P, S - EARLY], U32, "w1_woven1_0")
-        nc.vector.tensor_copy(late[:], all_words1[:].indirect(entries(offs_sb, EARLY, S - EARLY)))
+        late = pick("x_words1_late", all_words1, U32, EARLY, S - EARLY, "w1_woven1_0")
         quantize_w1(1, 1, 1, woven_11)
-        woven_13 = at("w1_woven1_3", [P, K_PASS], BF16, 8192 + 2048)
-        weave_w1(woven_13, 1, 0, 3, 1, 0, nc.vector.tensor_copy)
-        quantize_w1(0, 2, 2, woven_02, at("w1_0_2_words", [P, 2 * P], U32, 8192))
+        woven_13 = at("w1_woven1_3", [P, K_PASS], BF16, AT_ALL_WORDS + 2048)
+        weave_w1(woven_13, 1, 0, 3, 1, nc.vector.tensor_copy)
+        quantize_w1(0, 2, 2, woven_02, at("w1_0_2_words", [P, 2 * P], U32, AT_ALL_WORDS))
         quantize_w1(1, 2, 1, woven_12)
         quantize_w1(1, 3, 1, woven_13)
 
@@ -188,7 +198,7 @@ def tile_picked_sagecat_mean_e_kernel(tc, xT, w1, w2, w3, offs, cen, pos1, pos2,
             words = early[:, first:first + count] if first < EARLY else late[:, first - EARLY:first - EARLY + count]
             mx(acc, w1_q[1, t][0], w1_q[1, t][1], words, x_scales[:, first:first + count], False, True)
 
-        planes = [sb("h%d" % t, [P, S], F32) for t in range(PACK)]
+        h = [sb("h%d" % t, [P, S], F32) for t in range(PACK)]
 
         def open_span(t, first, count, tag):
             acc = psum.tile([P, count], F32, name="acc", tag=tag)
@@ -197,47 +207,41 @@ def tile_picked_sagecat_mean_e_kernel(tc, xT, w1, w2, w3, offs, cen, pos1, pos2,
 
         def close_span(acc, t, first, count):
             second_pass(acc[:], t, first, count)
-            nc.scalar.activation(planes[t][:, first:first + count], acc[:], RELU)
+            nc.scalar.activation(h[t][:, first:first + count], acc[:], RELU)
 
         def upper_half(t):
             acc = psum.tile([P, BANK], F32, name="acc", tag="acc")
             for first, count in ((BANK, EARLY - BANK), (EARLY, S - EARLY)):
                 first_pass(acc[:, first - BANK:first - BANK + count], t, first, count)
                 second_pass(acc[:, first - BANK:first - BANK + count], t, first, count)
-            nc.scalar.activation(planes[t][:, BANK:S], acc[:], RELU)
+            nc.scalar.activation(h[t][:, BANK:S], acc[:], RELU)
 
-        accs = [open_span(0, first, count, "acc" if first else "z") for first, count in SPANS]
-        ahead = open_span(1, 0, BANK, "z")
-        for acc, (first, count) in zip(accs, SPANS):
+        h0_accs = [open_span(0, first, count, "acc" if first else "z") for first, count in SPANS]
+        h1_acc = open_span(1, 0, BANK, "z")
+        for acc, (first, count) in zip(h0_accs, SPANS):
             close_span(acc, 0, first, count)
-        close_span(ahead, 1, 0, BANK)
+        close_span(h1_acc, 1, 0, BANK)
         upper_half(1)
         for t in (2, 3):
             close_span(open_span(t, 0, BANK, "acc"), t, 0, BANK)
             upper_half(t)
-        h = planes
 
         w32_woven = sb("w32_woven", [P, 2 * N * PACK], BF16, "w1_1_3_words")
         for i in range(2):
             weave(nc.scalar, w32_woven[:, i * N * PACK:(i + 1) * N * PACK], w32_raw[i][:])
 
         z_sum = [psum.tile([P, PACK, P], F32, name="z_sum", tag="z") for vt in range(V_TILES)]
+        z_pairs = [sb("z_pairs0", [P, 8 * P], BF16), at("z_pairs1", [P, 8 * P], BF16, AT_Z_PAIRS)]
 
-        z_pairs = [sb("z_pairs0", [P, 8 * P], BF16), at("z_pairs1", [P, 8 * P], BF16, 4096)]
-
-        lent = {(2, 2): 0, (2, 3): 2048}
-
-        def gather_z(t, v0, count, into=None):
+        def gather_z(t):
             for d in range(NEIGHBOURS):
-                if (t, d) in lent:
-                    got = at("got", [P, count], F32, lent[t, d])[:]
-                elif into is None:
-                    got = ring.tile([P, count], F32, name="got", tag="got", bufs=14)[:]
+                if (t, d) in AT_GOT:
+                    got = at("got", [P, V], F32, AT_GOT[t, d])
                 else:
-                    got = into[:, d, :]
-                nc.vector.tensor_copy(got, h[t][:].indirect(entries(pos_sb[d], v0, count)))
-                for a in range(count // P):
-                    nc.tensor.matmul(z_sum[v0 // P + a][:, t, :], got[:, a * P:(a + 1) * P], ident[:],
+                    got = ring.tile([P, V], F32, name="got", tag="got", bufs=GOT_BUFS)
+                nc.vector.tensor_copy(got[:], h[t][:].indirect(pos_sb[d][:]))
+                for vt in range(V_TILES):
+                    nc.tensor.matmul(z_sum[vt][:, t, :], got[:, vt * P:(vt + 1) * P], ident[:],
                                      start=(d == 0), stop=(d == NEIGHBOURS - 1), is_transpose=True)
 
         def turn_back(u, vt):
@@ -253,26 +257,27 @@ def tile_picked_sagecat_mean_e_kernel(tc, xT, w1, w2, w3, offs, cen, pos1, pos2,
 
         last = len(PIECES) - 1
 
-        def gather_cen(name, v0, count, offset):
-            got = at(name, [P, PACK, count], BF16, offset)
+        def gather_cen(b):
+            v0, count = PIECES[b]
+            got = at("cen_got%d" % b, [P, PACK, count], BF16, AT_CEN_GOT[b])
             for t in range(PACK):
                 nc.vector.tensor_copy(got[:, t, :], h[t][:].indirect(entries(cen_sb, v0, count)))
             return got
 
-        def weave_cen(b, got, woven):
+        def weave_cen(b, got):
+            woven = at("cen_woven%d" % b, [P, PIECES[b][1] * PACK], BF16, AT_CEN_WOVEN[b])
+            dst, src = line_wise(woven[:], got[:])
             if b < last:
-                nc.scalar.copy(woven[:].rearrange("p (c i t) -> p c t i", i=4, t=PACK), got.rearrange("p t (c i) -> p c t i", i=4))
+                nc.scalar.copy(dst, src)
             else:
-                weave(nc.vector, woven[:], got)
+                nc.vector.tensor_copy(dst, src)
             return woven
 
         def open_out(b, z_q):
-            v0, count = PIECES[b]
-            words, scales = z_q
-            cols = slice(0, count)
+            count = PIECES[b][1]
             accs = [psum.tile([P, count], F32, name="out_acc", tag=("z" if b < last else "acc")) for m in range(N // P)]
             for m in range(N // P):
-                mx(accs[m][:], w32, slice(m * P, (m + 1) * P), words[:, cols], scales[:, cols], True, False)
+                mx(accs[m][:], w32, slice(m * P, (m + 1) * P), z_q[0][:], z_q[1][:], True, False)
             return accs
 
         def close_out(b, accs, cen_q):
@@ -284,32 +289,29 @@ def tile_picked_sagecat_mean_e_kernel(tc, xT, w1, w2, w3, offs, cen, pos1, pos2,
                     nc.scalar.copy(res[:, m, :], accs[m][:])
                 else:
                     nc.vector.tensor_copy(res[:, m, :], accs[m][:])
-                if b == last:
-                    nc.sync.dma_start(out[m * P:(m + 1) * P, v0:v0 + count], res[:, m, :])
-            if b < last:
-                nc.sync.dma_start(out[:, v0:v0 + count].rearrange("(m p) v -> p m v", p=P), res[:])
+                nc.sync.dma_start(out[m * P:(m + 1) * P, v0:v0 + count], res[:, m, :])
 
-        gather_z(0, 0, V)
-        gather_z(1, 0, V)
+        gather_z(0)
+        gather_z(1)
         z_back = [psum.tile([P, 2, Z_HALF], F32, name="z_back", tag="acc") for half in range(2)]
         for vt in range(V_TILES):
             turn_back(0, vt)
-        gather_z(2, 0, V)
+        gather_z(2)
         w32 = quantize("w32", w32_woven[:])
-        gather_z(3, 0, V)
+        gather_z(3)
         for vt in range(V_TILES):
             turn_back(1, vt)
-        got0 = gather_cen("cen_got0", 0, 256, 0)
-        got1 = gather_cen("cen_got1", 256, 128, 2048)
+        cen_got0 = gather_cen(0)
+        cen_got1 = gather_cen(1)
         z_woven0 = weave_z(0)
-        cen_woven0 = weave_cen(0, got0[:], at("cen_woven0", [P, 256 * PACK], BF16, 6080))
+        cen_woven0 = weave_cen(0, cen_got0)
         z_woven1 = weave_z(1)
-        cen_woven1 = weave_cen(1, got1[:], at("cen_woven1", [P, P * PACK], BF16, 4096))
+        cen_woven1 = weave_cen(1, cen_got1)
         out0 = open_out(0, quantize("z0", z_woven0[:]))
         close_out(0, out0, quantize("cen0", cen_woven0[:]))
-        got2 = gather_cen("cen_got2", 384, 128, 0)
+        cen_got2 = gather_cen(2)
         out1 = open_out(1, quantize("z1", z_woven1[:, 0:P * PACK]))
         close_out(1, out1, quantize("cen1", cen_woven1[:]))
-        cen_woven2 = weave_cen(2, got2[:], at("cen_woven2", [P, P * PACK], BF16, 2560))
-        out2 = open_out(2, quantize("z2", z_woven1[:, P * PACK:2 * P * PACK], at("z2_words", [P, P], U32, 2048)))
+        cen_woven2 = weave_cen(2, cen_got2)
+        out2 = open_out(2, quantize("z2", z_woven1[:, P * PACK:2 * P * PACK], at("z2_words", [P, P], U32, AT_Z_LAST_WORDS)))
         close_out(2, out2, quantize("cen2", cen_woven2[:]))

@@ -21,20 +21,13 @@ K_PASS = P * PACK
 BANK = 512
 GROUP = 16
 LINE = 4
-SCALE_ROWS = 4
 NEIGHBOURS = 4
 V_TILES = V // P
 
-X_LOADS = [
-    [[(512, 256), (512, 256)], [(512, 256)], [(256, 256), (256, 0)]],
-    [[(512, 128), (256, 128)], [(256, 256), (256, 0), (128, 64)], [(128, 128), (128, 0), (128, 64)], [(128, 128), (128, 0)]],
-]
-W1_LOADS = [[(0, 384), (384, 128)], [(0, 512)]]
-EARLY = 768
-SPANS = [(0, 256), (256, 256), (512, 256), (768, 128), (896, 128)]
+SLICE = 256
+SLICES = S // SLICE
 PIECES = [(0, 256), (256, 128), (384, 128)]
 Z_HALF = V // 2
-WOVEN_BUFS = 4
 GOT_BUFS = 14
 
 AT_GOT = {(2, 2): 0, (2, 3): 2048}
@@ -42,7 +35,10 @@ AT_CEN_GOT = [0, 2048, 0]
 AT_Z_PAIRS = 4096
 AT_CEN_WOVEN = [AT_Z_PAIRS + 1984, AT_Z_PAIRS, 2560]
 AT_Z_LAST_WORDS = 2048
-AT_ALL_WORDS = 8192
+AT_ROW = 8192
+AT_W1_10 = 18432
+AT_W1_02 = AT_W1_10 - 2048 + 64
+AT_W1_10_WORDS = 20480
 
 
 def tile_picked_sagecat_mean_e_kernel(tc, xT, w1, w2, w3, offs, cen, pos1, pos2, pos3, pos4, out):
@@ -50,14 +46,17 @@ def tile_picked_sagecat_mean_e_kernel(tc, xT, w1, w2, w3, offs, cen, pos1, pos2,
     with ExitStack() as ctx:
         keep = ctx.enter_context(tc.tile_pool(name="keep", bufs=1))
         placed = ctx.enter_context(tc.tile_pool(name="placed", bufs=1))
-        ring = ctx.enter_context(tc.tile_pool(name="ring", bufs=WOVEN_BUFS))
-        psum = ctx.enter_context(tc.psum_pool(name="psum", bufs=4))
+        ring = ctx.enter_context(tc.tile_pool(name="ring", bufs=GOT_BUFS))
+        psum = ctx.enter_context(tc.psum_pool(name="psum", bufs=1))
 
         def sb(name, shape, dtype, bytes_of=None):
             return keep.tile(shape, dtype, name=name, tag=(bytes_of or name), align_bytes=64)
 
         def at(name, shape, dtype, offset):
             return placed.tile(shape, dtype, name=name, offset=offset, align_bytes=64)
+
+        def bank(name, shape, index):
+            return psum.tile(shape, F32, name=name, offset=index * BANK * 4)
 
         def load_list(name, src):
             tile = sb(name, list(src.shape), U16)
@@ -92,32 +91,21 @@ def tile_picked_sagecat_mean_e_kernel(tc, xT, w1, w2, w3, offs, cen, pos1, pos2,
         ident = sb("ident", [P, P], F32)
         make_identity(nc, ident[:])
 
-        x_runs = []
+        offs_sb = load_list("offs", offs)
+        x_raw = {}
         for g in range(2):
-            rows = xT[g * K_PASS:(g + 1) * K_PASS, :].rearrange("(p j) t -> p j t", j=PACK)
-            runs = []
-            c0 = 0
-            for load in X_LOADS[g]:
-                total = sum(width for width, on_vector in load)
-                raw = sb("x_raw%d_%d" % (g, c0), [P, PACK, total], F32)
-                nc.sync.dma_start(raw[:], rows[:, :, c0:c0 + total])
-                first = 0
-                for width, on_vector in load:
-                    runs.append((c0 + first, width, on_vector, raw[:, :, first:first + width]))
-                    first = first + width
-                c0 = c0 + total
-            x_runs.append(runs)
-            if g == 0:
-                offs_sb = load_list("offs", offs)
+            rows = xT[g * K_PASS:(g + 1) * K_PASS, :].rearrange("(p j) t -> j p t", j=PACK)
+            for j in range(PACK):
+                if (g, j) == (1, 0):
+                    x_raw[g, j] = at("x_raw10", [P, T], F32, AT_ROW)
+                else:
+                    x_raw[g, j] = sb("x_raw%d%d" % (g, j), [P, T], F32)
+                nc.sync.dma_start(x_raw[g, j][:], rows[j])
         w1_raw = []
         for g in range(2):
-            rows = w1[g * K_PASS:(g + 1) * K_PASS, :].rearrange("(p j) c -> p j c", j=PACK)
-            parts = []
-            for part, (c0, width) in enumerate(W1_LOADS[g]):
-                raw = sb("w1_raw%d_%d" % (g, part), [P, PACK, width], F32)
-                nc.sync.dma_start(raw[:], rows[:, :, c0:c0 + width])
-                parts.append(raw)
-            w1_raw.append(parts)
+            raw = sb("w1_raw%d" % g, [P, PACK, H], F32)
+            nc.sync.dma_start(raw[:], w1[g * K_PASS:(g + 1) * K_PASS, :].rearrange("(p j) c -> p j c", j=PACK))
+            w1_raw.append(raw)
         pos_sb = [load_list("pos%d" % (d + 1), src) for d, src in enumerate((pos1, pos2, pos3, pos4))]
         cen_sb = load_list("cen", cen)
         w32_raw = []
@@ -128,38 +116,71 @@ def tile_picked_sagecat_mean_e_kernel(tc, xT, w1, w2, w3, offs, cen, pos1, pos2,
                 nc.sync.dma_start(raw[:, t, :], dealt[t])
             w32_raw.append(raw)
 
-        all_scales = sb("all_scales", [P, T], U8)
-        nc.gpsimd.memset(all_scales[:].bitcast(U32), 0)
+        picked = [sb("picked%d" % g, [P, PACK, S], BF16) for g in range(2)]
+        x_words = [sb("x_words%d" % g, [P, S], U32) for g in range(2)]
+        x_scales = [sb("x_scales%d" % g, [P, S], U8) for g in range(2)]
 
-        def quantize_nodes(g, words):
-            for c0, width, on_vector, raw in x_runs[g]:
-                if width == BANK:
-                    woven = ring.tile([P, width * PACK], BF16, name="x_woven", tag="x_woven", align_bytes=64)
-                else:
-                    woven = sb("x_woven%d_%d" % (g, c0), [P, width * PACK], BF16)
-                on_scalar = width - on_vector
-                if on_scalar:
-                    weave(nc.scalar, woven[:, 0:on_scalar * PACK], raw[:, :, 0:on_scalar])
-                if on_vector:
-                    weave(nc.vector, woven[:, on_scalar * PACK:width * PACK], raw[:, :, on_scalar:width])
-                nc.vector.quantize_mx(out=words[:, c0:c0 + width].bitcast(FP8X4),
-                                      scales=all_scales[SCALE_ROWS * (1 - g):P, c0:c0 + width], in_=woven[:])
-            return words
+        def pick(g, j, first, count):
+            nc.vector.tensor_copy(picked[g][:, j, first:first + count], x_raw[g, j][:].indirect(entries(offs_sb, first, count)))
 
-        def pick(name, src, dtype, first, count, bytes_of=None):
-            tile = sb(name, [P, count], dtype, bytes_of)
-            nc.vector.tensor_copy(tile[:], src[:].indirect(entries(offs_sb, first, count)))
-            return tile
+        def cast_row(eng, g, j):
+            row = sb("x_cast%d%d" % (g, j), [P, T], BF16)
+            if eng is nc.vector:
+                nc.vector.tensor_copy(row[:], x_raw[g, j][:])
+            else:
+                nc.scalar.activation(row[:], x_raw[g, j][:], COPY)
+            return row
 
-        x_words0 = pick("x_words0", quantize_nodes(0, sb("all_words0", [P, T], U32)), U32, 0, S)
-        all_words1 = quantize_nodes(1, at("all_words1", [P, T], U32, AT_ALL_WORDS))
+        def pick_on_scalar(g, j, row):
+            nc.scalar.activation(picked[g][:, j, :], row[:].indirect(offs_sb[:]), COPY)
 
-        def weave_w1(woven, g, part, t0, count, copy=nc.scalar.copy):
-            c0, width = W1_LOADS[g][part]
-            src = w1_raw[g][part][:].rearrange("p j (b t i) -> p b t j i", t=PACK, i=LINE)
+        def weave_x(eng, g, s, woven, at_slice=0):
+            dst, src = line_wise(woven[:, at_slice * SLICE * PACK:(at_slice + 1) * SLICE * PACK], picked[g][:, :, s * SLICE:(s + 1) * SLICE])
+            if eng is nc.vector:
+                nc.vector.tensor_copy(dst, src)
+            else:
+                nc.scalar.copy(dst, src)
+
+        def woven_tile(g, s, count):
+            return sb("x_woven%d%d" % (g, s), [P, count * SLICE * PACK], BF16)
+
+        def quantize_x(g, s, woven):
+            cols = slice(s * SLICE, s * SLICE + woven.shape[1] // PACK)
+            nc.vector.quantize_mx(out=x_words[g][:, cols].bitcast(FP8X4), scales=x_scales[g][:, cols], in_=woven[:])
+
+        pick(0, 0, 0, S)
+        pick_on_scalar(0, 1, cast_row(nc.scalar, 0, 1))
+        pick(0, 2, 0, S)
+        pick(0, 3, 0, SLICE)
+        pick(0, 3, SLICE, SLICE)
+        pick(0, 3, 2 * SLICE, 2 * SLICE)
+        low0, third0 = woven_tile(0, 0, 2), woven_tile(0, 2, 1)
+        weave_x(nc.scalar, 0, 0, low0, 0)
+        weave_x(nc.scalar, 0, 1, low0, 1)
+        weave_x(nc.scalar, 0, 2, third0)
+        row0 = cast_row(nc.vector, 1, 0)
+        last0 = at("x_woven03", [P, SLICE * PACK], BF16, AT_ROW)
+        weave_x(nc.vector, 0, 3, last0)
+        quantize_x(0, 0, low0)
+        quantize_x(0, 3, last0)
+        quantize_x(0, 2, third0)
+        pick_on_scalar(1, 0, row0)
+        row1 = cast_row(nc.vector, 1, 1)
+        pick_on_scalar(1, 1, row1)
+        pick(1, 2, 0, S)
+        for s in range(SLICES):
+            pick(1, 3, s * SLICE, SLICE)
+        low1, third1, last1 = woven_tile(1, 0, 2), woven_tile(1, 2, 1), woven_tile(1, 3, 1)
+        weave_x(nc.scalar, 1, 0, low1, 0)
+        weave_x(nc.scalar, 1, 1, low1, 1)
+        weave_x(nc.scalar, 1, 2, third1)
+        weave_x(nc.vector, 1, 3, last1)
+
+        def weave_w1(woven, g, t0, count, copy=nc.scalar.copy):
+            src = w1_raw[g][:].rearrange("p j (b t i) -> p b t j i", t=PACK, i=LINE)
             dst = woven[:].rearrange("p (t b i j) -> p b t j i", b=P // LINE, i=LINE, j=PACK)
-            blocks = slice(c0 // (PACK * LINE), (c0 + width) // (PACK * LINE))
-            copy(dst[:, blocks, 0:count], src[:, :, t0:t0 + count])
+            copy(dst[:, :, 0:count], src[:, :, t0:t0 + count])
+            return woven
 
         w1_q = {}
 
@@ -168,69 +189,49 @@ def tile_picked_sagecat_mean_e_kernel(tc, xT, w1, w2, w3, offs, cen, pos1, pos2,
             for t in range(count):
                 w1_q[g, t0 + t] = (weights, slice(t * P, (t + 1) * P))
 
-        woven_00 = sb("w1_woven0_0", [P, 2 * K_PASS], BF16)
-        woven_02 = sb("w1_woven0_2", [P, 2 * K_PASS], BF16)
-        woven_10 = sb("w1_woven1_0", [P, K_PASS], BF16)
-        woven_11 = sb("w1_woven1_1", [P, K_PASS], BF16)
-        weave_w1(woven_00, 0, 0, 0, 2)
-        weave_w1(woven_00, 0, 1, 0, 2)
-        weave_w1(woven_02, 0, 1, 2, 2)
-        weave_w1(woven_02, 0, 0, 2, 2)
-        woven_12 = sb("w1_woven1_2", [P, K_PASS], BF16)
-        for t, woven in enumerate((woven_10, woven_11, woven_12)):
-            weave_w1(woven, 1, 0, t, 1)
-        x_scales = pick("x_scales", all_scales, U8, 0, S)
-        quantize_w1(0, 0, 2, woven_00)
-        early = pick("x_words1_early", all_words1, U32, 0, EARLY, "w1_raw0_1")
-        quantize_w1(1, 0, 1, woven_10)
-        late = pick("x_words1_late", all_words1, U32, EARLY, S - EARLY, "w1_woven1_0")
+        woven_00 = weave_w1(sb("w1_woven0_0", [P, K_PASS], BF16), 0, 0, 1, nc.vector.tensor_copy)
+        quantize_x(1, 0, low1)
+        quantize_w1(0, 0, 1, woven_00)
+        quantize_x(1, 3, last1)
+        quantize_x(1, 2, third1)
+        quantize_w1(1, 0, 1, weave_w1(at("w1_woven1_0", [P, K_PASS], BF16, AT_W1_10), 1, 0, 1),
+                    at("w1_1_0_words", [P, P], U32, AT_W1_10_WORDS))
+        woven_12 = weave_w1(sb("w1_woven1_2", [P, 2 * K_PASS], BF16), 1, 2, 2)
+        woven_01 = weave_w1(at("w1_woven0_1", [P, K_PASS], BF16, AT_W1_10 - 960), 0, 1, 1, nc.vector.tensor_copy)
+        woven_11 = weave_w1(at("w1_woven1_1", [P, K_PASS], BF16, AT_W1_10 + 960), 1, 1, 1, nc.vector.tensor_copy)
+        quantize_w1(0, 1, 1, woven_01)
         quantize_w1(1, 1, 1, woven_11)
-        woven_13 = at("w1_woven1_3", [P, K_PASS], BF16, AT_ALL_WORDS + 2048)
-        weave_w1(woven_13, 1, 0, 3, 1, nc.vector.tensor_copy)
-        quantize_w1(0, 2, 2, woven_02, at("w1_0_2_words", [P, 2 * P], U32, AT_ALL_WORDS))
-        quantize_w1(1, 2, 1, woven_12)
-        quantize_w1(1, 3, 1, woven_13)
-
-        def first_pass(acc, t, first, count):
-            mx(acc, w1_q[0, t][0], w1_q[0, t][1], x_words0[:, first:first + count], x_scales[SCALE_ROWS:P, first:first + count], True, False)
-
-        def second_pass(acc, t, first, count):
-            words = early[:, first:first + count] if first < EARLY else late[:, first - EARLY:first - EARLY + count]
-            mx(acc, w1_q[1, t][0], w1_q[1, t][1], words, x_scales[:, first:first + count], False, True)
+        quantize_w1(1, 2, 2, woven_12)
 
         h = [sb("h%d" % t, [P, S], F32) for t in range(PACK)]
 
-        def open_span(t, first, count, tag):
-            acc = psum.tile([P, count], F32, name="acc", tag=tag)
-            first_pass(acc[:], t, first, count)
+        def one_pass(acc, g, t, first, count):
+            mx(acc[:], w1_q[g, t][0], w1_q[g, t][1], x_words[g][:, first:first + count], x_scales[g][:, first:first + count], g == 0, g == 1)
+
+        def open_span(t, first, count, index):
+            acc = bank("acc%d_%d" % (t, first), [P, count], index)
+            one_pass(acc, 0, t, first, count)
             return acc
 
         def close_span(acc, t, first, count):
-            second_pass(acc[:], t, first, count)
+            one_pass(acc, 1, t, first, count)
             nc.scalar.activation(h[t][:, first:first + count], acc[:], RELU)
 
-        def upper_half(t):
-            acc = psum.tile([P, BANK], F32, name="acc", tag="acc")
-            for first, count in ((BANK, EARLY - BANK), (EARLY, S - EARLY)):
-                first_pass(acc[:, first - BANK:first - BANK + count], t, first, count)
-                second_pass(acc[:, first - BANK:first - BANK + count], t, first, count)
-            nc.scalar.activation(h[t][:, BANK:S], acc[:], RELU)
-
-        h0_accs = [open_span(0, first, count, "acc" if first else "z") for first, count in SPANS]
-        h1_acc = open_span(1, 0, BANK, "z")
-        for acc, (first, count) in zip(h0_accs, SPANS):
-            close_span(acc, 0, first, count)
-        close_span(h1_acc, 1, 0, BANK)
-        upper_half(1)
+        h0_accs = [open_span(0, s * SLICE, SLICE, s) for s in range(SLICES)]
+        for s in range(SLICES):
+            close_span(h0_accs[s], 0, s * SLICE, SLICE)
+        quantize_w1(0, 2, 2, weave_w1(at("w1_woven0_2", [P, 2 * K_PASS], BF16, AT_W1_10_WORDS), 0, 2, 2))
+        for half in range(2):
+            close_span(open_span(1, half * BANK, BANK, 4 + half), 1, half * BANK, BANK)
         for t in (2, 3):
-            close_span(open_span(t, 0, BANK, "acc"), t, 0, BANK)
-            upper_half(t)
+            for half in range(2):
+                close_span(open_span(t, half * BANK, BANK, 10 - 2 * t + half), t, half * BANK, BANK)
 
-        w32_woven = sb("w32_woven", [P, 2 * N * PACK], BF16, "w1_1_3_words")
+        w32_woven = sb("w32_woven", [P, 2 * N * PACK], BF16, "w1_1_2_words")
         for i in range(2):
             weave(nc.scalar, w32_woven[:, i * N * PACK:(i + 1) * N * PACK], w32_raw[i][:])
 
-        z_sum = [psum.tile([P, PACK, P], F32, name="z_sum", tag="z") for vt in range(V_TILES)]
+        z_sum = [bank("z_sum%d" % vt, [P, PACK, P], 4 + vt) for vt in range(V_TILES)]
         z_pairs = [sb("z_pairs0", [P, 8 * P], BF16), at("z_pairs1", [P, 8 * P], BF16, AT_Z_PAIRS)]
 
         def gather_z(t):
@@ -238,7 +239,7 @@ def tile_picked_sagecat_mean_e_kernel(tc, xT, w1, w2, w3, offs, cen, pos1, pos2,
                 if (t, d) in AT_GOT:
                     got = at("got", [P, V], F32, AT_GOT[t, d])
                 else:
-                    got = ring.tile([P, V], F32, name="got", tag="got", bufs=GOT_BUFS)
+                    got = ring.tile([P, V], F32, name="got", tag="got")
                 nc.vector.tensor_copy(got[:], h[t][:].indirect(pos_sb[d][:]))
                 for vt in range(V_TILES):
                     nc.tensor.matmul(z_sum[vt][:, t, :], got[:, vt * P:(vt + 1) * P], ident[:],
@@ -275,7 +276,7 @@ def tile_picked_sagecat_mean_e_kernel(tc, xT, w1, w2, w3, offs, cen, pos1, pos2,
 
         def open_out(b, z_q):
             count = PIECES[b][1]
-            accs = [psum.tile([P, count], F32, name="out_acc", tag=("z" if b < last else "acc")) for m in range(N // P)]
+            accs = [bank("out_acc%d_%d" % (b, m), [P, count], (4 + 2 * b + m) if b < last else (2 + m)) for m in range(N // P)]
             for m in range(N // P):
                 mx(accs[m][:], w32, slice(m * P, (m + 1) * P), z_q[0][:], z_q[1][:], True, False)
             return accs
@@ -293,7 +294,7 @@ def tile_picked_sagecat_mean_e_kernel(tc, xT, w1, w2, w3, offs, cen, pos1, pos2,
 
         gather_z(0)
         gather_z(1)
-        z_back = [psum.tile([P, 2, Z_HALF], F32, name="z_back", tag="acc") for half in range(2)]
+        z_back = [bank("z_back%d" % half, [P, 2, Z_HALF], half) for half in range(2)]
         for vt in range(V_TILES):
             turn_back(0, vt)
         gather_z(2)

@@ -26,6 +26,7 @@ V_TILES = V // P
 
 SLICE = 256
 SLICES = S // SLICE
+WARM_UPS = 3
 PIECES = [(0, 256), (256, 128), (384, 128)]
 Z_HALF = V // 2
 GOT_BUFS = 14
@@ -37,8 +38,8 @@ AT_CEN_WOVEN = [AT_Z_PAIRS + 1984, AT_Z_PAIRS, 2560]
 AT_Z_LAST_WORDS = 2048
 AT_ROW = 8192
 AT_W1_10 = 18432
-AT_W1_02 = AT_W1_10 - 2048 + 64
-AT_W1_10_WORDS = 20480
+AT_W1_00 = 22528
+AT_W1_10_WORDS = 24576
 
 
 def tile_picked_sagecat_mean_e_kernel(tc, xT, w1, w2, w3, offs, cen, pos1, pos2, pos3, pos4, out):
@@ -119,6 +120,10 @@ def tile_picked_sagecat_mean_e_kernel(tc, xT, w1, w2, w3, offs, cen, pos1, pos2,
         picked = [sb("picked%d" % g, [P, PACK, S], BF16) for g in range(2)]
         x_words = [sb("x_words%d" % g, [P, S], U32) for g in range(2)]
         x_scales = [sb("x_scales%d" % g, [P, S], U8) for g in range(2)]
+        last_scales = at("x_scales_last", [P, SLICE], U8, AT_W1_10 - SLICE + 64)
+
+        def scales_of(g, first, count):
+            return last_scales[:] if (g, first) == (1, S - SLICE) else x_scales[g][:, first:first + count]
 
         def pick(g, j, first, count):
             nc.vector.tensor_copy(picked[g][:, j, first:first + count], x_raw[g, j][:].indirect(entries(offs_sb, first, count)))
@@ -146,7 +151,7 @@ def tile_picked_sagecat_mean_e_kernel(tc, xT, w1, w2, w3, offs, cen, pos1, pos2,
 
         def quantize_x(g, s, woven):
             cols = slice(s * SLICE, s * SLICE + woven.shape[1] // PACK)
-            nc.vector.quantize_mx(out=x_words[g][:, cols].bitcast(FP8X4), scales=x_scales[g][:, cols], in_=woven[:])
+            nc.vector.quantize_mx(out=x_words[g][:, cols].bitcast(FP8X4), scales=scales_of(g, cols.start, cols.stop - cols.start), in_=woven[:])
 
         pick(0, 0, 0, S)
         pick_on_scalar(0, 1, cast_row(nc.scalar, 0, 1))
@@ -170,15 +175,14 @@ def tile_picked_sagecat_mean_e_kernel(tc, xT, w1, w2, w3, offs, cen, pos1, pos2,
         pick(1, 2, 0, S)
         for s in range(SLICES):
             pick(1, 3, s * SLICE, SLICE)
-        low1, third1, last1 = woven_tile(1, 0, 2), woven_tile(1, 2, 1), woven_tile(1, 3, 1)
+        low1, third1 = woven_tile(1, 0, 2), woven_tile(1, 2, 1)
         weave_x(nc.scalar, 1, 0, low1, 0)
         weave_x(nc.scalar, 1, 1, low1, 1)
         weave_x(nc.scalar, 1, 2, third1)
-        weave_x(nc.vector, 1, 3, last1)
 
         def weave_w1(woven, g, t0, count, copy=nc.scalar.copy):
             src = w1_raw[g][:].rearrange("p j (b t i) -> p b t j i", t=PACK, i=LINE)
-            dst = woven[:].rearrange("p (t b i j) -> p b t j i", b=P // LINE, i=LINE, j=PACK)
+            dst = woven[:, :].rearrange("p (t b i j) -> p b t j i", b=P // LINE, i=LINE, j=PACK)
             copy(dst[:, :, 0:count], src[:, :, t0:t0 + count])
             return woven
 
@@ -189,45 +193,63 @@ def tile_picked_sagecat_mean_e_kernel(tc, xT, w1, w2, w3, offs, cen, pos1, pos2,
             for t in range(count):
                 w1_q[g, t0 + t] = (weights, slice(t * P, (t + 1) * P))
 
-        woven_00 = weave_w1(sb("w1_woven0_0", [P, K_PASS], BF16), 0, 0, 1, nc.vector.tensor_copy)
+        woven_00 = weave_w1(at("w1_woven0_0", [P, K_PASS], BF16, AT_W1_00), 0, 0, 1, nc.vector.tensor_copy)
         quantize_x(1, 0, low1)
         quantize_w1(0, 0, 1, woven_00)
-        quantize_x(1, 3, last1)
+        last1 = at("x_woven13", [P, SLICE * PACK], BF16, AT_W1_00)
+        weave_x(nc.vector, 1, 3, last1)
         quantize_x(1, 2, third1)
         quantize_w1(1, 0, 1, weave_w1(at("w1_woven1_0", [P, K_PASS], BF16, AT_W1_10), 1, 0, 1),
                     at("w1_1_0_words", [P, P], U32, AT_W1_10_WORDS))
-        woven_12 = weave_w1(sb("w1_woven1_2", [P, 2 * K_PASS], BF16), 1, 2, 2)
-        woven_01 = weave_w1(at("w1_woven0_1", [P, K_PASS], BF16, AT_W1_10 - 960), 0, 1, 1, nc.vector.tensor_copy)
-        woven_11 = weave_w1(at("w1_woven1_1", [P, K_PASS], BF16, AT_W1_10 + 960), 1, 1, 1, nc.vector.tensor_copy)
-        quantize_w1(0, 1, 1, woven_01)
+        quantize_x(1, 3, last1)
+        woven_11 = weave_w1(sb("w1_woven1_1", [P, K_PASS], BF16), 1, 1, 1)
+        woven_01 = weave_w1(at("w1_woven0_1", [P, K_PASS], BF16, AT_W1_10 + 64), 0, 1, 1, nc.vector.tensor_copy)
         quantize_w1(1, 1, 1, woven_11)
-        quantize_w1(1, 2, 2, woven_12)
+        quantize_w1(0, 1, 1, woven_01)
 
         h = [sb("h%d" % t, [P, S], F32) for t in range(PACK)]
 
         def one_pass(acc, g, t, first, count):
-            mx(acc[:], w1_q[g, t][0], w1_q[g, t][1], x_words[g][:, first:first + count], x_scales[g][:, first:first + count], g == 0, g == 1)
+            mx(acc, w1_q[g, t][0], w1_q[g, t][1], x_words[g][:, first:first + count], scales_of(g, first, count), g == 0, g == 1)
 
         def open_span(t, first, count, index):
             acc = bank("acc%d_%d" % (t, first), [P, count], index)
-            one_pass(acc, 0, t, first, count)
+            one_pass(acc[:], 0, t, first, count)
             return acc
 
         def close_span(acc, t, first, count):
-            one_pass(acc, 1, t, first, count)
-            nc.scalar.activation(h[t][:, first:first + count], acc[:], RELU)
+            one_pass(acc[:], 1, t, first, count)
+            if (t, first) == (0, SLICE):
+                nc.vector.tensor_scalar_max(h[t][:, first:first + count], acc[:], 0.0)
+            else:
+                nc.scalar.activation(h[t][:, first:first + count], acc[:], RELU)
 
+        def plane(t, index):
+            close_span(open_span(t, 0, BANK, index), t, 0, BANK)
+            acc = bank("upper%d" % t, [P, BANK], index + 1)
+            for first in (BANK, BANK + SLICE):
+                for g in range(2):
+                    one_pass(acc[:, first - BANK:first - BANK + SLICE], g, t, first, SLICE)
+            nc.scalar.activation(h[t][:, BANK:S], acc[:], RELU)
+
+        nc.tensor.transpose(bank("warm_start", [P, P], 7)[:], low1[:, 0:2 * P].bitcast(F32), ident[:])
+        warm = bank("warm", [P, BANK], 7)
+        for step in range(WARM_UPS):
+            mx(warm[:], (x_words[0], x_scales[0]), slice(0, P), x_words[0][:, 0:BANK], x_scales[0][:, 0:BANK], True, True)
         h0_accs = [open_span(0, s * SLICE, SLICE, s) for s in range(SLICES)]
         for s in range(SLICES):
             close_span(h0_accs[s], 0, s * SLICE, SLICE)
-        quantize_w1(0, 2, 2, weave_w1(at("w1_woven0_2", [P, 2 * K_PASS], BF16, AT_W1_10_WORDS), 0, 2, 2))
-        for half in range(2):
-            close_span(open_span(1, half * BANK, BANK, 4 + half), 1, half * BANK, BANK)
-        for t in (2, 3):
-            for half in range(2):
-                close_span(open_span(t, half * BANK, BANK, 10 - 2 * t + half), t, half * BANK, BANK)
+        rest = at("w1_woven_rest", [P, 4 * K_PASS], BF16, AT_W1_10_WORDS)
+        for g in range(2):
+            weave_w1(rest[:, g * 2 * K_PASS:(g + 1) * 2 * K_PASS], g, 2, 2)
+        rest_q = quantize("w1_rest", rest[:])
+        for g in range(2):
+            for t in (2, 3):
+                w1_q[g, t] = (rest_q, slice((2 * g + t - 2) * P, (2 * g + t - 1) * P))
+        for t, index in ((1, 4), (2, 6), (3, 4)):
+            plane(t, index)
 
-        w32_woven = sb("w32_woven", [P, 2 * N * PACK], BF16, "w1_1_2_words")
+        w32_woven = sb("w32_woven", [P, 2 * N * PACK], BF16, "w1_rest_words")
         for i in range(2):
             weave(nc.scalar, w32_woven[:, i * N * PACK:(i + 1) * N * PACK], w32_raw[i][:])
 

@@ -26,7 +26,6 @@ V_TILES = V // P
 
 SLICE = 256
 SLICES = S // SLICE
-WARM_UPS = 3
 PIECES = [(0, 256), (256, 128), (384, 128)]
 Z_HALF = V // 2
 GOT_BUFS = 14
@@ -40,6 +39,12 @@ AT_ROW = 8192
 AT_W1_10 = 18432
 AT_W1_00 = 22528
 AT_W1_10_WORDS = 24576
+OVERLAP = 64
+
+PLANE_BANKS = {1: 4, 2: 6, 3: 4}
+Z_SUM_BANK = 4
+Z_BACK_BANK = 0
+LAST_OUT_BANK = 2
 
 
 def tile_picked_sagecat_mean_e_kernel(tc, xT, w1, w2, w3, offs, cen, pos1, pos2, pos3, pos4, out):
@@ -120,7 +125,7 @@ def tile_picked_sagecat_mean_e_kernel(tc, xT, w1, w2, w3, offs, cen, pos1, pos2,
         picked = [sb("picked%d" % g, [P, PACK, S], BF16) for g in range(2)]
         x_words = [sb("x_words%d" % g, [P, S], U32) for g in range(2)]
         x_scales = [sb("x_scales%d" % g, [P, S], U8) for g in range(2)]
-        last_scales = at("x_scales_last", [P, SLICE], U8, AT_W1_10 - SLICE + 64)
+        last_scales = at("x_scales_last", [P, SLICE], U8, AT_W1_10 - SLICE + OVERLAP)
 
         def scales_of(g, first, count):
             return last_scales[:] if (g, first) == (1, S - SLICE) else x_scales[g][:, first:first + count]
@@ -203,7 +208,7 @@ def tile_picked_sagecat_mean_e_kernel(tc, xT, w1, w2, w3, offs, cen, pos1, pos2,
                     at("w1_1_0_words", [P, P], U32, AT_W1_10_WORDS))
         quantize_x(1, 3, last1)
         woven_11 = weave_w1(sb("w1_woven1_1", [P, K_PASS], BF16), 1, 1, 1)
-        woven_01 = weave_w1(at("w1_woven0_1", [P, K_PASS], BF16, AT_W1_10 + 64), 0, 1, 1, nc.vector.tensor_copy)
+        woven_01 = weave_w1(at("w1_woven0_1", [P, K_PASS], BF16, AT_W1_10 + OVERLAP), 0, 1, 1, nc.vector.tensor_copy)
         quantize_w1(1, 1, 1, woven_11)
         quantize_w1(0, 1, 1, woven_01)
 
@@ -232,10 +237,6 @@ def tile_picked_sagecat_mean_e_kernel(tc, xT, w1, w2, w3, offs, cen, pos1, pos2,
                     one_pass(acc[:, first - BANK:first - BANK + SLICE], g, t, first, SLICE)
             nc.scalar.activation(h[t][:, BANK:S], acc[:], RELU)
 
-        nc.tensor.transpose(bank("warm_start", [P, P], 7)[:], low1[:, 0:2 * P].bitcast(F32), ident[:])
-        warm = bank("warm", [P, BANK], 7)
-        for step in range(WARM_UPS):
-            mx(warm[:], (x_words[0], x_scales[0]), slice(0, P), x_words[0][:, 0:BANK], x_scales[0][:, 0:BANK], True, True)
         h0_accs = [open_span(0, s * SLICE, SLICE, s) for s in range(SLICES)]
         for s in range(SLICES):
             close_span(h0_accs[s], 0, s * SLICE, SLICE)
@@ -246,14 +247,14 @@ def tile_picked_sagecat_mean_e_kernel(tc, xT, w1, w2, w3, offs, cen, pos1, pos2,
         for g in range(2):
             for t in (2, 3):
                 w1_q[g, t] = (rest_q, slice((2 * g + t - 2) * P, (2 * g + t - 1) * P))
-        for t, index in ((1, 4), (2, 6), (3, 4)):
-            plane(t, index)
+        for t in range(1, PACK):
+            plane(t, PLANE_BANKS[t])
 
         w32_woven = sb("w32_woven", [P, 2 * N * PACK], BF16, "w1_rest_words")
         for i in range(2):
             weave(nc.scalar, w32_woven[:, i * N * PACK:(i + 1) * N * PACK], w32_raw[i][:])
 
-        z_sum = [bank("z_sum%d" % vt, [P, PACK, P], 4 + vt) for vt in range(V_TILES)]
+        z_sum = [bank("z_sum%d" % vt, [P, PACK, P], Z_SUM_BANK + vt) for vt in range(V_TILES)]
         z_pairs = [sb("z_pairs0", [P, 8 * P], BF16), at("z_pairs1", [P, 8 * P], BF16, AT_Z_PAIRS)]
 
         def gather_z(t):
@@ -298,7 +299,8 @@ def tile_picked_sagecat_mean_e_kernel(tc, xT, w1, w2, w3, offs, cen, pos1, pos2,
 
         def open_out(b, z_q):
             count = PIECES[b][1]
-            accs = [bank("out_acc%d_%d" % (b, m), [P, count], (4 + 2 * b + m) if b < last else (2 + m)) for m in range(N // P)]
+            first_bank = Z_SUM_BANK + 2 * b if b < last else LAST_OUT_BANK
+            accs = [bank("out_acc%d_%d" % (b, m), [P, count], first_bank + m) for m in range(N // P)]
             for m in range(N // P):
                 mx(accs[m][:], w32, slice(m * P, (m + 1) * P), z_q[0][:], z_q[1][:], True, False)
             return accs
@@ -316,7 +318,7 @@ def tile_picked_sagecat_mean_e_kernel(tc, xT, w1, w2, w3, offs, cen, pos1, pos2,
 
         gather_z(0)
         gather_z(1)
-        z_back = [bank("z_back%d" % half, [P, 2, Z_HALF], half) for half in range(2)]
+        z_back = [bank("z_back%d" % half, [P, 2, Z_HALF], Z_BACK_BANK + half) for half in range(2)]
         for vt in range(V_TILES):
             turn_back(0, vt)
         gather_z(2)

@@ -14,6 +14,8 @@ U8 = mybir.dt.uint8
 FP8X4 = mybir.dt.float8_e4m3fn_x4
 COPY = mybir.ActivationFunctionType.Copy
 RELU = mybir.ActivationFunctionType.Relu
+ADD = mybir.AluOpType.add
+MULT = mybir.AluOpType.mult
 
 P = 128
 PACK = 4
@@ -23,40 +25,31 @@ GROUP = 16
 LINE = 4
 NEIGHBOURS = 4
 V_TILES = V // P
-
 SLICE = 256
-SLICES = S // SLICE
 PIECES = [(0, 256), (256, 128), (384, 128)]
 Z_HALF = V // 2
-GOT_BUFS = 14
 
-AT_GOT = {(2, 2): 0, (2, 3): 2048}
-AT_CEN_GOT = [0, 2048, 0]
-AT_Z_PAIRS = 4096
-AT_CEN_WOVEN = [AT_Z_PAIRS + 1984, AT_Z_PAIRS, 2560]
-AT_Z_LAST_WORDS = 2048
-AT_ROW = 8192
-AT_W1_10 = 18432
-AT_W1_00 = 22528
-AT_W1_10_WORDS = 24576
-OVERLAP = 64
-
-PLANE_BANKS = {1: 4, 2: 6, 3: 4}
-Z_SUM_BANK = 4
-Z_BACK_BANK = 0
-LAST_OUT_BANK = 2
+SPAN = [SLICE, BANK, BANK, BANK]
+H_BANK = [0, 4, 6, 0]
+AT_W1_WORDS = 24576
+AT_GOT = {(2, 3): 12288}
+AT_Z_PAIRS = 2048
+AT_CEN_WOVEN = [64, 2112, 3136]
+AT_CEN_GOT = 12288 - 4096 + 64
+AT_W32_WORDS = 12288 + 64
+AT_W32 = 16384
 
 
 def tile_picked_sagecat_mean_e_kernel(tc, xT, w1, w2, w3, offs, cen, pos1, pos2, pos3, pos4, out):
     nc = tc.nc
+    vec, sca = nc.vector, nc.scalar
     with ExitStack() as ctx:
         keep = ctx.enter_context(tc.tile_pool(name="keep", bufs=1))
         placed = ctx.enter_context(tc.tile_pool(name="placed", bufs=1))
-        ring = ctx.enter_context(tc.tile_pool(name="ring", bufs=GOT_BUFS))
         psum = ctx.enter_context(tc.psum_pool(name="psum", bufs=1))
 
-        def sb(name, shape, dtype, bytes_of=None):
-            return keep.tile(shape, dtype, name=name, tag=(bytes_of or name), align_bytes=64)
+        def sb(name, shape, dtype):
+            return keep.tile(shape, dtype, name=name, tag=name, align_bytes=64)
 
         def at(name, shape, dtype, offset):
             return placed.tile(shape, dtype, name=name, offset=offset, align_bytes=64)
@@ -69,30 +62,32 @@ def tile_picked_sagecat_mean_e_kernel(tc, xT, w1, w2, w3, offs, cen, pos1, pos2,
             nc.sync.dma_start(tile[:], src)
             return tile
 
-        def entries(tile, first, count):
-            return tile[:, first // GROUP:(first + count) // GROUP]
+        def gather(eng, dst, window, offsets, first, count):
+            picked_in = window[:].indirect(offsets[:, first // GROUP:(first + count) // GROUP])
+            if eng is vec:
+                vec.tensor_copy(dst, picked_in)
+            else:
+                sca.activation(dst, picked_in, COPY)
 
-        def line_wise(dst, src):
-            return dst.rearrange("p (c i t) -> p c t i", i=LINE, t=PACK), src.rearrange("p t (c i) -> p c t i", i=LINE)
+        def move(eng, dst, src):
+            if eng is vec:
+                vec.tensor_copy(dst, src)
+            else:
+                sca.copy(dst, src)
 
         def weave(eng, dst, src):
-            dst, src = line_wise(dst, src)
-            if eng is nc.vector:
-                nc.vector.tensor_copy(dst, src)
-            else:
-                nc.scalar.activation(dst, src, COPY)
+            move(eng, dst.rearrange("p (c i t) -> p c t i", i=LINE, t=PACK), src.rearrange("p t (c i) -> p c t i", i=LINE))
 
-        def quantize(name, src, words=None):
+        def quantize(name, src, offset=None):
             width = src.shape[1] // PACK
-            if words is None:
-                words = sb(name + "_words", [P, width], U32)
+            words = sb(name + "_words", [P, width], U32) if offset is None else at(name + "_words", [P, width], U32, offset)
             scales = sb(name + "_scales", [P, width], U8)
-            nc.vector.quantize_mx(out=words[:].bitcast(FP8X4), scales=scales[:], in_=src)
+            vec.quantize_mx(out=words[:].bitcast(FP8X4), scales=scales[:], in_=src)
             return words, scales
 
-        def mx(acc, weights, cols, words, scales, start, stop):
+        def mx(acc, weights, cols, moving, start, stop):
             nc.tensor.matmul_mx(out=acc, lhsT=weights[0][:, cols].bitcast(FP8X4), lhsT_scale=weights[1][:, cols],
-                                rhs=words.bitcast(FP8X4), rhs_scale=scales, start=start, stop=stop)
+                                rhs=moving[0].bitcast(FP8X4), rhs_scale=moving[1], start=start, stop=stop)
 
         ident = sb("ident", [P, P], F32)
         make_identity(nc, ident[:])
@@ -102,10 +97,7 @@ def tile_picked_sagecat_mean_e_kernel(tc, xT, w1, w2, w3, offs, cen, pos1, pos2,
         for g in range(2):
             rows = xT[g * K_PASS:(g + 1) * K_PASS, :].rearrange("(p j) t -> j p t", j=PACK)
             for j in range(PACK):
-                if (g, j) == (1, 0):
-                    x_raw[g, j] = at("x_raw10", [P, T], F32, AT_ROW)
-                else:
-                    x_raw[g, j] = sb("x_raw%d%d" % (g, j), [P, T], F32)
+                x_raw[g, j] = sb("x_raw%d%d" % (g, j), [P, T], F32)
                 nc.sync.dma_start(x_raw[g, j][:], rows[j])
         w1_raw = []
         for g in range(2):
@@ -123,220 +115,201 @@ def tile_picked_sagecat_mean_e_kernel(tc, xT, w1, w2, w3, offs, cen, pos1, pos2,
             w32_raw.append(raw)
 
         picked = [sb("picked%d" % g, [P, PACK, S], BF16) for g in range(2)]
-        x_words = [sb("x_words%d" % g, [P, S], U32) for g in range(2)]
-        x_scales = [sb("x_scales%d" % g, [P, S], U8) for g in range(2)]
-        last_scales = at("x_scales_last", [P, SLICE], U8, AT_W1_10 - SLICE + OVERLAP)
+        x_woven = {(g, half): sb("x_woven%d%d" % (g, half), [P, BANK * PACK], BF16) for g in range(2) for half in range(2)}
+        x_q = {}
 
-        def scales_of(g, first, count):
-            return last_scales[:] if (g, first) == (1, S - SLICE) else x_scales[g][:, first:first + count]
+        def pick(eng, g, j, first, count):
+            gather(eng, picked[g][:, j, first:first + count], x_raw[g, j], offs_sb, first, count)
 
-        def pick(g, j, first, count):
-            nc.vector.tensor_copy(picked[g][:, j, first:first + count], x_raw[g, j][:].indirect(entries(offs_sb, first, count)))
+        def weave_x(eng, g, s):
+            at_col = (s % 2) * SLICE * PACK
+            weave(eng, x_woven[g, s // 2][:, at_col:at_col + SLICE * PACK], picked[g][:, :, s * SLICE:(s + 1) * SLICE])
 
-        def cast_row(eng, g, j):
-            row = sb("x_cast%d%d" % (g, j), [P, T], BF16)
-            if eng is nc.vector:
-                nc.vector.tensor_copy(row[:], x_raw[g, j][:])
-            else:
-                nc.scalar.activation(row[:], x_raw[g, j][:], COPY)
-            return row
-
-        def pick_on_scalar(g, j, row):
-            nc.scalar.activation(picked[g][:, j, :], row[:].indirect(offs_sb[:]), COPY)
-
-        def weave_x(eng, g, s, woven, at_slice=0):
-            dst, src = line_wise(woven[:, at_slice * SLICE * PACK:(at_slice + 1) * SLICE * PACK], picked[g][:, :, s * SLICE:(s + 1) * SLICE])
-            if eng is nc.vector:
-                nc.vector.tensor_copy(dst, src)
-            else:
-                nc.scalar.copy(dst, src)
-
-        def woven_tile(g, s, count):
-            return sb("x_woven%d%d" % (g, s), [P, count * SLICE * PACK], BF16)
-
-        def quantize_x(g, s, woven):
-            cols = slice(s * SLICE, s * SLICE + woven.shape[1] // PACK)
-            nc.vector.quantize_mx(out=x_words[g][:, cols].bitcast(FP8X4), scales=scales_of(g, cols.start, cols.stop - cols.start), in_=woven[:])
-
-        pick(0, 0, 0, S)
-        pick_on_scalar(0, 1, cast_row(nc.scalar, 0, 1))
-        pick(0, 2, 0, S)
-        pick(0, 3, 0, SLICE)
-        pick(0, 3, SLICE, SLICE)
-        pick(0, 3, 2 * SLICE, 2 * SLICE)
-        low0, third0 = woven_tile(0, 0, 2), woven_tile(0, 2, 1)
-        weave_x(nc.scalar, 0, 0, low0, 0)
-        weave_x(nc.scalar, 0, 1, low0, 1)
-        weave_x(nc.scalar, 0, 2, third0)
-        row0 = cast_row(nc.vector, 1, 0)
-        last0 = at("x_woven03", [P, SLICE * PACK], BF16, AT_ROW)
-        weave_x(nc.vector, 0, 3, last0)
-        quantize_x(0, 0, low0)
-        quantize_x(0, 3, last0)
-        quantize_x(0, 2, third0)
-        pick_on_scalar(1, 0, row0)
-        row1 = cast_row(nc.vector, 1, 1)
-        pick_on_scalar(1, 1, row1)
-        pick(1, 2, 0, S)
-        for s in range(SLICES):
-            pick(1, 3, s * SLICE, SLICE)
-        low1, third1 = woven_tile(1, 0, 2), woven_tile(1, 2, 1)
-        weave_x(nc.scalar, 1, 0, low1, 0)
-        weave_x(nc.scalar, 1, 1, low1, 1)
-        weave_x(nc.scalar, 1, 2, third1)
-
-        def weave_w1(woven, g, t0, count, copy=nc.scalar.copy):
-            src = w1_raw[g][:].rearrange("p j (b t i) -> p b t j i", t=PACK, i=LINE)
-            dst = woven[:, :].rearrange("p (t b i j) -> p b t j i", b=P // LINE, i=LINE, j=PACK)
-            copy(dst[:, :, 0:count], src[:, :, t0:t0 + count])
-            return woven
+        def quantize_x(g, half):
+            x_q[g, half] = quantize("x%d%d" % (g, half), x_woven[g, half][:])
 
         w1_q = {}
 
-        def quantize_w1(g, t0, count, woven, words=None):
-            weights = quantize("w1_%d_%d" % (g, t0), woven[:], words)
-            for t in range(count):
-                w1_q[g, t0 + t] = (weights, slice(t * P, (t + 1) * P))
+        w1_groups = [[(0, 0)], [(0, 1)], [(1, 0)], [(1, 1)], [(0, 2), (0, 3), (1, 2), (1, 3)]]
+        w1_woven = [sb("w1_woven%d" % n, [P, len(group) * K_PASS], BF16) for n, group in enumerate(w1_groups[:-1])]
+        w1_woven.append(at("w1_woven_rest", [P, len(w1_groups[-1]) * K_PASS], BF16, AT_W32))
 
-        woven_00 = weave_w1(at("w1_woven0_0", [P, K_PASS], BF16, AT_W1_00), 0, 0, 1, nc.vector.tensor_copy)
-        quantize_x(1, 0, low1)
-        quantize_w1(0, 0, 1, woven_00)
-        last1 = at("x_woven13", [P, SLICE * PACK], BF16, AT_W1_00)
-        weave_x(nc.vector, 1, 3, last1)
-        quantize_x(1, 2, third1)
-        quantize_w1(1, 0, 1, weave_w1(at("w1_woven1_0", [P, K_PASS], BF16, AT_W1_10), 1, 0, 1),
-                    at("w1_1_0_words", [P, P], U32, AT_W1_10_WORDS))
-        quantize_x(1, 3, last1)
-        woven_11 = weave_w1(sb("w1_woven1_1", [P, K_PASS], BF16), 1, 1, 1)
-        woven_01 = weave_w1(at("w1_woven0_1", [P, K_PASS], BF16, AT_W1_10 + OVERLAP), 0, 1, 1, nc.vector.tensor_copy)
-        quantize_w1(1, 1, 1, woven_11)
-        quantize_w1(0, 1, 1, woven_01)
+        def weave_w1(eng, g, t0, count):
+            n = [n for n, group in enumerate(w1_groups) if (g, t0) in group][0]
+            place = w1_groups[n].index((g, t0))
+            src = w1_raw[g][:].rearrange("p j (b t i) -> p b t j i", t=PACK, i=LINE)
+            dst = w1_woven[n][:, place * K_PASS:(place + count) * K_PASS].rearrange("p (t b i j) -> p b t j i", b=P // LINE, i=LINE, j=PACK)
+            move(eng, dst, src[:, :, t0:t0 + count])
+
+        def quantize_w1(n):
+            weights = quantize("w1_%d" % n, w1_woven[n][:], AT_W1_WORDS if n in (2, 4) else None)
+            for place, key in enumerate(w1_groups[n]):
+                w1_q[key] = (weights, slice(place * P, (place + 1) * P))
 
         h = [sb("h%d" % t, [P, S], F32) for t in range(PACK)]
+        h_acc = {}
 
-        def one_pass(acc, g, t, first, count):
-            mx(acc, w1_q[g, t][0], w1_q[g, t][1], x_words[g][:, first:first + count], scales_of(g, first, count), g == 0, g == 1)
+        def h_pass(g, t):
+            width = SPAN[t]
+            for n in range(S // width):
+                if g == 0:
+                    h_acc[t, n] = bank("h_acc%d%d" % (t, n), [P, width], H_BANK[t] + n)
+                words, scales = x_q[g, n * width // BANK]
+                cols = slice(n * width % BANK, n * width % BANK + width)
+                mx(h_acc[t, n][:], w1_q[g, t][0], w1_q[g, t][1], (words[:, cols], scales[:, cols]), g == 0, g == 1)
 
-        def open_span(t, first, count, index):
-            acc = bank("acc%d_%d" % (t, first), [P, count], index)
-            one_pass(acc[:], 0, t, first, count)
-            return acc
-
-        def close_span(acc, t, first, count):
-            one_pass(acc[:], 1, t, first, count)
-            if (t, first) == (0, SLICE):
-                nc.vector.tensor_scalar_max(h[t][:, first:first + count], acc[:], 0.0)
+        def relu(eng, t, n):
+            dst = h[t][:, n * SPAN[t]:(n + 1) * SPAN[t]]
+            if eng is vec:
+                vec.tensor_scalar_max(dst, h_acc[t, n][:], 0.0)
             else:
-                nc.scalar.activation(h[t][:, first:first + count], acc[:], RELU)
+                sca.activation(dst, h_acc[t, n][:], RELU)
 
-        def plane(t, index):
-            close_span(open_span(t, 0, BANK, index), t, 0, BANK)
-            acc = bank("upper%d" % t, [P, BANK], index + 1)
-            for first in (BANK, BANK + SLICE):
-                for g in range(2):
-                    one_pass(acc[:, first - BANK:first - BANK + SLICE], g, t, first, SLICE)
-            nc.scalar.activation(h[t][:, BANK:S], acc[:], RELU)
+        pick(vec, 0, 0, 0, S)
+        pick(sca, 0, 1, 0, S)
+        pick(vec, 0, 2, 0, S)
+        pick(vec, 0, 3, 0, BANK)
+        pick(sca, 0, 3, BANK, BANK)
+        weave_x(vec, 0, 0)
+        weave_x(sca, 0, 3)
+        weave_x(vec, 0, 1)
+        weave_x(vec, 0, 2)
+        quantize_x(0, 0)
+        pick(sca, 1, 0, 0, S)
+        quantize_x(0, 1)
+        pick(vec, 1, 1, 0, S)
+        pick(vec, 1, 2, 0, BANK)
+        pick(sca, 1, 2, BANK, BANK)
+        pick(vec, 1, 3, 0, P)
+        pick(sca, 1, 3, P, P)
+        for s in range(1, 4):
+            pick(sca, 1, 3, s * SLICE, SLICE)
+        weave_x(vec, 1, 0)
+        weave_x(vec, 1, 1)
+        weave_x(vec, 1, 2)
+        quantize_x(1, 0)
+        weave_w1(sca, 0, 0, 1)
+        quantize_w1(0)
+        h_pass(0, 0)
+        weave_x(vec, 1, 3)
+        weave_w1(sca, 0, 1, 1)
+        quantize_x(1, 1)
+        quantize_w1(1)
+        h_pass(0, 1)
+        weave_w1(sca, 0, 2, 2)
+        weave_w1(vec, 1, 0, 1)
+        weave_w1(vec, 1, 2, 1)
+        quantize_w1(2)
+        h_pass(1, 0)
+        weave_w1(sca, 1, 1, 1)
+        weave_w1(sca, 1, 3, 1)
+        quantize_w1(3)
+        h_pass(1, 1)
+        relu(vec, 0, 0)
+        relu(sca, 0, 1)
+        relu(vec, 0, 2)
+        relu(sca, 0, 3)
+        quantize_w1(4)
+        for t in (2, 3):
+            h_pass(0, t)
+            h_pass(1, t)
 
-        h0_accs = [open_span(0, s * SLICE, SLICE, s) for s in range(SLICES)]
-        for s in range(SLICES):
-            close_span(h0_accs[s], 0, s * SLICE, SLICE)
-        rest = at("w1_woven_rest", [P, 4 * K_PASS], BF16, AT_W1_10_WORDS)
-        for g in range(2):
-            weave_w1(rest[:, g * 2 * K_PASS:(g + 1) * 2 * K_PASS], g, 2, 2)
-        rest_q = quantize("w1_rest", rest[:])
-        for g in range(2):
-            for t in (2, 3):
-                w1_q[g, t] = (rest_q, slice((2 * g + t - 2) * P, (2 * g + t - 1) * P))
-        for t in range(1, PACK):
-            plane(t, PLANE_BANKS[t])
-
-        w32_woven = sb("w32_woven", [P, 2 * N * PACK], BF16, "w1_rest_words")
-        for i in range(2):
-            weave(nc.scalar, w32_woven[:, i * N * PACK:(i + 1) * N * PACK], w32_raw[i][:])
-
-        z_sum = [bank("z_sum%d" % vt, [P, PACK, P], Z_SUM_BANK + vt) for vt in range(V_TILES)]
+        z_sum = [bank("z_sum%d" % vt, [P, PACK, P], 2 + vt) for vt in range(V_TILES)]
         z_pairs = [sb("z_pairs0", [P, 8 * P], BF16), at("z_pairs1", [P, 8 * P], BF16, AT_Z_PAIRS)]
 
-        def gather_z(t):
-            for d in range(NEIGHBOURS):
-                if (t, d) in AT_GOT:
-                    got = at("got", [P, V], F32, AT_GOT[t, d])
-                else:
-                    got = ring.tile([P, V], F32, name="got", tag="got")
-                nc.vector.tensor_copy(got[:], h[t][:].indirect(pos_sb[d][:]))
+        def gather_z(eng, t, d):
+            if (t, d) in AT_GOT:
+                got = at("got%d%d" % (t, d), [P, V], F32, AT_GOT[t, d])
+            else:
+                got = sb("got%d%d" % (t, d), [P, V], F32)
+            gather(eng, got[:], h[t], pos_sb[d], 0, V)
+            return got
+
+        def add_z(t, gots):
+            for d, got in enumerate(gots):
                 for vt in range(V_TILES):
                     nc.tensor.matmul(z_sum[vt][:, t, :], got[:, vt * P:(vt + 1) * P], ident[:],
-                                     start=(d == 0), stop=(d == NEIGHBOURS - 1), is_transpose=True)
+                                     start=(d == 0), stop=(d == len(gots) - 1), is_transpose=True)
 
         def turn_back(u, vt):
             pairs = z_pairs[vt // 2][:, (2 * u + vt % 2) * 2 * P:(2 * u + vt % 2 + 1) * 2 * P]
-            nc.scalar.activation(pairs.rearrange("v (p e) -> v p e", e=2),
-                                 z_sum[vt][:, 2 * u:2 * u + 2, :].rearrange("v e p -> v p e"), COPY, scale=1.0 / NEIGHBOURS)
+            sca.activation(pairs.rearrange("v (p i e) -> v p e i", i=LINE, e=2),
+                           z_sum[vt][:, 2 * u:2 * u + 2, :].rearrange("v e (p i) -> v p e i", i=LINE), COPY, scale=1.0 / NEIGHBOURS)
             nc.tensor.transpose(z_back[vt // 2][:, u, (vt % 2) * P:(vt % 2 + 1) * P], pairs.bitcast(F32), ident[:])
 
         def weave_z(half):
             woven = sb("z_woven%d" % half, [P, Z_HALF * PACK], BF16)
-            nc.scalar.copy(woven[:].bitcast(F32).rearrange("p (v u) -> p v u", u=2), z_back[half][:].rearrange("p u v -> p v u"))
+            sca.copy(woven[:].bitcast(F32).rearrange("p (v i u) -> p v u i", i=2, u=2),
+                     z_back[half][:].rearrange("p u (v i) -> p v u i", i=2))
             return woven
 
-        last = len(PIECES) - 1
+        w32_woven = at("w32_woven", [P, 2 * N * PACK], BF16, AT_W32)
+        for i in range(2):
+            dst = w32_woven[:, i * N * PACK:(i + 1) * N * PACK].rearrange("p (c i t) -> p c t i", i=LINE, t=PACK)
+            nc.gpsimd.tensor_scalar(dst, w32_raw[i][:].rearrange("p t (c i) -> p c t i", i=LINE), 1.0, 0.0, MULT, ADD)
+        g03 = gather_z(sca, 0, 3)
+        g02 = gather_z(vec, 0, 2)
+        relu(sca, 1, 0)
+        relu(sca, 1, 1)
+        g01 = gather_z(vec, 0, 1)
+        relu(vec, 2, 0)
+        relu(vec, 2, 1)
+        add_z(0, [g03, g02, g01, gather_z(vec, 0, 0)])
+        for t in range(1, PACK):
+            gots = [gather_z((sca, vec)[d % 2], t, d) for d in range(NEIGHBOURS)]
+            add_z(t, gots)
+            if t == 1:
+                relu(sca, 3, 0)
+                relu(sca, 3, 1)
+        last_sums = gots[2:]
+        z_back = [bank("z_back%d" % half, [P, 2, Z_HALF], 6 + half) for half in range(2)]
+        for vt in range(V_TILES):
+            turn_back(0, vt)
 
-        def gather_cen(b):
+        cen_got = at("cen_got", [P, PACK, V], BF16, AT_CEN_GOT)
+
+        def gather_cen(eng, t, v0=0, count=V):
+            gather(eng, cen_got[:, t, v0:v0 + count], h[t], cen_sb, v0, count)
+
+        def weave_cen(b):
             v0, count = PIECES[b]
-            got = at("cen_got%d" % b, [P, PACK, count], BF16, AT_CEN_GOT[b])
-            for t in range(PACK):
-                nc.vector.tensor_copy(got[:, t, :], h[t][:].indirect(entries(cen_sb, v0, count)))
-            return got
-
-        def weave_cen(b, got):
-            woven = at("cen_woven%d" % b, [P, PIECES[b][1] * PACK], BF16, AT_CEN_WOVEN[b])
-            dst, src = line_wise(woven[:], got[:])
-            if b < last:
-                nc.scalar.copy(dst, src)
-            else:
-                nc.vector.tensor_copy(dst, src)
+            woven = at("cen_woven%d" % b, [P, count * PACK], BF16, AT_CEN_WOVEN[b])
+            weave(vec, woven[:], cen_got[:, :, v0:v0 + count])
             return woven
 
-        def open_out(b, z_q):
+        def open_out(b, z_q, first_bank):
             count = PIECES[b][1]
-            first_bank = Z_SUM_BANK + 2 * b if b < last else LAST_OUT_BANK
             accs = [bank("out_acc%d_%d" % (b, m), [P, count], first_bank + m) for m in range(N // P)]
             for m in range(N // P):
-                mx(accs[m][:], w32, slice(m * P, (m + 1) * P), z_q[0][:], z_q[1][:], True, False)
+                mx(accs[m][:], w32, slice(m * P, (m + 1) * P), z_q, True, False)
             return accs
 
-        def close_out(b, accs, cen_q):
+        def close_out(b, accs, cen_q, engines):
             v0, count = PIECES[b]
             res = sb("res%d" % b, [P, N // P, count], F32)
             for m in range(N // P):
-                mx(accs[m][:], w32, slice(N + m * P, N + (m + 1) * P), cen_q[0][:], cen_q[1][:], False, True)
-                if m == 0 or b < last:
-                    nc.scalar.copy(res[:, m, :], accs[m][:])
-                else:
-                    nc.vector.tensor_copy(res[:, m, :], accs[m][:])
+                mx(accs[m][:], w32, slice(N + m * P, N + (m + 1) * P), (cen_q[0][:], cen_q[1][:]), False, True)
+                move(engines[m], res[:, m, :], accs[m][:])
                 nc.sync.dma_start(out[m * P:(m + 1) * P, v0:v0 + count], res[:, m, :])
 
-        gather_z(0)
-        gather_z(1)
-        z_back = [bank("z_back%d" % half, [P, 2, Z_HALF], Z_BACK_BANK + half) for half in range(2)]
-        for vt in range(V_TILES):
-            turn_back(0, vt)
-        gather_z(2)
-        w32 = quantize("w32", w32_woven[:])
-        gather_z(3)
+        gather_cen(sca, 3)
+        gather_cen(sca, 2, Z_HALF, Z_HALF)
+        w32 = quantize("w32", w32_woven[:], AT_W32_WORDS)
+        gather_cen(vec, 0)
+        gather_cen(vec, 2, 0, Z_HALF)
+        gather_cen(vec, 1)
         for vt in range(V_TILES):
             turn_back(1, vt)
-        cen_got0 = gather_cen(0)
-        cen_got1 = gather_cen(1)
         z_woven0 = weave_z(0)
-        cen_woven0 = weave_cen(0, cen_got0)
         z_woven1 = weave_z(1)
-        cen_woven1 = weave_cen(1, cen_got1)
-        out0 = open_out(0, quantize("z0", z_woven0[:]))
-        close_out(0, out0, quantize("cen0", cen_woven0[:]))
-        cen_got2 = gather_cen(2)
-        out1 = open_out(1, quantize("z1", z_woven1[:, 0:P * PACK]))
-        close_out(1, out1, quantize("cen1", cen_woven1[:]))
-        cen_woven2 = weave_cen(2, cen_got2)
-        out2 = open_out(2, quantize("z2", z_woven1[:, P * PACK:2 * P * PACK], at("z2_words", [P, P], U32, AT_Z_LAST_WORDS)))
-        close_out(2, out2, quantize("cen2", cen_woven2[:]))
+        cen_woven0 = weave_cen(0)
+        z0 = quantize("z0", z_woven0[:])
+        out0 = open_out(0, (z0[0][:], z0[1][:]), 0)
+        close_out(0, out0, quantize("cen0", cen_woven0[:]), (sca, sca))
+        z1 = quantize("z1", z_woven1[:])
+        cen_woven1 = weave_cen(1)
+        out1 = open_out(1, (z1[0][:, 0:P], z1[1][:, 0:P]), 2)
+        out2 = open_out(2, (z1[0][:, P:2 * P], z1[1][:, P:2 * P]), 4)
+        cen_woven2 = weave_cen(2)
+        close_out(1, out1, quantize("cen1", cen_woven1[:]), (sca, sca))
+        close_out(2, out2, quantize("cen2", cen_woven2[:]), (sca, vec))

@@ -30,6 +30,7 @@ PIECES = [(0, 256), (256, 128), (384, 128)]
 Z_HALF = V // 2
 
 SPAN = [SLICE, BANK, BANK, BANK]
+SHARE = 18
 H_BANK = [0, 4, 6, 0]
 AT_W1_WORDS = 24576
 AT_GOT = {(2, 3): 12288}
@@ -92,13 +93,14 @@ def tile_picked_sagecat_mean_e_kernel(tc, xT, w1, w2, w3, offs, cen, pos1, pos2,
         ident = sb("ident", [P, P], F32)
         make_identity(nc, ident[:])
 
-        offs_sb = load_list("offs", offs)
         x_raw = {}
         for g in range(2):
             rows = xT[g * K_PASS:(g + 1) * K_PASS, :].rearrange("(p j) t -> j p t", j=PACK)
             for j in range(PACK):
                 x_raw[g, j] = sb("x_raw%d%d" % (g, j), [P, T], F32)
                 nc.sync.dma_start(x_raw[g, j][:], rows[j])
+                if (g, j) == (0, 0):
+                    offs_sb = load_list("offs", offs)
         w1_raw = []
         for g in range(2):
             raw = sb("w1_raw%d" % g, [P, PACK, H], F32)
@@ -134,12 +136,12 @@ def tile_picked_sagecat_mean_e_kernel(tc, xT, w1, w2, w3, offs, cen, pos1, pos2,
         w1_woven = [sb("w1_woven%d" % n, [P, len(group) * K_PASS], BF16) for n, group in enumerate(w1_groups[:-1])]
         w1_woven.append(at("w1_woven_rest", [P, len(w1_groups[-1]) * K_PASS], BF16, AT_W32))
 
-        def weave_w1(eng, g, t0, count):
+        def weave_w1(eng, g, t0, count, runs=slice(0, P // LINE)):
             n = [n for n, group in enumerate(w1_groups) if (g, t0) in group][0]
             place = w1_groups[n].index((g, t0))
             src = w1_raw[g][:].rearrange("p j (b t i) -> p b t j i", t=PACK, i=LINE)
             dst = w1_woven[n][:, place * K_PASS:(place + count) * K_PASS].rearrange("p (t b i j) -> p b t j i", b=P // LINE, i=LINE, j=PACK)
-            move(eng, dst, src[:, :, t0:t0 + count])
+            move(eng, dst[:, runs], src[:, runs, t0:t0 + count])
 
         def quantize_w1(n):
             weights = quantize("w1_%d" % n, w1_woven[n][:], AT_W1_WORDS if n in (2, 4) else None)
@@ -197,11 +199,12 @@ def tile_picked_sagecat_mean_e_kernel(tc, xT, w1, w2, w3, offs, cen, pos1, pos2,
         quantize_w1(1)
         h_pass(0, 1)
         weave_w1(sca, 0, 2, 2)
-        weave_w1(vec, 1, 0, 1)
-        weave_w1(vec, 1, 2, 1)
+        weave_w1(vec, 1, 0, 1, slice(0, SHARE))
+        weave_w1(sca, 1, 0, 1, slice(SHARE, P // LINE))
         quantize_w1(2)
         h_pass(1, 0)
-        weave_w1(sca, 1, 1, 1)
+        weave_w1(vec, 1, 1, 1)
+        weave_w1(vec, 1, 2, 1)
         weave_w1(sca, 1, 3, 1)
         quantize_w1(3)
         h_pass(1, 1)

@@ -33,12 +33,13 @@ SPAN = [SLICE, BANK, BANK, BANK]
 SHARE = 18
 H_BANK = [0, 4, 6, 0]
 AT_W1_WORDS = 24576
-AT_GOT = {(2, 3): 12288}
-AT_Z_PAIRS = 2048
-AT_CEN_WOVEN = [64, 2112, 3136]
+AT_GOT = 12288
+AT_W2_RAW = 26624
+AT_Z_LOW = 2048
+AT_CEN_WOVEN = [2112, 4160, 5184]
 AT_CEN_GOT = 12288 - 4096 + 64
-AT_W32_WORDS = 12288 + 64
-AT_W32 = 16384
+AT_W32_WORDS = 64
+AT_W32 = 20480
 
 
 def tile_picked_sagecat_mean_e_kernel(tc, xT, w1, w2, w3, offs, cen, pos1, pos2, pos3, pos4, out):
@@ -110,7 +111,7 @@ def tile_picked_sagecat_mean_e_kernel(tc, xT, w1, w2, w3, offs, cen, pos1, pos2,
         cen_sb = load_list("cen", cen)
         w32_raw = []
         for name, src in (("w3_raw", w3), ("w2_raw", w2)):
-            raw = sb(name, [P, PACK, N], F32)
+            raw = at(name, [P, PACK, N], F32, AT_W2_RAW) if name == "w2_raw" else sb(name, [P, PACK, N], F32)
             dealt = src.rearrange("(b t r) c -> t b r c", t=PACK, r=LINE)
             for t in range(PACK):
                 nc.sync.dma_start(raw[:, t, :], dealt[t])
@@ -217,28 +218,37 @@ def tile_picked_sagecat_mean_e_kernel(tc, xT, w1, w2, w3, offs, cen, pos1, pos2,
             h_pass(0, t)
             h_pass(1, t)
 
-        z_sum = [bank("z_sum%d" % vt, [P, PACK, P], 2 + vt) for vt in range(V_TILES)]
-        z_pairs = [sb("z_pairs0", [P, 8 * P], BF16), at("z_pairs1", [P, 8 * P], BF16, AT_Z_PAIRS)]
+        z_sum = {vt: bank("z_sum%d" % vt, [P, PACK, P], 2 + vt) for vt in (2, 3)}
+        z_pairs = {1: sb("z_pairs1", [P, 8 * P], BF16)}
+        z_low = at("z_low", [P, PACK, Z_HALF], F32, AT_Z_LOW)
 
-        def gather_z(eng, t, d):
-            if (t, d) in AT_GOT:
-                got = at("got%d%d" % (t, d), [P, V], F32, AT_GOT[t, d])
-            else:
-                got = sb("got%d%d" % (t, d), [P, V], F32)
-            gather(eng, got[:], h[t], pos_sb[d], 0, V)
-            return got
+        got = {}
 
-        def add_z(t, gots):
-            for d, got in enumerate(gots):
-                for vt in range(V_TILES):
-                    nc.tensor.matmul(z_sum[vt][:, t, :], got[:, vt * P:(vt + 1) * P], ident[:],
-                                     start=(d == 0), stop=(d == len(gots) - 1), is_transpose=True)
+        def columns(t, half, d):
+            if t >= 2:
+                return got[t, half][:, d, :]
+            return got[t][:, d, half * Z_HALF:(half + 1) * Z_HALF]
+
+        def add_low(t):
+            two = at("two%d" % t, [P, 2, Z_HALF], F32, AT_W2_RAW + t % 2 * 2 * Z_HALF * 4)
+            nc.gpsimd.tensor_tensor(two[:], columns(t, 0, slice(0, 2)), columns(t, 0, slice(2, 4)), ADD)
+            nc.gpsimd.tensor_tensor(z_low[:, t, :], two[:, 0, :], two[:, 1, :], ADD)
+
+        def add_z(t):
+            for d in range(NEIGHBOURS):
+                for vt in (2, 3):
+                    nc.tensor.matmul(z_sum[vt][:, t, :], columns(t, 1, d)[:, (vt - 2) * P:(vt - 1) * P], ident[:],
+                                     start=(d == 0), stop=(d == NEIGHBOURS - 1), is_transpose=True)
 
         def turn_back(u, vt):
             pairs = z_pairs[vt // 2][:, (2 * u + vt % 2) * 2 * P:(2 * u + vt % 2 + 1) * 2 * P]
             sca.activation(pairs.rearrange("v (p i e) -> v p e i", i=LINE, e=2),
                            z_sum[vt][:, 2 * u:2 * u + 2, :].rearrange("v e (p i) -> v p e i", i=LINE), COPY, scale=1.0 / NEIGHBOURS)
             nc.tensor.transpose(z_back[vt // 2][:, u, (vt % 2) * P:(vt % 2 + 1) * P], pairs.bitcast(F32), ident[:])
+
+        def on_gpsimd(dst, src, factor):
+            nc.gpsimd.tensor_scalar(dst.rearrange("p (c i t) -> p c t i", i=LINE, t=PACK),
+                                    src.rearrange("p t (c i) -> p c t i", i=LINE), factor, 0.0, MULT, ADD)
 
         def weave_z(half):
             woven = sb("z_woven%d" % half, [P, Z_HALF * PACK], BF16)
@@ -248,25 +258,29 @@ def tile_picked_sagecat_mean_e_kernel(tc, xT, w1, w2, w3, offs, cen, pos1, pos2,
 
         w32_woven = at("w32_woven", [P, 2 * N * PACK], BF16, AT_W32)
         for i in range(2):
-            dst = w32_woven[:, i * N * PACK:(i + 1) * N * PACK].rearrange("p (c i t) -> p c t i", i=LINE, t=PACK)
-            nc.gpsimd.tensor_scalar(dst, w32_raw[i][:].rearrange("p t (c i) -> p c t i", i=LINE), 1.0, 0.0, MULT, ADD)
-        g03 = gather_z(sca, 0, 3)
-        g02 = gather_z(vec, 0, 2)
-        relu(sca, 1, 0)
-        relu(sca, 1, 1)
-        g01 = gather_z(vec, 0, 1)
-        relu(vec, 2, 0)
-        relu(vec, 2, 1)
-        add_z(0, [g03, g02, g01, gather_z(vec, 0, 0)])
-        for t in range(1, PACK):
-            gots = [gather_z((sca, vec)[d % 2], t, d) for d in range(NEIGHBOURS)]
-            add_z(t, gots)
-            if t == 1:
-                relu(sca, 3, 0)
-                relu(sca, 3, 1)
-        last_sums = gots[2:]
-        z_back = [bank("z_back%d" % half, [P, 2, Z_HALF], 6 + half) for half in range(2)]
-        for vt in range(V_TILES):
+            on_gpsimd(w32_woven[:, i * N * PACK:(i + 1) * N * PACK], w32_raw[i][:], 1.0)
+        for t in range(2):
+            got[t] = sb("got%d" % t, [P, NEIGHBOURS, V], F32)
+            for d in range(NEIGHBOURS):
+                gather((sca, vec)[d % 2], got[t][:, d, :], h[t], pos_sb[d], 0, V)
+                if (t, d) == (0, 1):
+                    relu(sca, 1, 0)
+                    relu(sca, 1, 1)
+            add_low(t)
+            add_z(t)
+            relu((vec, sca)[t], 2 + t, 0)
+            relu((vec, sca)[t], 2 + t, 1)
+        for t in (2, 3):
+            for half in range(2):
+                shape = [P, NEIGHBOURS, Z_HALF]
+                got[t, half] = at("got21", shape, F32, AT_GOT) if (t, half) == (2, 1) else sb("got%d%d" % (t, half), shape, F32)
+                for d in range(NEIGHBOURS):
+                    gather((sca, vec)[d % 2], columns(t, half, d), h[t], pos_sb[d], half * Z_HALF, Z_HALF)
+            add_low(t)
+            add_z(t)
+        z_woven0 = sb("z_woven0", [P, Z_HALF * PACK], BF16)
+        z_back = {1: bank("z_back1", [P, 2, Z_HALF], 7)}
+        for vt in (2, 3):
             turn_back(0, vt)
 
         cen_got = at("cen_got", [P, PACK, V], BF16, AT_CEN_GOT)
@@ -296,20 +310,20 @@ def tile_picked_sagecat_mean_e_kernel(tc, xT, w1, w2, w3, offs, cen, pos1, pos2,
                 nc.sync.dma_start(out[m * P:(m + 1) * P, v0:v0 + count], res[:, m, :])
 
         gather_cen(sca, 3)
-        gather_cen(sca, 2, Z_HALF, Z_HALF)
-        w32 = quantize("w32", w32_woven[:], AT_W32_WORDS)
+        gather_cen(sca, 2)
         gather_cen(vec, 0)
-        gather_cen(vec, 2, 0, Z_HALF)
         gather_cen(vec, 1)
-        for vt in range(V_TILES):
+        for vt in (2, 3):
             turn_back(1, vt)
-        z_woven0 = weave_z(0)
+        vec.tensor_scalar_mul(z_woven0[:].rearrange("p (c i t) -> p c t i", i=LINE, t=PACK),
+                              z_low[:].rearrange("p t (c i) -> p c t i", i=LINE), 1.0 / NEIGHBOURS)
+        w32 = quantize("w32", w32_woven[:], AT_W32_WORDS)
         z_woven1 = weave_z(1)
-        cen_woven0 = weave_cen(0)
         z0 = quantize("z0", z_woven0[:])
+        cen_woven0 = weave_cen(0)
         out0 = open_out(0, (z0[0][:], z0[1][:]), 0)
-        close_out(0, out0, quantize("cen0", cen_woven0[:]), (sca, sca))
         z1 = quantize("z1", z_woven1[:])
+        close_out(0, out0, quantize("cen0", cen_woven0[:]), (sca, sca))
         cen_woven1 = weave_cen(1)
         out1 = open_out(1, (z1[0][:, 0:P], z1[1][:, 0:P]), 2)
         out2 = open_out(2, (z1[0][:, P:2 * P], z1[1][:, P:2 * P]), 4)

@@ -278,7 +278,7 @@ def tile_picked_sagecat_mean_e_kernel(tc, xT, w1, w2, w3, offs, cen, pos1, pos2,
                     gather((sca, vec)[d % 2], columns(t, half, d), h[t], pos_sb[d], half * Z_HALF, Z_HALF)
             add_low(t)
             add_z(t)
-        z_woven0 = sb("z_woven0", [P, Z_HALF * PACK], BF16)
+        z_woven0 = at("z_woven0", [P, Z_HALF * PACK], BF16, AT_GOT + 64)
         z_back = {1: bank("z_back1", [P, 2, Z_HALF], 7)}
         for vt in (2, 3):
             turn_back(0, vt)
@@ -309,10 +309,10 @@ def tile_picked_sagecat_mean_e_kernel(tc, xT, w1, w2, w3, offs, cen, pos1, pos2,
                 move(engines[m], res[:, m, :], accs[m][:])
                 nc.sync.dma_start(out[m * P:(m + 1) * P, v0:v0 + count], res[:, m, :])
 
-        gather_cen(sca, 3)
-        gather_cen(sca, 2)
         gather_cen(vec, 0)
         gather_cen(vec, 1)
+        gather_cen(sca, 2)
+        gather_cen(sca, 3)
         for vt in (2, 3):
             turn_back(1, vt)
         vec.tensor_scalar_mul(z_woven0[:].rearrange("p (c i t) -> p c t i", i=LINE, t=PACK),
@@ -321,12 +321,12 @@ def tile_picked_sagecat_mean_e_kernel(tc, xT, w1, w2, w3, offs, cen, pos1, pos2,
         z_woven1 = weave_z(1)
         z0 = quantize("z0", z_woven0[:])
         cen_woven0 = weave_cen(0)
-        out0 = open_out(0, (z0[0][:], z0[1][:]), 0)
-        z1 = quantize("z1", z_woven1[:])
+        out0 = open_out(0, (z0[0][:], z0[1][:]), 4)
+        z1 = quantize("z1", z_woven1[:], AT_GOT + 64)
         close_out(0, out0, quantize("cen0", cen_woven0[:]), (sca, sca))
         cen_woven1 = weave_cen(1)
-        out1 = open_out(1, (z1[0][:, 0:P], z1[1][:, 0:P]), 2)
-        out2 = open_out(2, (z1[0][:, P:2 * P], z1[1][:, P:2 * P]), 4)
+        out1 = open_out(1, (z1[0][:, 0:P], z1[1][:, 0:P]), 0)
+        out2 = open_out(2, (z1[0][:, P:2 * P], z1[1][:, P:2 * P]), 2)
         cen_woven2 = weave_cen(2)
         close_out(1, out1, quantize("cen1", cen_woven1[:]), (sca, sca))
         close_out(2, out2, quantize("cen2", cen_woven2[:]), (sca, vec))

@@ -262,20 +262,21 @@ def tile_picked_sagecat_mean_e_kernel(tc, xT, w1, w2, w3, offs, cen, pos1, pos2,
         for t in range(2):
             got[t] = sb("got%d" % t, [P, NEIGHBOURS, V], F32)
             for d in range(NEIGHBOURS):
-                gather((sca, vec)[d % 2], got[t][:, d, :], h[t], pos_sb[d], 0, V)
+                gather(sca if (t, d) in ((0, 0), (0, 2), (1, 0)) else vec, got[t][:, d, :], h[t], pos_sb[d], 0, V)
                 if (t, d) == (0, 1):
                     relu(sca, 1, 0)
                     relu(sca, 1, 1)
             add_low(t)
             add_z(t)
-            relu((vec, sca)[t], 2 + t, 0)
-            relu((vec, sca)[t], 2 + t, 1)
+        for t in (2, 3):
+            relu(sca, t, 0)
+            relu(sca, t, 1)
         for t in (2, 3):
             for half in range(2):
                 shape = [P, NEIGHBOURS, Z_HALF]
                 got[t, half] = at("got21", shape, F32, AT_GOT) if (t, half) == (2, 1) else sb("got%d%d" % (t, half), shape, F32)
                 for d in range(NEIGHBOURS):
-                    gather((sca, vec)[d % 2], columns(t, half, d), h[t], pos_sb[d], half * Z_HALF, Z_HALF)
+                    gather(sca if half == 1 or (t, d) == (3, 0) else vec, columns(t, half, d), h[t], pos_sb[d], half * Z_HALF, Z_HALF)
             add_low(t)
             add_z(t)
         z_woven0 = at("z_woven0", [P, Z_HALF * PACK], BF16, AT_GOT + 64)
@@ -294,18 +295,18 @@ def tile_picked_sagecat_mean_e_kernel(tc, xT, w1, w2, w3, offs, cen, pos1, pos2,
             weave(vec, woven[:], cen_got[:, :, v0:v0 + count])
             return woven
 
-        def open_out(b, z_q, first_bank):
+        def open_out(b, matrix, moving, first_bank):
             count = PIECES[b][1]
             accs = [bank("out_acc%d_%d" % (b, m), [P, count], first_bank + m) for m in range(N // P)]
             for m in range(N // P):
-                mx(accs[m][:], w32, slice(m * P, (m + 1) * P), z_q, True, False)
+                mx(accs[m][:], w32, slice(matrix * N + m * P, matrix * N + (m + 1) * P), (moving[0][:], moving[1][:]), True, False)
             return accs
 
-        def close_out(b, accs, cen_q, engines):
+        def close_out(b, accs, matrix, moving, engines):
             v0, count = PIECES[b]
             res = sb("res%d" % b, [P, N // P, count], F32)
             for m in range(N // P):
-                mx(accs[m][:], w32, slice(N + m * P, N + (m + 1) * P), (cen_q[0][:], cen_q[1][:]), False, True)
+                mx(accs[m][:], w32, slice(matrix * N + m * P, matrix * N + (m + 1) * P), (moving[0][:], moving[1][:]), False, True)
                 move(engines[m], res[:, m, :], accs[m][:])
                 nc.sync.dma_start(out[m * P:(m + 1) * P, v0:v0 + count], res[:, m, :])
 
@@ -319,14 +320,13 @@ def tile_picked_sagecat_mean_e_kernel(tc, xT, w1, w2, w3, offs, cen, pos1, pos2,
                               z_low[:].rearrange("p t (c i) -> p c t i", i=LINE), 1.0 / NEIGHBOURS)
         w32 = quantize("w32", w32_woven[:], AT_W32_WORDS)
         z_woven1 = weave_z(1)
-        z0 = quantize("z0", z_woven0[:])
+        out0 = open_out(0, 0, quantize("z0", z_woven0[:]), 4)
         cen_woven0 = weave_cen(0)
-        out0 = open_out(0, (z0[0][:], z0[1][:]), 4)
-        z1 = quantize("z1", z_woven1[:], AT_GOT + 64)
-        close_out(0, out0, quantize("cen0", cen_woven0[:]), (sca, sca))
         cen_woven1 = weave_cen(1)
-        out1 = open_out(1, (z1[0][:, 0:P], z1[1][:, 0:P]), 0)
-        out2 = open_out(2, (z1[0][:, P:2 * P], z1[1][:, P:2 * P]), 2)
+        close_out(0, out0, 1, quantize("cen0", cen_woven0[:]), (sca, sca))
         cen_woven2 = weave_cen(2)
-        close_out(1, out1, quantize("cen1", cen_woven1[:]), (sca, sca))
-        close_out(2, out2, quantize("cen2", cen_woven2[:]), (sca, vec))
+        out1 = open_out(1, 1, quantize("cen1", cen_woven1[:]), 0)
+        out2 = open_out(2, 1, quantize("cen2", cen_woven2[:]), 2)
+        for b, accs in ((1, out1), (2, out2)):
+            z_q = quantize("z%d" % b, z_woven1[:, (b - 1) * P * PACK:b * P * PACK], AT_GOT + 64 + (b - 1) * P * 4)
+            close_out(b, accs, 0, z_q, (vec, sca))

@@ -23,23 +23,33 @@ K_PASS = P * PACK
 BANK = 512
 GROUP = 16
 LINE = 4
+RUNS = P // LINE
 NEIGHBOURS = 4
-V_TILES = V // P
-SLICE = 256
-PIECES = [(0, 256), (256, 128), (384, 128)]
-Z_HALF = V // 2
+HALF = V // 2
+LOW, HIGH = 0, 1
+W3, W2 = 0, 1
 
+SLICE = 256
 SPAN = [SLICE, BANK, BANK, BANK]
-SHARE = 18
+VECTOR_RUNS = 18
+VECTOR_CEN = 192
+PIECES = [(0, 256), (256, 128), (384, 128)]
+
 H_BANK = [0, 4, 6, 0]
-AT_W1_WORDS = 24576
-AT_GOT = 12288
-AT_W2_RAW = 26624
+Z_SUM_BANK = 4
+Z_BACK_BANK = 6
+OUT_BANK = [4, 0, 2]
+
+OVERLAP = 64
 AT_Z_LOW = 2048
-AT_CEN_WOVEN = [2112, 4160, 5184]
-AT_CEN_GOT = 12288 - 4096 + 64
-AT_W32_WORDS = 64
-AT_W32 = 20480
+AT_HIGH2 = 12288
+AT_W1_REST = 20480
+AT_W1_WORDS = 24576
+AT_W2_RAW = 26624
+AT_CEN_GOT = AT_HIGH2 - 4096 + OVERLAP
+AT_Z_WOVEN = AT_HIGH2 + OVERLAP
+AT_W32_WORDS = AT_W2_RAW + OVERLAP
+AT_CEN_WOVEN = [AT_W32_WORDS + 2048, AT_Z_LOW + 2048 + OVERLAP, AT_Z_LOW + 3072 + OVERLAP]
 
 
 def tile_picked_sagecat_mean_e_kernel(tc, xT, w1, w2, w3, offs, cen, pos1, pos2, pos3, pos4, out):
@@ -50,10 +60,9 @@ def tile_picked_sagecat_mean_e_kernel(tc, xT, w1, w2, w3, offs, cen, pos1, pos2,
         placed = ctx.enter_context(tc.tile_pool(name="placed", bufs=1))
         psum = ctx.enter_context(tc.psum_pool(name="psum", bufs=1))
 
-        def sb(name, shape, dtype):
-            return keep.tile(shape, dtype, name=name, tag=name, align_bytes=64)
-
-        def at(name, shape, dtype, offset):
+        def sb(name, shape, dtype, offset=None):
+            if offset is None:
+                return keep.tile(shape, dtype, name=name, tag=name, align_bytes=64)
             return placed.tile(shape, dtype, name=name, offset=offset, align_bytes=64)
 
         def bank(name, shape, index):
@@ -65,11 +74,11 @@ def tile_picked_sagecat_mean_e_kernel(tc, xT, w1, w2, w3, offs, cen, pos1, pos2,
             return tile
 
         def gather(eng, dst, window, offsets, first, count):
-            picked_in = window[:].indirect(offsets[:, first // GROUP:(first + count) // GROUP])
+            looked_up = window[:].indirect(offsets[:, first // GROUP:(first + count) // GROUP])
             if eng is vec:
-                vec.tensor_copy(dst, picked_in)
+                vec.tensor_copy(dst, looked_up)
             else:
-                sca.activation(dst, picked_in, COPY)
+                sca.activation(dst, looked_up, COPY)
 
         def move(eng, dst, src):
             if eng is vec:
@@ -77,19 +86,19 @@ def tile_picked_sagecat_mean_e_kernel(tc, xT, w1, w2, w3, offs, cen, pos1, pos2,
             else:
                 sca.copy(dst, src)
 
-        def weave(eng, dst, src):
-            move(eng, dst.rearrange("p (c i t) -> p c t i", i=LINE, t=PACK), src.rearrange("p t (c i) -> p c t i", i=LINE))
+        def line_wise(dst, src):
+            return dst.rearrange("p (c i t) -> p c t i", i=LINE, t=PACK), src.rearrange("p t (c i) -> p c t i", i=LINE)
 
         def quantize(name, src, offset=None):
             width = src.shape[1] // PACK
-            words = sb(name + "_words", [P, width], U32) if offset is None else at(name + "_words", [P, width], U32, offset)
+            words = sb(name + "_words", [P, width], U32, offset)
             scales = sb(name + "_scales", [P, width], U8)
             vec.quantize_mx(out=words[:].bitcast(FP8X4), scales=scales[:], in_=src)
             return words, scales
 
-        def mx(acc, weights, cols, moving, start, stop):
+        def mx(acc, weights, cols, words, scales, start, stop):
             nc.tensor.matmul_mx(out=acc, lhsT=weights[0][:, cols].bitcast(FP8X4), lhsT_scale=weights[1][:, cols],
-                                rhs=moving[0].bitcast(FP8X4), rhs_scale=moving[1], start=start, stop=stop)
+                                rhs=words.bitcast(FP8X4), rhs_scale=scales, start=start, stop=stop)
 
         ident = sb("ident", [P, P], F32)
         make_identity(nc, ident[:])
@@ -110,15 +119,15 @@ def tile_picked_sagecat_mean_e_kernel(tc, xT, w1, w2, w3, offs, cen, pos1, pos2,
         pos_sb = [load_list("pos%d" % (d + 1), src) for d, src in enumerate((pos1, pos2, pos3, pos4))]
         cen_sb = load_list("cen", cen)
         w32_raw = []
-        for name, src in (("w3_raw", w3), ("w2_raw", w2)):
-            raw = at(name, [P, PACK, N], F32, AT_W2_RAW) if name == "w2_raw" else sb(name, [P, PACK, N], F32)
+        for name, src, offset in (("w3_raw", w3, None), ("w2_raw", w2, AT_W2_RAW)):
+            raw = sb(name, [P, PACK, N], F32, offset)
             dealt = src.rearrange("(b t r) c -> t b r c", t=PACK, r=LINE)
             for t in range(PACK):
                 nc.sync.dma_start(raw[:, t, :], dealt[t])
             w32_raw.append(raw)
 
         picked = [sb("picked%d" % g, [P, PACK, S], BF16) for g in range(2)]
-        x_woven = {(g, half): sb("x_woven%d%d" % (g, half), [P, BANK * PACK], BF16) for g in range(2) for half in range(2)}
+        x_woven = {(g, n): sb("x_woven%d%d" % (g, n), [P, BANK * PACK], BF16) for g in range(2) for n in range(2)}
         x_q = {}
 
         def pick(eng, g, j, first, count):
@@ -126,26 +135,26 @@ def tile_picked_sagecat_mean_e_kernel(tc, xT, w1, w2, w3, offs, cen, pos1, pos2,
 
         def weave_x(eng, g, s):
             at_col = (s % 2) * SLICE * PACK
-            weave(eng, x_woven[g, s // 2][:, at_col:at_col + SLICE * PACK], picked[g][:, :, s * SLICE:(s + 1) * SLICE])
+            move(eng, *line_wise(x_woven[g, s // 2][:, at_col:at_col + SLICE * PACK], picked[g][:, :, s * SLICE:(s + 1) * SLICE]))
 
-        def quantize_x(g, half):
-            x_q[g, half] = quantize("x%d%d" % (g, half), x_woven[g, half][:])
-
-        w1_q = {}
+        def quantize_x(g, n):
+            x_q[g, n] = quantize("x%d%d" % (g, n), x_woven[g, n][:])
 
         w1_groups = [[(0, 0)], [(0, 1)], [(1, 0)], [(1, 1)], [(0, 2), (0, 3), (1, 2), (1, 3)]]
-        w1_woven = [sb("w1_woven%d" % n, [P, len(group) * K_PASS], BF16) for n, group in enumerate(w1_groups[:-1])]
-        w1_woven.append(at("w1_woven_rest", [P, len(w1_groups[-1]) * K_PASS], BF16, AT_W32))
+        w1_words_at = [None, None, AT_W1_WORDS, None, AT_W1_WORDS]
+        w1_woven_at = [None, None, None, None, AT_W1_REST]
+        w1_woven = [sb("w1_woven%d" % n, [P, len(group) * K_PASS], BF16, w1_woven_at[n]) for n, group in enumerate(w1_groups)]
+        w1_q = {}
 
-        def weave_w1(eng, g, t0, count, runs=slice(0, P // LINE)):
+        def weave_w1(eng, g, t0, count, runs=slice(0, RUNS)):
             n = [n for n, group in enumerate(w1_groups) if (g, t0) in group][0]
             place = w1_groups[n].index((g, t0))
             src = w1_raw[g][:].rearrange("p j (b t i) -> p b t j i", t=PACK, i=LINE)
-            dst = w1_woven[n][:, place * K_PASS:(place + count) * K_PASS].rearrange("p (t b i j) -> p b t j i", b=P // LINE, i=LINE, j=PACK)
+            dst = w1_woven[n][:, place * K_PASS:(place + count) * K_PASS].rearrange("p (t b i j) -> p b t j i", b=RUNS, i=LINE, j=PACK)
             move(eng, dst[:, runs], src[:, runs, t0:t0 + count])
 
         def quantize_w1(n):
-            weights = quantize("w1_%d" % n, w1_woven[n][:], AT_W1_WORDS if n in (2, 4) else None)
+            weights = quantize("w1_%d" % n, w1_woven[n][:], w1_words_at[n])
             for place, key in enumerate(w1_groups[n]):
                 w1_q[key] = (weights, slice(place * P, (place + 1) * P))
 
@@ -159,7 +168,7 @@ def tile_picked_sagecat_mean_e_kernel(tc, xT, w1, w2, w3, offs, cen, pos1, pos2,
                     h_acc[t, n] = bank("h_acc%d%d" % (t, n), [P, width], H_BANK[t] + n)
                 words, scales = x_q[g, n * width // BANK]
                 cols = slice(n * width % BANK, n * width % BANK + width)
-                mx(h_acc[t, n][:], w1_q[g, t][0], w1_q[g, t][1], (words[:, cols], scales[:, cols]), g == 0, g == 1)
+                mx(h_acc[t, n][:], w1_q[g, t][0], w1_q[g, t][1], words[:, cols], scales[:, cols], g == 0, g == 1)
 
         def relu(eng, t, n):
             dst = h[t][:, n * SPAN[t]:(n + 1) * SPAN[t]]
@@ -185,7 +194,7 @@ def tile_picked_sagecat_mean_e_kernel(tc, xT, w1, w2, w3, offs, cen, pos1, pos2,
         pick(sca, 1, 2, BANK, BANK)
         pick(vec, 1, 3, 0, P)
         pick(sca, 1, 3, P, P)
-        for s in range(1, 4):
+        for s in range(1, S // SLICE):
             pick(sca, 1, 3, s * SLICE, SLICE)
         weave_x(vec, 1, 0)
         weave_x(vec, 1, 1)
@@ -200,133 +209,124 @@ def tile_picked_sagecat_mean_e_kernel(tc, xT, w1, w2, w3, offs, cen, pos1, pos2,
         quantize_w1(1)
         h_pass(0, 1)
         weave_w1(sca, 0, 2, 2)
-        weave_w1(vec, 1, 0, 1, slice(0, SHARE))
-        weave_w1(sca, 1, 0, 1, slice(SHARE, P // LINE))
+        weave_w1(vec, 1, 0, 1, slice(0, VECTOR_RUNS))
+        weave_w1(sca, 1, 0, 1, slice(VECTOR_RUNS, RUNS))
         quantize_w1(2)
         h_pass(1, 0)
         weave_w1(vec, 1, 1, 1)
-        weave_w1(vec, 1, 2, 1)
-        weave_w1(sca, 1, 3, 1)
+        weave_w1(sca, 1, 2, 2)
         quantize_w1(3)
         h_pass(1, 1)
-        relu(vec, 0, 0)
-        relu(sca, 0, 1)
-        relu(vec, 0, 2)
-        relu(sca, 0, 3)
+        for n in range(S // SLICE):
+            relu((vec, sca)[n % 2], 0, n)
         quantize_w1(4)
         for t in (2, 3):
             h_pass(0, t)
             h_pass(1, t)
 
-        z_sum = {vt: bank("z_sum%d" % vt, [P, PACK, P], 2 + vt) for vt in (2, 3)}
-        z_pairs = {1: sb("z_pairs1", [P, 8 * P], BF16)}
-        z_low = at("z_low", [P, PACK, Z_HALF], F32, AT_Z_LOW)
-
+        z_sum = [bank("z_sum%d" % n, [P, PACK, P], Z_SUM_BANK + n) for n in range(2)]
+        z_pairs = sb("z_pairs", [P, 8 * P], BF16)
+        z_low = sb("z_low", [P, PACK, HALF], F32, AT_Z_LOW)
         got = {}
 
         def columns(t, half, d):
             if t >= 2:
                 return got[t, half][:, d, :]
-            return got[t][:, d, half * Z_HALF:(half + 1) * Z_HALF]
+            return got[t][:, d, half * HALF:(half + 1) * HALF]
 
         def add_low(t):
-            two = at("two%d" % t, [P, 2, Z_HALF], F32, AT_W2_RAW + t % 2 * 2 * Z_HALF * 4)
-            nc.gpsimd.tensor_tensor(two[:], columns(t, 0, slice(0, 2)), columns(t, 0, slice(2, 4)), ADD)
+            two = sb("two%d" % t, [P, 2, HALF], F32, AT_W2_RAW + t % 2 * 2 * HALF * 4)
+            nc.gpsimd.tensor_tensor(two[:], columns(t, LOW, slice(0, 2)), columns(t, LOW, slice(2, 4)), ADD)
             nc.gpsimd.tensor_tensor(z_low[:, t, :], two[:, 0, :], two[:, 1, :], ADD)
 
-        def add_z(t):
+        def add_high(t):
             for d in range(NEIGHBOURS):
-                for vt in (2, 3):
-                    nc.tensor.matmul(z_sum[vt][:, t, :], columns(t, 1, d)[:, (vt - 2) * P:(vt - 1) * P], ident[:],
+                for n in range(2):
+                    nc.tensor.matmul(z_sum[n][:, t, :], columns(t, HIGH, d)[:, n * P:(n + 1) * P], ident[:],
                                      start=(d == 0), stop=(d == NEIGHBOURS - 1), is_transpose=True)
 
-        def turn_back(u, vt):
-            pairs = z_pairs[vt // 2][:, (2 * u + vt % 2) * 2 * P:(2 * u + vt % 2 + 1) * 2 * P]
-            sca.activation(pairs.rearrange("v (p i e) -> v p e i", i=LINE, e=2),
-                           z_sum[vt][:, 2 * u:2 * u + 2, :].rearrange("v e (p i) -> v p e i", i=LINE), COPY, scale=1.0 / NEIGHBOURS)
-            nc.tensor.transpose(z_back[vt // 2][:, u, (vt % 2) * P:(vt % 2 + 1) * P], pairs.bitcast(F32), ident[:])
+        def turn_back(u):
+            for n in range(2):
+                pairs = z_pairs[:, (2 * u + n) * 2 * P:(2 * u + n + 1) * 2 * P]
+                sca.activation(pairs.rearrange("v (p i e) -> v p e i", i=LINE, e=2),
+                               z_sum[n][:, 2 * u:2 * u + 2, :].rearrange("v e (p i) -> v p e i", i=LINE), COPY, scale=1.0 / NEIGHBOURS)
+                nc.tensor.transpose(z_back[n][:, u, :], pairs.bitcast(F32), ident[:])
 
-        def on_gpsimd(dst, src, factor):
-            nc.gpsimd.tensor_scalar(dst.rearrange("p (c i t) -> p c t i", i=LINE, t=PACK),
-                                    src.rearrange("p t (c i) -> p c t i", i=LINE), factor, 0.0, MULT, ADD)
-
-        def weave_z(half):
-            woven = sb("z_woven%d" % half, [P, Z_HALF * PACK], BF16)
-            sca.copy(woven[:].bitcast(F32).rearrange("p (v i u) -> p v u i", i=2, u=2),
-                     z_back[half][:].rearrange("p u (v i) -> p v u i", i=2))
-            return woven
-
-        w32_woven = at("w32_woven", [P, 2 * N * PACK], BF16, AT_W32)
-        for i in range(2):
-            on_gpsimd(w32_woven[:, i * N * PACK:(i + 1) * N * PACK], w32_raw[i][:], 1.0)
+        w32_woven = sb("w32_woven", [P, 2 * N * PACK], BF16, AT_W1_REST)
+        for matrix in (W3, W2):
+            nc.gpsimd.tensor_scalar(w32_woven[:, matrix * N * PACK:(matrix + 1) * N * PACK].rearrange("p (c t) -> p c t", t=PACK),
+                                    w32_raw[matrix][:].rearrange("p t c -> p c t"), 1.0, 0.0, MULT, ADD)
+        on_scalar = ((0, 0), (1, 0), (1, 2))
         for t in range(2):
             got[t] = sb("got%d" % t, [P, NEIGHBOURS, V], F32)
             for d in range(NEIGHBOURS):
-                gather(sca if (t, d) in ((0, 0), (0, 2), (1, 0)) else vec, got[t][:, d, :], h[t], pos_sb[d], 0, V)
-                if (t, d) == (0, 1):
-                    relu(sca, 1, 0)
-                    relu(sca, 1, 1)
+                gather(sca if (t, d) in on_scalar else vec, got[t][:, d, :], h[t], pos_sb[d], 0, V)
+                if d == 1:
+                    relu(sca, t + 1, 0)
+                    relu(sca, t + 1, 1)
             add_low(t)
-            add_z(t)
-        for t in (2, 3):
-            relu(sca, t, 0)
-            relu(sca, t, 1)
-        for t in (2, 3):
-            for half in range(2):
-                shape = [P, NEIGHBOURS, Z_HALF]
-                got[t, half] = at("got21", shape, F32, AT_GOT) if (t, half) == (2, 1) else sb("got%d%d" % (t, half), shape, F32)
+            add_high(t)
+        relu(sca, 3, 0)
+        relu(sca, 3, 1)
+        for half in (LOW, HIGH):
+            for t in (2, 3):
+                got[t, half] = sb("got%d%d" % (t, half), [P, NEIGHBOURS, HALF], F32, AT_HIGH2 if (t, half) == (2, HIGH) else None)
                 for d in range(NEIGHBOURS):
-                    gather(sca if half == 1 or (t, d) == (3, 0) else vec, columns(t, half, d), h[t], pos_sb[d], half * Z_HALF, Z_HALF)
-            add_low(t)
-            add_z(t)
-        z_woven0 = at("z_woven0", [P, Z_HALF * PACK], BF16, AT_GOT + 64)
-        z_back = {1: bank("z_back1", [P, 2, Z_HALF], 7)}
-        for vt in (2, 3):
-            turn_back(0, vt)
+                    eng = sca if half == HIGH or (t, d) == (3, 0) else vec
+                    gather(eng, columns(t, half, d), h[t], pos_sb[d], half * HALF, HALF)
+                (add_low, add_high)[half](t)
+        low_woven = sb("low_woven", [P, HALF * PACK], BF16, AT_Z_WOVEN)
+        z_back = [bank("z_back%d" % n, [P, 2, P], Z_BACK_BANK + n) for n in range(2)]
+        turn_back(0)
 
-        cen_got = at("cen_got", [P, PACK, V], BF16, AT_CEN_GOT)
+        cen_got = sb("cen_got", [P, PACK, V], BF16, AT_CEN_GOT)
 
-        def gather_cen(eng, t, v0=0, count=V):
-            gather(eng, cen_got[:, t, v0:v0 + count], h[t], cen_sb, v0, count)
+        def gather_cen(eng, t, first, count):
+            gather(eng, cen_got[:, t, first:first + count], h[t], cen_sb, first, count)
 
         def weave_cen(b):
-            v0, count = PIECES[b]
-            woven = at("cen_woven%d" % b, [P, count * PACK], BF16, AT_CEN_WOVEN[b])
-            weave(vec, woven[:], cen_got[:, :, v0:v0 + count])
+            first, count = PIECES[b]
+            woven = sb("cen_woven%d" % b, [P, count * PACK], BF16, AT_CEN_WOVEN[b])
+            move(vec, *line_wise(woven[:], cen_got[:, :, first:first + count]))
             return woven
 
-        def open_out(b, matrix, moving, first_bank):
-            count = PIECES[b][1]
-            accs = [bank("out_acc%d_%d" % (b, m), [P, count], first_bank + m) for m in range(N // P)]
+        gather_cen(vec, 0, 0, V)
+        gather_cen(vec, 1, 0, V)
+        gather_cen(vec, 2, 0, VECTOR_CEN)
+        gather_cen(sca, 2, VECTOR_CEN, V - VECTOR_CEN)
+        gather_cen(sca, 3, 0, V)
+        turn_back(1)
+
+        def weights_of(matrix, m):
+            return slice(matrix * N + m * P, matrix * N + (m + 1) * P)
+
+        def open_out(b, matrix, moving):
+            accs = [bank("out_acc%d_%d" % (b, m), [P, PIECES[b][1]], OUT_BANK[b] + m) for m in range(N // P)]
             for m in range(N // P):
-                mx(accs[m][:], w32, slice(matrix * N + m * P, matrix * N + (m + 1) * P), (moving[0][:], moving[1][:]), True, False)
+                mx(accs[m][:], w32, weights_of(matrix, m), moving[0][:], moving[1][:], True, False)
             return accs
 
         def close_out(b, accs, matrix, moving, engines):
-            v0, count = PIECES[b]
+            first, count = PIECES[b]
             res = sb("res%d" % b, [P, N // P, count], F32)
             for m in range(N // P):
-                mx(accs[m][:], w32, slice(matrix * N + m * P, matrix * N + (m + 1) * P), (moving[0][:], moving[1][:]), False, True)
+                mx(accs[m][:], w32, weights_of(matrix, m), moving[0][:], moving[1][:], False, True)
                 move(engines[m], res[:, m, :], accs[m][:])
-                nc.sync.dma_start(out[m * P:(m + 1) * P, v0:v0 + count], res[:, m, :])
+                nc.sync.dma_start(out[m * P:(m + 1) * P, first:first + count], res[:, m, :])
 
-        gather_cen(vec, 0)
-        gather_cen(vec, 1)
-        gather_cen(sca, 2)
-        gather_cen(sca, 3)
-        for vt in (2, 3):
-            turn_back(1, vt)
-        vec.tensor_scalar_mul(z_woven0[:].rearrange("p (c i t) -> p c t i", i=LINE, t=PACK),
-                              z_low[:].rearrange("p t (c i) -> p c t i", i=LINE), 1.0 / NEIGHBOURS)
+        vec.tensor_scalar_mul(*line_wise(low_woven[:], z_low[:]), 1.0 / NEIGHBOURS)
         w32 = quantize("w32", w32_woven[:], AT_W32_WORDS)
-        z_woven1 = weave_z(1)
-        out0 = open_out(0, 0, quantize("z0", z_woven0[:]), 4)
+        high_woven = [sb("high_woven%d" % n, [P, P * PACK], BF16) for n in range(2)]
+        for n in range(2):
+            sca.copy(high_woven[n][:].bitcast(F32).rearrange("p (v i u) -> p v u i", i=2, u=2),
+                     z_back[n][:].rearrange("p u (v i) -> p v u i", i=2))
+        out0 = open_out(0, W3, quantize("z0", low_woven[:]))
         cen_woven0 = weave_cen(0)
         cen_woven1 = weave_cen(1)
-        close_out(0, out0, 1, quantize("cen0", cen_woven0[:]), (sca, sca))
+        close_out(0, out0, W2, quantize("cen0", cen_woven0[:]), (sca, sca))
         cen_woven2 = weave_cen(2)
-        out1 = open_out(1, 1, quantize("cen1", cen_woven1[:]), 0)
-        out2 = open_out(2, 1, quantize("cen2", cen_woven2[:]), 2)
+        out1 = open_out(1, W2, quantize("cen1", cen_woven1[:]))
+        out2 = open_out(2, W2, quantize("cen2", cen_woven2[:]))
         for b, accs in ((1, out1), (2, out2)):
-            z_q = quantize("z%d" % b, z_woven1[:, (b - 1) * P * PACK:b * P * PACK], AT_GOT + 64 + (b - 1) * P * 4)
-            close_out(b, accs, 0, z_q, (vec, sca))
+            z_q = quantize("z%d" % b, high_woven[b - 1][:], AT_Z_WOVEN + (b - 1) * P * 4)
+            close_out(b, accs, W3, z_q, (vec, sca))

from contextlib import ExitStack

import concourse.mybir as mybir
from concourse.masks import make_identity

K, T, S, V, H, N = 1024, 2048, 1024, 512, 512, 256
FLOPS = 2 * K * H * S + 2 * 2 * H * N * V

F32 = mybir.dt.float32
BF16 = mybir.dt.bfloat16
U32 = mybir.dt.uint32
U16 = mybir.dt.uint16
U8 = mybir.dt.uint8
FP8X4 = mybir.dt.float8_e4m3fn_x4
COPY = mybir.ActivationFunctionType.Copy
RELU = mybir.ActivationFunctionType.Relu
ADD = mybir.AluOpType.add
MULT = mybir.AluOpType.mult

P = 128
PACK = 4
K_PASS = P * PACK
BANK = 512
GROUP = 16
LINE = 4
RUNS = P // LINE
NEIGHBOURS = 4
HALF = V // 2
LOW, HIGH = 0, 1
W3, W2 = 0, 1

SLICE = 256
SPAN = [SLICE, BANK, BANK, BANK]
VECTOR_RUNS = 18
VECTOR_CEN = 192
PIECES = [(0, 256), (256, 128), (384, 128)]

H_BANK = [0, 4, 6, 0]
Z_SUM_BANK = 4
Z_BACK_BANK = 6
OUT_BANK = [4, 0, 2]

OVERLAP = 64
AT_Z_LOW = 2048
AT_HIGH2 = 12288
AT_W1_REST = 20480
AT_W1_WORDS = 24576
AT_W2_RAW = 26624
AT_CEN_GOT = AT_HIGH2 - 4096 + OVERLAP
AT_Z_WOVEN = AT_HIGH2 + OVERLAP
AT_W32_WORDS = AT_W2_RAW + OVERLAP
AT_CEN_WOVEN = [AT_W32_WORDS + 2048, AT_Z_LOW + 2048 + OVERLAP, AT_Z_LOW + 3072 + OVERLAP]


def tile_picked_sagecat_mean_e_kernel(tc, xT, w1, w2, w3, offs, cen, pos1, pos2, pos3, pos4, out):
    nc = tc.nc
    vec, sca = nc.vector, nc.scalar
    with ExitStack() as ctx:
        keep = ctx.enter_context(tc.tile_pool(name="keep", bufs=1))
        placed = ctx.enter_context(tc.tile_pool(name="placed", bufs=1))
        psum = ctx.enter_context(tc.psum_pool(name="psum", bufs=1))

        def sb(name, shape, dtype, offset=None):
            if offset is None:
                return keep.tile(shape, dtype, name=name, tag=name, align_bytes=64)
            return placed.tile(shape, dtype, name=name, offset=offset, align_bytes=64)

        def bank(name, shape, index):
            return psum.tile(shape, F32, name=name, offset=index * BANK * 4)

        def load_list(name, src):
            tile = sb(name, list(src.shape), U16)
            nc.sync.dma_start(tile[:], src)
            return tile

        def gather(eng, dst, window, offsets, first, count):
            looked_up = window[:].indirect(offsets[:, first // GROUP:(first + count) // GROUP])
            if eng is vec:
                vec.tensor_copy(dst, looked_up)
            else:
                sca.activation(dst, looked_up, COPY)

        def move(eng, dst, src):
            if eng is vec:
                vec.tensor_copy(dst, src)
            else:
                sca.copy(dst, src)

        def line_wise(dst, src):
            return dst.rearrange("p (c i t) -> p c t i", i=LINE, t=PACK), src.rearrange("p t (c i) -> p c t i", i=LINE)

        def quantize(name, src, offset=None):
            width = src.shape[1] // PACK
            words = sb(name + "_words", [P, width], U32, offset)
            scales = sb(name + "_scales", [P, width], U8)
            vec.quantize_mx(out=words[:].bitcast(FP8X4), scales=scales[:], in_=src)
            return words, scales

        def mx(acc, weights, cols, words, scales, start, stop):
            nc.tensor.matmul_mx(out=acc, lhsT=weights[0][:, cols].bitcast(FP8X4), lhsT_scale=weights[1][:, cols],
                                rhs=words.bitcast(FP8X4), rhs_scale=scales, start=start, stop=stop)

        ident = sb("ident", [P, P], F32)
        make_identity(nc, ident[:])

        x_raw = {}
        for g in range(2):
            rows = xT[g * K_PASS:(g + 1) * K_PASS, :].rearrange("(p j) t -> j p t", j=PACK)
            for j in range(PACK):
                x_raw[g, j] = sb("x_raw%d%d" % (g, j), [P, T], F32)
                nc.sync.dma_start(x_raw[g, j][:], rows[j])
                if (g, j) == (0, 0):
                    offs_sb = load_list("offs", offs)
        w1_raw = []
        for g in range(2):
            raw = sb("w1_raw%d" % g, [P, PACK, H], F32)
            nc.sync.dma_start(raw[:], w1[g * K_PASS:(g + 1) * K_PASS, :].rearrange("(p j) c -> p j c", j=PACK))
            w1_raw.append(raw)
        pos_sb = [load_list("pos%d" % (d + 1), src) for d, src in enumerate((pos1, pos2, pos3, pos4))]
        cen_sb = load_list("cen", cen)
        w32_raw = []
        for name, src, offset in (("w3_raw", w3, None), ("w2_raw", w2, AT_W2_RAW)):
            raw = sb(name, [P, PACK, N], F32, offset)
            dealt = src.rearrange("(b t r) c -> t b r c", t=PACK, r=LINE)
            for t in range(PACK):
                nc.sync.dma_start(raw[:, t, :], dealt[t])
            w32_raw.append(raw)

        picked = [sb("picked%d" % g, [P, PACK, S], BF16) for g in range(2)]
        x_woven = {(g, n): sb("x_woven%d%d" % (g, n), [P, BANK * PACK], BF16) for g in range(2) for n in range(2)}
        x_q = {}

        def pick(eng, g, j, first, count):
            gather(eng, picked[g][:, j, first:first + count], x_raw[g, j], offs_sb, first, count)

        def weave_x(eng, g, s):
            at_col = (s % 2) * SLICE * PACK
            move(eng, *line_wise(x_woven[g, s // 2][:, at_col:at_col + SLICE * PACK], picked[g][:, :, s * SLICE:(s + 1) * SLICE]))

        def quantize_x(g, n):
            x_q[g, n] = quantize("x%d%d" % (g, n), x_woven[g, n][:])

        w1_groups = [[(0, 0)], [(0, 1)], [(1, 0)], [(1, 1)], [(0, 2), (0, 3), (1, 2), (1, 3)]]
        w1_words_at = [None, None, AT_W1_WORDS, None, AT_W1_WORDS]
        w1_woven_at = [None, None, None, None, AT_W1_REST]
        w1_woven = [sb("w1_woven%d" % n, [P, len(group) * K_PASS], BF16, w1_woven_at[n]) for n, group in enumerate(w1_groups)]
        w1_q = {}

        def weave_w1(eng, g, t0, count, runs=slice(0, RUNS)):
            n = [n for n, group in enumerate(w1_groups) if (g, t0) in group][0]
            place = w1_groups[n].index((g, t0))
            src = w1_raw[g][:].rearrange("p j (b t i) -> p b t j i", t=PACK, i=LINE)
            dst = w1_woven[n][:, place * K_PASS:(place + count) * K_PASS].rearrange("p (t b i j) -> p b t j i", b=RUNS, i=LINE, j=PACK)
            move(eng, dst[:, runs], src[:, runs, t0:t0 + count])

        def quantize_w1(n):
            weights = quantize("w1_%d" % n, w1_woven[n][:], w1_words_at[n])
            for place, key in enumerate(w1_groups[n]):
                w1_q[key] = (weights, slice(place * P, (place + 1) * P))

        h = [sb("h%d" % t, [P, S], F32) for t in range(PACK)]
        h_acc = {}

        def h_pass(g, t):
            width = SPAN[t]
            for n in range(S // width):
                if g == 0:
                    h_acc[t, n] = bank("h_acc%d%d" % (t, n), [P, width], H_BANK[t] + n)
                words, scales = x_q[g, n * width // BANK]
                cols = slice(n * width % BANK, n * width % BANK + width)
                mx(h_acc[t, n][:], w1_q[g, t][0], w1_q[g, t][1], words[:, cols], scales[:, cols], g == 0, g == 1)

        def relu(eng, t, n):
            dst = h[t][:, n * SPAN[t]:(n + 1) * SPAN[t]]
            if eng is vec:
                vec.tensor_scalar_max(dst, h_acc[t, n][:], 0.0)
            else:
                sca.activation(dst, h_acc[t, n][:], RELU)

        pick(vec, 0, 0, 0, S)
        pick(sca, 0, 1, 0, S)
        pick(vec, 0, 2, 0, S)
        pick(vec, 0, 3, 0, BANK)
        pick(sca, 0, 3, BANK, BANK)
        weave_x(vec, 0, 0)
        weave_x(sca, 0, 3)
        weave_x(vec, 0, 1)
        weave_x(vec, 0, 2)
        quantize_x(0, 0)
        pick(sca, 1, 0, 0, S)
        quantize_x(0, 1)
        pick(vec, 1, 1, 0, S)
        pick(vec, 1, 2, 0, BANK)
        pick(sca, 1, 2, BANK, BANK)
        pick(vec, 1, 3, 0, P)
        pick(sca, 1, 3, P, P)
        for s in range(1, S // SLICE):
            pick(sca, 1, 3, s * SLICE, SLICE)
        weave_x(vec, 1, 0)
        weave_x(vec, 1, 1)
        weave_x(vec, 1, 2)
        quantize_x(1, 0)
        weave_w1(sca, 0, 0, 1)
        quantize_w1(0)
        h_pass(0, 0)
        weave_x(vec, 1, 3)
        weave_w1(sca, 0, 1, 1)
        quantize_x(1, 1)
        quantize_w1(1)
        h_pass(0, 1)
        weave_w1(sca, 0, 2, 2)
        weave_w1(vec, 1, 0, 1, slice(0, VECTOR_RUNS))
        weave_w1(sca, 1, 0, 1, slice(VECTOR_RUNS, RUNS))
        quantize_w1(2)
        h_pass(1, 0)
        weave_w1(vec, 1, 1, 1)
        weave_w1(sca, 1, 2, 2)
        quantize_w1(3)
        h_pass(1, 1)
        for n in range(S // SLICE):
            relu((vec, sca)[n % 2], 0, n)
        quantize_w1(4)
        for t in (2, 3):
            h_pass(0, t)
            h_pass(1, t)

        z_sum = [bank("z_sum%d" % n, [P, PACK, P], Z_SUM_BANK + n) for n in range(2)]
        z_pairs = sb("z_pairs", [P, 8 * P], BF16)
        z_low = sb("z_low", [P, PACK, HALF], F32, AT_Z_LOW)
        got = {}

        def columns(t, half, d):
            if t >= 2:
                return got[t, half][:, d, :]
            return got[t][:, d, half * HALF:(half + 1) * HALF]

        def add_low(t):
            two = sb("two%d" % t, [P, 2, HALF], F32, AT_W2_RAW + t % 2 * 2 * HALF * 4)
            nc.gpsimd.tensor_tensor(two[:], columns(t, LOW, slice(0, 2)), columns(t, LOW, slice(2, 4)), ADD)
            nc.gpsimd.tensor_tensor(z_low[:, t, :], two[:, 0, :], two[:, 1, :], ADD)

        def add_high(t):
            for d in range(NEIGHBOURS):
                for n in range(2):
                    nc.tensor.matmul(z_sum[n][:, t, :], columns(t, HIGH, d)[:, n * P:(n + 1) * P], ident[:],
                                     start=(d == 0), stop=(d == NEIGHBOURS - 1), is_transpose=True)

        def turn_back(u):
            for n in range(2):
                pairs = z_pairs[:, (2 * u + n) * 2 * P:(2 * u + n + 1) * 2 * P]
                sca.activation(pairs.rearrange("v (p i e) -> v p e i", i=LINE, e=2),
                               z_sum[n][:, 2 * u:2 * u + 2, :].rearrange("v e (p i) -> v p e i", i=LINE), COPY, scale=1.0 / NEIGHBOURS)
                nc.tensor.transpose(z_back[n][:, u, :], pairs.bitcast(F32), ident[:])

        w32_woven = sb("w32_woven", [P, 2 * N * PACK], BF16, AT_W1_REST)
        for matrix in (W3, W2):
            nc.gpsimd.tensor_scalar(w32_woven[:, matrix * N * PACK:(matrix + 1) * N * PACK].rearrange("p (c t) -> p c t", t=PACK),
                                    w32_raw[matrix][:].rearrange("p t c -> p c t"), 1.0, 0.0, MULT, ADD)
        on_scalar = ((0, 0), (1, 0), (1, 2))
        for t in range(2):
            got[t] = sb("got%d" % t, [P, NEIGHBOURS, V], F32)
            for d in range(NEIGHBOURS):
                gather(sca if (t, d) in on_scalar else vec, got[t][:, d, :], h[t], pos_sb[d], 0, V)
                if d == 1:
                    relu(sca, t + 1, 0)
                    relu(sca, t + 1, 1)
            add_low(t)
            add_high(t)
        relu(sca, 3, 0)
        relu(sca, 3, 1)
        for half in (LOW, HIGH):
            for t in (2, 3):
                got[t, half] = sb("got%d%d" % (t, half), [P, NEIGHBOURS, HALF], F32, AT_HIGH2 if (t, half) == (2, HIGH) else None)
                for d in range(NEIGHBOURS):
                    eng = sca if half == HIGH or (t, d) == (3, 0) else vec
                    gather(eng, columns(t, half, d), h[t], pos_sb[d], half * HALF, HALF)
                (add_low, add_high)[half](t)
        low_woven = sb("low_woven", [P, HALF * PACK], BF16, AT_Z_WOVEN)
        z_back = [bank("z_back%d" % n, [P, 2, P], Z_BACK_BANK + n) for n in range(2)]
        turn_back(0)

        cen_got = sb("cen_got", [P, PACK, V], BF16, AT_CEN_GOT)

        def gather_cen(eng, t, first, count):
            gather(eng, cen_got[:, t, first:first + count], h[t], cen_sb, first, count)

        def weave_cen(b):
            first, count = PIECES[b]
            woven = sb("cen_woven%d" % b, [P, count * PACK], BF16, AT_CEN_WOVEN[b])
            move(vec, *line_wise(woven[:], cen_got[:, :, first:first + count]))
            return woven

        gather_cen(vec, 0, 0, V)
        gather_cen(vec, 1, 0, V)
        gather_cen(vec, 2, 0, VECTOR_CEN)
        gather_cen(sca, 2, VECTOR_CEN, V - VECTOR_CEN)
        gather_cen(sca, 3, 0, V)
        turn_back(1)

        def weights_of(matrix, m):
            return slice(matrix * N + m * P, matrix * N + (m + 1) * P)

        def open_out(b, matrix, moving):
            accs = [bank("out_acc%d_%d" % (b, m), [P, PIECES[b][1]], OUT_BANK[b] + m) for m in range(N // P)]
            for m in range(N // P):
                mx(accs[m][:], w32, weights_of(matrix, m), moving[0][:], moving[1][:], True, False)
            return accs

        def close_out(b, accs, matrix, moving, engines):
            first, count = PIECES[b]
            res = sb("res%d" % b, [P, N // P, count], F32)
            for m in range(N // P):
                mx(accs[m][:], w32, weights_of(matrix, m), moving[0][:], moving[1][:], False, True)
                move(engines[m], res[:, m, :], accs[m][:])
                nc.sync.dma_start(out[m * P:(m + 1) * P, first:first + count], res[:, m, :])

        vec.tensor_scalar_mul(*line_wise(low_woven[:], z_low[:]), 1.0 / NEIGHBOURS)
        w32 = quantize("w32", w32_woven[:], AT_W32_WORDS)
        high_woven = [sb("high_woven%d" % n, [P, P * PACK], BF16) for n in range(2)]
        for n in range(2):
            sca.copy(high_woven[n][:].bitcast(F32).rearrange("p (v i u) -> p v u i", i=2, u=2),
                     z_back[n][:].rearrange("p u (v i) -> p v u i", i=2))
        out0 = open_out(0, W3, quantize("z0", low_woven[:]))
        cen_woven0 = weave_cen(0)
        cen_woven1 = weave_cen(1)
        close_out(0, out0, W2, quantize("cen0", cen_woven0[:]), (sca, sca))
        cen_woven2 = weave_cen(2)
        out1 = open_out(1, W2, quantize("cen1", cen_woven1[:]))
        out2 = open_out(2, W2, quantize("cen2", cen_woven2[:]))
        for b, accs in ((1, out1), (2, out2)):
            z_q = quantize("z%d" % b, high_woven[b - 1][:], AT_Z_WOVEN + (b - 1) * P * 4)
            close_out(b, accs, W3, z_q, (vec, sca))
